import numpy as np
import ml_dtypes


def mxq(x, axis, fmt="e4m3"):
    dtype, down = {"e4m3": (ml_dtypes.float8_e4m3fn, 7), "e5m2": (ml_dtypes.float8_e5m2, 14)}[fmt]
    v = np.moveaxis(np.asarray(x, np.float32).astype(ml_dtypes.bfloat16).astype(np.float64), axis, -1)
    blocks = v.reshape(v.shape[:-1] + (-1, 32))
    amax = np.abs(blocks).max(-1, keepdims=True)
    byte = np.maximum(np.where(amax > 0, np.frexp(amax)[1] - 1 + 127, 0) - down, 1)
    scale = np.exp2(byte - 127.0)
    codes = (blocks / scale).astype(np.float32).astype(dtype).astype(np.float64)
    return np.moveaxis((codes * scale).reshape(v.shape), -1, axis)


WIDE = False


def mx_kscale(k):
    if not WIDE:
        return np.ones(k)
    levels = np.array([10, -10, 5, -5, 0])
    if k % 512:
        return np.exp2(np.random.permutation(np.resize(levels, k // 32))).repeat(32)
    a = np.empty((k // 512, 16))
    for p in range(k // 512):
        a[p, :8] = np.random.permutation(np.resize(levels, 8))
        for g in range(8):
            far = levels[np.abs(levels - a[p, g]) >= 10]
            a[p, g + 8] = far[np.random.randint(len(far))]
    return np.exp2(a.ravel()).repeat(32)


def f64(x):
    return np.asarray(x).astype(np.float64)


def striped(idx):
    return np.tile(idx.reshape(-1, 16).T, (8, 1)).astype(np.uint16)


def unstriped(offs):
    return offs[:16].T.reshape(-1).astype(np.int64)


E2M1 = np.array([0.0, 0.5, 1.0, 1.5, 2.0, 3.0, 4.0, 6.0, -0.0, -0.5, -1.0, -1.5, -2.0, -3.0, -4.0, -6.0])


def pack_weight(w, fmt):
    k, n = w.shape
    w = f64(np.asarray(w, np.float32).astype(ml_dtypes.bfloat16)).reshape(k // 32, 32, n)
    amax = np.abs(w).max(1)
    if fmt == "e4m3":
        byte = np.frexp(amax)[1] - 1 + 127 - 7
    else:
        mant, ex = np.frexp(amax / 6.0)
        byte = np.where(mant > 0.5, ex, ex - 1) + 127
    byte = np.clip(np.where(amax > 0, byte, 1), 1, 254)
    scaled = (w * np.exp2(127.0 - byte)[:, None, :]).reshape(k, n).astype(np.float32)
    by_word = np.ascontiguousarray(scaled.reshape(k // 512, 128, 4, n).transpose(0, 1, 3, 2))
    if fmt == "e4m3":
        words = by_word.astype(ml_dtypes.float8_e4m3fn).view(np.uint8)
    else:
        c = by_word.astype(ml_dtypes.float4_e2m1fn).view(np.uint8) & 0xF
        words = (c[..., 0::2] | (c[..., 1::2] << 4)).reshape(k // 512, 128, 2 * n)
    return np.ascontiguousarray(words), np.ascontiguousarray(byte.astype(np.uint8).reshape(k // 512, 16, n))


def unpack_weight(words, scales, fmt):
    g, _, n = scales.shape
    words = np.ascontiguousarray(words).reshape(g, 128, n, -1)
    if fmt == "e4m3":
        vals = words.view(ml_dtypes.float8_e4m3fn).astype(np.float64)
    else:
        nib = np.empty((g, 128, n, 4), np.uint8)
        nib[..., 0::2] = words & 0xF
        nib[..., 1::2] = words >> 4
        vals = E2M1[nib]
    vals = vals * np.repeat(np.exp2(scales.astype(np.float64) - 127.0), 8, axis=1)[..., None]
    return vals.transpose(0, 1, 3, 2).reshape(g * 512, n)


def d_relu(v):
    return (v > 0).astype(np.float64)


K, T, E, C, H, N = 512, 768, 6, 128, 512, 512


def by_expert(wq, xq):
    return np.concatenate([wq[e].T @ xq[:, e * C:(e + 1) * C] for e in range(E)], axis=1)


def setup_inputs():
    n = np.random.standard_normal
    v = mx_kscale(N)
    u = mx_kscale(H)
    slot_token = np.random.permutation(T)[:E * C]
    w_slot = np.random.uniform(0.2, 1.0, E * C)
    dy = pack_weight(n((N, T)) * v[:, None], "e4m3")
    return {
        "dy_words": dy[0],
        "dy_scales": dy[1],
        "wt": (n((N, K)) / np.sqrt(N) / v[:, None]).astype(np.float32),
        "wbt": (n((E, N, H)) / np.sqrt(N) / v[None, :, None] * u).astype(np.float32),
        "wat": (n((E, H, K)) / np.sqrt(H) / u[None, :, None]).astype(np.float32),
        "a": (n((H, E * C))).astype(np.float32),
        "gate": (np.tile(w_slot, (128, 1))).astype(np.float32),
        "offs": striped(slot_token),
    }


def reference(dy_words, dy_scales, wt, wbt, wat, a, gate, offs):
    wtq = mxq(f64(wt), 0, "e4m3")
    wbtq = mxq(f64(wbt), 1, "e4m3")
    watq = mxq(f64(wat), 1, "e4m3")
    idx = unstriped(offs)
    dy = unpack_weight(dy_words, dy_scales, "e4m3")
    base = wtq.T @ dy
    dh = f64(gate[:1]) * by_expert(wbtq, dy[:, idx]) * d_relu(f64(a))
    dx = by_expert(watq, mxq(dh, 0, "e4m3"))
    c = np.zeros((K, T))
    c[:, idx] = dx
    return base + c

@@ -1,0 +1,215 @@
+from contextlib import ExitStack
+
+import concourse.mybir as mybir
+from concourse.masks import make_identity
+
+K, T, E, C, H, N = 512, 768, 6, 128, 512, 512
+FLOPS = 2 * T * (N * K + N * H + H * K)
+
+F32 = mybir.dt.float32
+BF16 = mybir.dt.bfloat16
+I32 = mybir.dt.int32
+U32 = mybir.dt.uint32
+U16 = mybir.dt.uint16
+U8 = mybir.dt.uint8
+FP8X4 = mybir.dt.float8_e4m3fn_x4
+ALU = mybir.AluOpType
+COPY = mybir.ActivationFunctionType.Copy
+
+P = 128
+PACK = 4
+WIDTH = 512
+LINE = 4
+K_TILES = K // P
+PAIR = 2 * C
+VECTOR_COLS = {"wb0": 256, "wa0": 256, "wb1": 256}
+
+
+def tile_moe_adb_relu_kernel(tc, dy_words, dy_scales, wt, wbt, wat, a, gate, offs, out):
+    nc = tc.nc
+    with ExitStack() as ctx:
+        keep = ctx.enter_context(tc.tile_pool(name="keep", bufs=1))
+        ring = ctx.enter_context(tc.tile_pool(name="ring", bufs=2))
+        psum = ctx.enter_context(tc.psum_pool(name="psum", bufs=2))
+
+        offsets = keep.tile([P, T // 16], U16, name="offsets")
+        words = keep.tile([P, T], I32, name="words", align_bytes=64)
+        scales = keep.tile([P, T], U8, name="scales", align_bytes=64)
+        slot_words = keep.tile([P, T], U32, name="slot_words", align_bytes=64)
+        slot_scales = keep.tile([P, T], U8, name="slot_scales", align_bytes=64)
+        gate_rows = keep.tile([P, C], F32, name="gate_rows")
+        gate_cols = keep.tile([P, 8], F32, name="gate_cols")
+        identity = keep.tile([P, P], F32, name="identity")
+        dx = keep.tile([P, K_TILES, T], F32, name="dx")
+        windows = [keep.tile([P, T], F32, name=f"window{kt}") for kt in range(K_TILES)]
+        raw = {}
+        saved = {}
+
+        def load_weight(name, matrix):
+            raw[name] = keep.tile([P, PACK, WIDTH], F32, name="raw_" + name)
+            nc.sync.dma_start(raw[name][:], matrix.rearrange("(p j) c -> p j c", j=PACK))
+
+        def load_saved(pair):
+            saved[pair] = keep.tile([P, PACK, PAIR], F32, name=f"saved{pair}")
+            nc.sync.dma_start(saved[pair][:], a[:, pair * PAIR : (pair + 1) * PAIR].rearrange("(p j) s -> p j s", j=PACK))
+
+        nc.vector.memset(scales[:].bitcast(I32), 0)
+        nc.sync.dma_start(words[:], dy_words[0].rearrange("p t d -> p (t d)").bitcast(I32))
+        nc.sync.dma_start(offsets[:], offs)
+        for q in range(4):
+            nc.scalar.dma_start(scales[32 * q : 32 * q + 4, :].bitcast(I32), dy_scales[0, 4 * q : 4 * q + 4, :].bitcast(I32))
+        nc.scalar.dma_start(gate_rows[:], gate.rearrange("r (e u) -> (r e) u", u=C)[0:P, :])
+        load_weight("wb0", wbt[0])
+        for e in range(E):
+            if e + 1 < E:
+                load_weight(f"wb{e + 1}", wbt[e + 1])
+            if e == 0 or (e % 2 == 1 and e + 1 < E):
+                load_saved((e + 1) // 2)
+            load_weight(f"wa{e}", wat[e])
+        load_weight("w", wt)
+
+        make_identity(nc, identity[:])
+        turned_gate = psum.tile([P, P], F32, name="turned_gate", tag="turned", bufs=1)
+        nc.tensor.transpose(turned_gate[:], gate_rows[:], identity[:])
+        nc.scalar.activation(gate_cols[:], turned_gate[:, 0:8], COPY)
+
+        grouped = {}
+        codes = {}
+        planes = {}
+
+        def round_weight(name):
+            grouped[name] = ring.tile([P, WIDTH, PACK], BF16, name="grouped", tag="grouped", bufs=4, align_bytes=64)
+            split = WIDTH - VECTOR_COLS.get(name, 0)
+            half = min(split, WIDTH // 2)
+            for engine, lo, hi in ((nc.scalar.copy, 0, half), (nc.scalar.copy, half, split), (nc.vector.tensor_copy, split, WIDTH)):
+                if hi > lo:
+                    engine(
+                        grouped[name][:, lo:hi, :].rearrange("p (c i) j -> p c j i", i=LINE),
+                        raw[name][:, :, lo:hi].rearrange("p j (c i) -> p c j i", i=LINE),
+                    )
+
+        def quantise_weight(name):
+            codes[name] = ring.tile([P, WIDTH], U32, name="codes", tag="codes", bufs=6, align_bytes=64)
+            planes[name] = ring.tile([P, WIDTH], U8, name="planes", tag="planes", bufs=6, align_bytes=64)
+            nc.vector.quantize_mx(
+                out=codes[name][:].bitcast(FP8X4),
+                scales=planes[name][:],
+                in_=grouped[name][:].rearrange("p c j -> p (c j)"),
+            )
+
+        def gather(pair):
+            cols = slice(pair * PAIR, (pair + 1) * PAIR)
+            entries = offsets[:, pair * PAIR // 16 : (pair + 1) * PAIR // 16]
+            nc.vector.tensor_copy(slot_words[:, cols], words[:].bitcast(U32).indirect(entries))
+            nc.vector.tensor_copy(slot_scales[:, cols], scales[:].indirect(entries))
+
+        turned = {}
+        dh_codes = {}
+        dh_planes = {}
+
+        def inner_sums(e):
+            slots = slice(e * C, (e + 1) * C)
+            sums = psum.tile([P, H], F32, name="sums", tag="sums")
+            nc.tensor.matmul_mx(
+                out=sums[:],
+                lhsT=slot_words[:, slots].bitcast(FP8X4),
+                lhsT_scale=slot_scales[:, slots],
+                rhs=codes[f"wb{e}"][:].bitcast(FP8X4),
+                rhs_scale=planes[f"wb{e}"][:],
+                start=True,
+                stop=True,
+            )
+            gated = ring.tile([P, H], F32, name="gated")
+            nc.scalar.activation(gated[:], sums[:], COPY, scale=gate_cols[:, e : e + 1])
+            turned[e] = psum.tile([P, PACK, C], F32, name="turned", tag="turned", bufs=1)
+            for j in range(PACK):
+                nc.tensor.transpose(turned[e][:, j, :], gated[:, j:H:PACK], identity[:])
+
+        def inner_gradient(e):
+            dh = ring.tile([P, C, PACK], BF16, name="dh", align_bytes=64)
+            lo = (e % 2) * C
+            nc.vector.scalar_tensor_tensor(
+                out=dh[:],
+                in0=saved[e // 2][:, :, lo : lo + C].rearrange("p j s -> p s j"),
+                scalar=0.0,
+                in1=turned[e][:].rearrange("p j s -> p s j"),
+                op0=ALU.is_gt,
+                op1=ALU.mult,
+            )
+            dh_codes[e] = ring.tile([P, C], U32, name="dh_codes", tag="dh_codes", bufs=3, align_bytes=64)
+            dh_planes[e] = ring.tile([P, C], U8, name="dh_planes", tag="dh_planes", bufs=3, align_bytes=64)
+            nc.vector.quantize_mx(
+                out=dh_codes[e][:].bitcast(FP8X4),
+                scales=dh_planes[e][:],
+                in_=dh[:].rearrange("p s j -> p (s j)"),
+            )
+
+        def adapter_product(e):
+            product = psum.tile([P, K_TILES, C], F32, name="product", tag="turned" if e + 1 < E else "last", bufs=1)
+            for kt in range(K_TILES):
+                cols = slice(kt * P, (kt + 1) * P)
+                nc.tensor.matmul_mx(
+                    out=product[:, kt, :],
+                    lhsT=codes[f"wa{e}"][:, cols].bitcast(FP8X4),
+                    lhsT_scale=planes[f"wa{e}"][:, cols],
+                    rhs=dh_codes[e][:].bitcast(FP8X4),
+                    rhs_scale=dh_planes[e][:],
+                    start=True,
+                    stop=True,
+                )
+            nc.scalar.copy(dx[:, :, e * C : (e + 1) * C], product[:])
+
+        def scatter(first, last, kt):
+            entries = offsets[:, first * C // 16 : (last + 1) * C // 16]
+            nc.vector.tensor_copy(windows[kt][:].indirect(entries), dx[:, kt, first * C : (last + 1) * C])
+
+        round_weight("wb0")
+        gather(0)
+        quantise_weight("wb0")
+        inner_sums(0)
+        round_weight("wb1")
+        inner_gradient(0)
+        quantise_weight("wb1")
+        inner_sums(1)
+        round_weight("wa0")
+        quantise_weight("wa0")
+        gather(1)
+        round_weight("wb2")
+        gather(2)
+        round_weight("wa1")
+        for e in range(E - 1):
+            inner_gradient(e + 1)
+            adapter_product(e)
+            if e + 2 < E:
+                quantise_weight(f"wb{e + 2}")
+                inner_sums(e + 2)
+            quantise_weight(f"wa{e + 1}")
+            for kt in range(K_TILES):
+                scatter(e, e, kt)
+            if e + 3 < E:
+                round_weight(f"wb{e + 3}")
+            if e + 2 < E:
+                round_weight(f"wa{e + 2}")
+        adapter_product(E - 1)
+        round_weight("w")
+        quantise_weight("w")
+        tails = [psum.tile([P, 2, T - WIDTH], F32, name=f"tail{h}", tag="sums") for h in range(2)]
+        for kt in range(K_TILES):
+            cols = slice(kt * P, (kt + 1) * P)
+            head = psum.tile([P, WIDTH], F32, name="head", tag="base", bufs=4)
+            parts = ((head[:], slice(0, WIDTH)), (tails[kt // 2][:, kt % 2, :], slice(WIDTH, T)))
+            for bank, tokens in parts:
+                nc.tensor.matmul_mx(
+                    out=bank,
+                    lhsT=codes["w"][:, cols].bitcast(FP8X4),
+                    lhsT_scale=planes["w"][:, cols],
+                    rhs=words[:, tokens].bitcast(FP8X4),
+                    rhs_scale=scales[:, tokens],
+                    start=True,
+                    stop=True,
+                )
+            scatter(E - 1, E - 1, kt)
+            result = ring.tile([P, T], F32, name="result", tag="result", bufs=4)
+            for bank, tokens in parts:
+                nc.vector.tensor_tensor(result[:, tokens], bank, windows[kt][:, tokens], ALU.add)
+            nc.sync.dma_start(out[cols, :], result[:])

@@ -22,7 +22,9 @@ WIDTH = 512
 LINE = 4
 K_TILES = K // P
 PAIR = 2 * C
-VECTOR_COLS = {"wb0": 256, "wa0": 256, "wb1": 256}
+HALF = WIDTH // 2
+LOADS = "dy gate wb0 sc wa0 a0 wb1 wa1 wb2 wb3 wa2 a1 wb4 wa4 wa3 wb5 a2 w wa5"
+STEPS = "c:wb0:0:s c:wb0:1:v g:0 Q:wb0:1 Q:wb0:0 c:wa0:0:s g:1 c:wa0:1:v Q:wa0:1 G:0 Q:wa0:0 M:0 q:0 c:wb1:1:s P:0 c:wb1:0:v Q:wb1:1 d:0:0:2 Q:wb1:0 G:1 c:wa1:0:s c:wa1:1:v M:1 Q:wa1:1 q:1 d:0:2:4 Q:wa1:0 P:1 c:wb2:1:s c:wb2:0:s d:1:0:2 Q:wb2:0 Q:wb2:1 d:1:2:4 s:00:2 c:wa2:0:v c:wb3:1:s Q:wa2:0 G:2 M:2 c:wb3:0:s Q:wb3:0 Q:wb3:1 c:wa2:1:s q:2 c:wb4:0:s s:00:1 s:00:0 s:00:3 Q:wa2:1 P:2 G:3 d:2:2:4 Q:wb4:0 c:wb4:1:s M:3 d:2:0:2 Q:wb4:1 c:wa3:0:v s:11:1 s:11:2 c:wa3:1:s Q:wa3:0 q:3 c:wa4:0:s g:2 Q:wa3:1 c:wb5:0:s s:11:0 s:22:1 s:11:3 G:4 c:wa4:1:v P:3 d:3:0:2 Q:wb5:0 c:wb5:1:s Q:wa4:0 Q:wb5:1 M:4 Q:wa4:1 c:wa5:1:s q:4 s:33:1 Q:wa5:1 s:22:3 s:22:0 d:3:2:4 s:22:2 s:33:0 G:5 c:wa5:0:s M:5 P:4 d:4:0:2 s:44:1 c:w:1:s Q:wa5:0 d:4:2:4 q:5 s:33:2 s:44:0 c:w:0:s Q:w:1 s:33:3 P:5 Q:w:0 s:44:2 d:5:0:2 d:5:2:4 s:44:3 B:0 B:1 B:2 B:3 s:55:0 s:55:1 A:0 s:55:2 A:1 s:55:3 A:2 A:3"
 
 
 def tile_moe_adb_relu_kernel(tc, dy_words, dy_scales, wt, wbt, wat, a, gate, offs, out):
@@ -40,36 +42,40 @@ def tile_moe_adb_relu_kernel(tc, dy_words, dy_scales, wt, wbt, wat, a, gate, off
         gate_rows = keep.tile([P, C], F32, name="gate_rows")
         gate_cols = keep.tile([P, 8], F32, name="gate_cols")
         identity = keep.tile([P, P], F32, name="identity")
-        dx = keep.tile([P, K_TILES, T], F32, name="dx")
+        dx = {}
         windows = [keep.tile([P, T], F32, name=f"window{kt}") for kt in range(K_TILES)]
         raw = {}
         saved = {}
 
         def load_weight(name, matrix):
-            raw[name] = keep.tile([P, PACK, WIDTH], F32, name="raw_" + name)
+            raw[name] = ring.tile([P, PACK, WIDTH], F32, name="raw_" + name, tag="raw", bufs=13)
             nc.sync.dma_start(raw[name][:], matrix.rearrange("(p j) c -> p j c", j=PACK))
 
         def load_saved(pair):
-            saved[pair] = keep.tile([P, PACK, PAIR], F32, name=f"saved{pair}")
+            saved[pair] = ring.tile([P, PACK, PAIR], F32, name=f"saved{pair}", tag="saved", bufs=3)
             nc.sync.dma_start(saved[pair][:], a[:, pair * PAIR : (pair + 1) * PAIR].rearrange("(p j) s -> p j s", j=PACK))
 
         nc.vector.memset(scales[:].bitcast(I32), 0)
-        nc.sync.dma_start(words[:], dy_words[0].rearrange("p t d -> p (t d)").bitcast(I32))
-        nc.sync.dma_start(offsets[:], offs)
-        for q in range(4):
-            nc.scalar.dma_start(scales[32 * q : 32 * q + 4, :].bitcast(I32), dy_scales[0, 4 * q : 4 * q + 4, :].bitcast(I32))
-        nc.scalar.dma_start(gate_rows[:], gate.rearrange("r (e u) -> (r e) u", u=C)[0:P, :])
-        load_weight("wb0", wbt[0])
+        matrices = {"w": wt}
         for e in range(E):
-            if e + 1 < E:
-                load_weight(f"wb{e + 1}", wbt[e + 1])
-            if e == 0 or (e % 2 == 1 and e + 1 < E):
-                load_saved((e + 1) // 2)
-            load_weight(f"wa{e}", wat[e])
-        load_weight("w", wt)
+            matrices[f"wb{e}"] = wbt[e]
+            matrices[f"wa{e}"] = wat[e]
+        for name in LOADS.split():
+            if name == "dy":
+                nc.sync.dma_start(words[:], dy_words[0].rearrange("p t d -> p (t d)").bitcast(I32))
+                nc.sync.dma_start(offsets[:], offs)
+            elif name == "gate":
+                nc.sync.dma_start(gate_rows[:], gate.rearrange("r (e u) -> (r e) u", u=C)[0:P, :])
+            elif name == "sc":
+                for q in range(4):
+                    nc.sync.dma_start(scales[32 * q : 32 * q + 4, :].bitcast(I32), dy_scales[0, 4 * q : 4 * q + 4, :].bitcast(I32))
+            elif name[0] == "a":
+                load_saved(int(name[1]))
+            else:
+                load_weight(name, matrices[name])
 
         make_identity(nc, identity[:])
-        turned_gate = psum.tile([P, P], F32, name="turned_gate", tag="turned", bufs=1)
+        turned_gate = psum.tile([P, P], F32, name="turned_gate", tag="turned")
         nc.tensor.transpose(turned_gate[:], gate_rows[:], identity[:])
         nc.scalar.activation(gate_cols[:], turned_gate[:, 0:8], COPY)
 
@@ -77,24 +83,25 @@ def tile_moe_adb_relu_kernel(tc, dy_words, dy_scales, wt, wbt, wat, a, gate, off
         codes = {}
         planes = {}
 
-        def round_weight(name):
-            grouped[name] = ring.tile([P, WIDTH, PACK], BF16, name="grouped", tag="grouped", bufs=4, align_bytes=64)
-            split = WIDTH - VECTOR_COLS.get(name, 0)
-            half = min(split, WIDTH // 2)
-            for engine, lo, hi in ((nc.scalar.copy, 0, half), (nc.scalar.copy, half, split), (nc.vector.tensor_copy, split, WIDTH)):
-                if hi > lo:
-                    engine(
-                        grouped[name][:, lo:hi, :].rearrange("p (c i) j -> p c j i", i=LINE),
-                        raw[name][:, :, lo:hi].rearrange("p j (c i) -> p c j i", i=LINE),
-                    )
+        def round_weight(name, part, engine):
+            grouped[name, part] = ring.tile([P, HALF, PACK], BF16, name="grouped", tag="order", bufs=30, align_bytes=64)
+            source = raw[name][:, :, part * HALF : (part + 1) * HALF]
+            if engine == "g":
+                nc.gpsimd.tensor_scalar(grouped[name, part][:], source.rearrange("p j c -> p c j"), 1.0, 0.0, ALU.mult, ALU.add)
+            else:
+                copy = nc.scalar.copy if engine == "s" else nc.vector.tensor_copy
+                copy(
+                    grouped[name, part][:].rearrange("p (c i) j -> p c j i", i=LINE),
+                    source.rearrange("p j (c i) -> p c j i", i=LINE),
+                )
 
-        def quantise_weight(name):
-            codes[name] = ring.tile([P, WIDTH], U32, name="codes", tag="codes", bufs=6, align_bytes=64)
-            planes[name] = ring.tile([P, WIDTH], U8, name="planes", tag="planes", bufs=6, align_bytes=64)
+        def quantise_weight(name, part):
+            codes[name, part] = ring.tile([P, HALF], U32, name="codes", tag="order", bufs=30, align_bytes=64)
+            planes[name, part] = ring.tile([P, HALF], U8, name="planes", tag="planes", bufs=26, align_bytes=64)
             nc.vector.quantize_mx(
-                out=codes[name][:].bitcast(FP8X4),
-                scales=planes[name][:],
-                in_=grouped[name][:].rearrange("p c j -> p (c j)"),
+                out=codes[name, part][:].bitcast(FP8X4),
+                scales=planes[name, part][:],
+                in_=grouped[name, part][:].rearrange("p c j -> p (c j)"),
             )
 
         def gather(pair):
@@ -104,112 +111,134 @@ def tile_moe_adb_relu_kernel(tc, dy_words, dy_scales, wt, wbt, wat, a, gate, off
             nc.vector.tensor_copy(slot_scales[:, cols], scales[:].indirect(entries))
 
         turned = {}
+        dh = {}
+        product = {}
         dh_codes = {}
         dh_planes = {}
 
         def inner_sums(e):
             slots = slice(e * C, (e + 1) * C)
             sums = psum.tile([P, H], F32, name="sums", tag="sums")
-            nc.tensor.matmul_mx(
-                out=sums[:],
-                lhsT=slot_words[:, slots].bitcast(FP8X4),
-                lhsT_scale=slot_scales[:, slots],
-                rhs=codes[f"wb{e}"][:].bitcast(FP8X4),
-                rhs_scale=planes[f"wb{e}"][:],
-                start=True,
-                stop=True,
-            )
-            gated = ring.tile([P, H], F32, name="gated")
+            for part in range(2):
+                nc.tensor.matmul_mx(
+                    out=sums[:, part * HALF : (part + 1) * HALF],
+                    lhsT=slot_words[:, slots].bitcast(FP8X4),
+                    lhsT_scale=slot_scales[:, slots],
+                    rhs=codes[f"wb{e}", part][:].bitcast(FP8X4),
+                    rhs_scale=planes[f"wb{e}", part][:],
+                    start=True,
+                    stop=True,
+                )
+            gated = ring.tile([P, H], F32, name="gated", tag="order", bufs=30, align_bytes=64)
             nc.scalar.activation(gated[:], sums[:], COPY, scale=gate_cols[:, e : e + 1])
-            turned[e] = psum.tile([P, PACK, C], F32, name="turned", tag="turned", bufs=1)
+            turned[e] = psum.tile([P, PACK, C], F32, name="turned", tag="turned")
             for j in range(PACK):
                 nc.tensor.transpose(turned[e][:, j, :], gated[:, j:H:PACK], identity[:])
 
         def inner_gradient(e):
-            dh = ring.tile([P, C, PACK], BF16, name="dh", align_bytes=64)
+            dh[e] = ring.tile([P, C, PACK], BF16, name="dh", tag="order", bufs=30, align_bytes=64)
             lo = (e % 2) * C
             nc.vector.scalar_tensor_tensor(
-                out=dh[:],
+                out=dh[e][:],
                 in0=saved[e // 2][:, :, lo : lo + C].rearrange("p j s -> p s j"),
                 scalar=0.0,
                 in1=turned[e][:].rearrange("p j s -> p s j"),
                 op0=ALU.is_gt,
                 op1=ALU.mult,
             )
-            dh_codes[e] = ring.tile([P, C], U32, name="dh_codes", tag="dh_codes", bufs=3, align_bytes=64)
-            dh_planes[e] = ring.tile([P, C], U8, name="dh_planes", tag="dh_planes", bufs=3, align_bytes=64)
+
+        def quantise_gradient(e):
+            dh_codes[e] = ring.tile([P, C], U32, name="dh_codes", tag="order", bufs=30, align_bytes=64)
+            dh_planes[e] = ring.tile([P, C], U8, name="dh_planes", tag="dh_planes", bufs=6, align_bytes=64)
             nc.vector.quantize_mx(
                 out=dh_codes[e][:].bitcast(FP8X4),
                 scales=dh_planes[e][:],
-                in_=dh[:].rearrange("p s j -> p (s j)"),
+                in_=dh[e][:].rearrange("p s j -> p (s j)"),
             )
 
         def adapter_product(e):
-            product = psum.tile([P, K_TILES, C], F32, name="product", tag="turned" if e + 1 < E else "last", bufs=1)
+            product[e] = psum.tile([P, K_TILES, C], F32, name="product", tag="product")
             for kt in range(K_TILES):
-                cols = slice(kt * P, (kt + 1) * P)
+                cols = slice(kt % 2 * P, (kt % 2 + 1) * P)
                 nc.tensor.matmul_mx(
-                    out=product[:, kt, :],
-                    lhsT=codes[f"wa{e}"][:, cols].bitcast(FP8X4),
-                    lhsT_scale=planes[f"wa{e}"][:, cols],
+                    out=product[e][:, kt, :],
+                    lhsT=codes[f"wa{e}", kt // 2][:, cols].bitcast(FP8X4),
+                    lhsT_scale=planes[f"wa{e}", kt // 2][:, cols],
                     rhs=dh_codes[e][:].bitcast(FP8X4),
                     rhs_scale=dh_planes[e][:],
                     start=True,
                     stop=True,
                 )
-            nc.scalar.copy(dx[:, :, e * C : (e + 1) * C], product[:])
+
+        def leave(e, lo, hi):
+            part = ring.tile([P, hi - lo, C], F32, name="dx", tag="order", bufs=30, align_bytes=64)
+            nc.scalar.copy(part[:], product[e][:, lo:hi, :])
+            for kt in range(lo, hi):
+                dx[e, kt] = part[:, kt - lo, :]
 
         def scatter(first, last, kt):
             entries = offsets[:, first * C // 16 : (last + 1) * C // 16]
-            nc.vector.tensor_copy(windows[kt][:].indirect(entries), dx[:, kt, first * C : (last + 1) * C])
+            nc.vector.tensor_copy(windows[kt][:].indirect(entries), dx[first, kt])
 
-        round_weight("wb0")
-        gather(0)
-        quantise_weight("wb0")
-        inner_sums(0)
-        round_weight("wb1")
-        inner_gradient(0)
-        quantise_weight("wb1")
-        inner_sums(1)
-        round_weight("wa0")
-        quantise_weight("wa0")
-        gather(1)
-        round_weight("wb2")
-        gather(2)
-        round_weight("wa1")
-        for e in range(E - 1):
-            inner_gradient(e + 1)
-            adapter_product(e)
-            if e + 2 < E:
-                quantise_weight(f"wb{e + 2}")
-                inner_sums(e + 2)
-            quantise_weight(f"wa{e + 1}")
-            for kt in range(K_TILES):
-                scatter(e, e, kt)
-            if e + 3 < E:
-                round_weight(f"wb{e + 3}")
-            if e + 2 < E:
-                round_weight(f"wa{e + 2}")
-        adapter_product(E - 1)
-        round_weight("w")
-        quantise_weight("w")
-        tails = [psum.tile([P, 2, T - WIDTH], F32, name=f"tail{h}", tag="sums") for h in range(2)]
-        for kt in range(K_TILES):
-            cols = slice(kt * P, (kt + 1) * P)
-            head = psum.tile([P, WIDTH], F32, name="head", tag="base", bufs=4)
-            parts = ((head[:], slice(0, WIDTH)), (tails[kt // 2][:, kt % 2, :], slice(WIDTH, T)))
-            for bank, tokens in parts:
+        heads = {}
+        tails = {}
+
+        def frozen_product(kt):
+            cols = slice(kt % 2 * P, (kt % 2 + 1) * P)
+            if kt % 2 == 0:
+                tails[kt // 2] = psum.tile([P, 2, T - WIDTH], F32, name="tail", tag="sums")
+            head = psum.tile([P, WIDTH], F32, name="head", tag=("base", "turned")[kt % 2])
+            heads[kt] = ((head[:], slice(0, WIDTH)), (tails[kt // 2][:, kt % 2, :], slice(WIDTH, T)))
+            for bank, tokens in heads[kt]:
                 nc.tensor.matmul_mx(
                     out=bank,
-                    lhsT=codes["w"][:, cols].bitcast(FP8X4),
-                    lhsT_scale=planes["w"][:, cols],
+                    lhsT=codes["w", kt // 2][:, cols].bitcast(FP8X4),
+                    lhsT_scale=planes["w", kt // 2][:, cols],
                     rhs=words[:, tokens].bitcast(FP8X4),
                     rhs_scale=scales[:, tokens],
                     start=True,
                     stop=True,
                 )
-            scatter(E - 1, E - 1, kt)
+
+        bases = {}
+
+        def park(kt):
+            bases[kt] = ring.tile([P, T], F32, name="base", tag="base")
+            for bank, tokens in heads[kt]:
+                nc.scalar.copy(bases[kt][:, tokens], bank)
+
+        def finish(kt):
             result = ring.tile([P, T], F32, name="result", tag="result", bufs=4)
-            for bank, tokens in parts:
-                nc.vector.tensor_tensor(result[:, tokens], bank, windows[kt][:, tokens], ALU.add)
-            nc.sync.dma_start(out[cols, :], result[:])
+            if kt in bases:
+                nc.gpsimd.tensor_tensor(result[:], bases[kt][:], windows[kt][:], ALU.add)
+            else:
+                for bank, tokens in heads[kt]:
+                    nc.vector.tensor_tensor(result[:, tokens], bank, windows[kt][:, tokens], ALU.add)
+            nc.sync.dma_start(out[kt * P : (kt + 1) * P, :], result[:])
+
+        for step in STEPS.split():
+            kind, *arg = step.split(":")
+            if kind == "c":
+                round_weight(arg[0], int(arg[1]), arg[2])
+            elif kind == "Q":
+                quantise_weight(arg[0], int(arg[1]))
+            elif kind == "g":
+                gather(int(arg[0]))
+            elif kind == "G":
+                inner_sums(int(arg[0]))
+            elif kind == "M":
+                inner_gradient(int(arg[0]))
+            elif kind == "q":
+                quantise_gradient(int(arg[0]))
+            elif kind == "P":
+                adapter_product(int(arg[0]))
+            elif kind == "d":
+                leave(int(arg[0]), int(arg[1]), int(arg[2]))
+            elif kind == "s":
+                scatter(int(arg[0][0]), int(arg[0][-1]), int(arg[1]))
+            elif kind == "B":
+                frozen_product(int(arg[0]))
+            elif kind == "E":
+                park(int(arg[0]))
+            else:
+                finish(int(arg[0]))

@@ -23,8 +23,8 @@ LINE = 4
 K_TILES = K // P
 PAIR = 2 * C
 HALF = WIDTH // 2
-LOADS = "dy gate wb0 sc wa0 a0 wb1 wa1 wb2 wb3 wa2 a1 wb4 wa4 wa3 wb5 a2 w wa5"
-STEPS = "c:wb0:0:s c:wb0:1:v g:0 Q:wb0:1 Q:wb0:0 c:wa0:0:s g:1 c:wa0:1:v Q:wa0:1 G:0 Q:wa0:0 M:0 q:0 c:wb1:1:s P:0 c:wb1:0:v Q:wb1:1 d:0:0:2 Q:wb1:0 G:1 c:wa1:0:s c:wa1:1:v M:1 Q:wa1:1 q:1 d:0:2:4 Q:wa1:0 P:1 c:wb2:1:s c:wb2:0:s d:1:0:2 Q:wb2:0 Q:wb2:1 d:1:2:4 s:00:2 c:wa2:0:v c:wb3:1:s Q:wa2:0 G:2 M:2 c:wb3:0:s Q:wb3:0 Q:wb3:1 c:wa2:1:s q:2 c:wb4:0:s s:00:1 s:00:0 s:00:3 Q:wa2:1 P:2 G:3 d:2:2:4 Q:wb4:0 c:wb4:1:s M:3 d:2:0:2 Q:wb4:1 c:wa3:0:v s:11:1 s:11:2 c:wa3:1:s Q:wa3:0 q:3 c:wa4:0:s g:2 Q:wa3:1 c:wb5:0:s s:11:0 s:22:1 s:11:3 G:4 c:wa4:1:v P:3 d:3:0:2 Q:wb5:0 c:wb5:1:s Q:wa4:0 Q:wb5:1 M:4 Q:wa4:1 c:wa5:1:s q:4 s:33:1 Q:wa5:1 s:22:3 s:22:0 d:3:2:4 s:22:2 s:33:0 G:5 c:wa5:0:s M:5 P:4 d:4:0:2 s:44:1 c:w:1:s Q:wa5:0 d:4:2:4 q:5 s:33:2 s:44:0 c:w:0:s Q:w:1 s:33:3 P:5 Q:w:0 s:44:2 d:5:0:2 d:5:2:4 s:44:3 B:0 B:1 B:2 B:3 s:55:0 s:55:1 A:0 s:55:2 A:1 s:55:3 A:2 A:3"
+LOADS = "dy gate wb0 sc a0 wa0 wb1 wb2 wa1 a1 wb3 wa2 wb4 wa3 a2 wb5 wa4 wa5 w"
+STEPS = "g:0 c:wb0:0:v c:wb0:1:s Q:wb0:0 Q:wb0:1 G:0 g:1 c:wa0:0:v c:wa0:1:s Q:wa0:0 M:0 Q:wa0:1 q:0 c:wb1:0:v c:wb1:1:s P:0:0 P:0:1 Q:wb1:0 Q:wb1:1 g:2 d:0:0:2 d:0:2:4 s:00:0 s:00:1 s:00:2 s:00:3 c:wb2:0:s G:1 c:wb2:1:s Q:wb2:0 M:1 c:wa1:0:s Q:wb2:1 q:1 c:wa1:1:s Q:wa1:0 P:1:0 c:wb3:0:v G:2 Q:wa1:1 P:1:1 d:1:0:2 s:11:0 s:11:1 c:wb3:1:s M:2 Q:wb3:0 q:2 Q:wb3:1 c:wa2:0:s Q:wa2:0 P:2:0 d:1:2:4 s:11:2 s:11:3 c:wa2:1:s G:3 Q:wa2:1 P:2:1 d:2:0:2 s:22:0 s:22:1 c:wb4:0:s M:3 c:wb4:1:s Q:wb4:0 q:3 Q:wb4:1 c:wa3:0:s Q:wa3:0 P:3:0 d:2:2:4 s:22:2 s:22:3 c:wa3:1:s G:4 Q:wa3:1 P:3:1 d:3:0:2 s:33:0 s:33:1 c:wb5:0:s M:4 c:wb5:1:s Q:wb5:0 q:4 Q:wb5:1 c:wa4:0:s Q:wa4:0 P:4:0 d:3:2:4 s:33:2 s:33:3 c:wa4:1:s G:5 Q:wa4:1 P:4:1 d:4:0:2 s:44:0 s:44:1 c:wa5:0:s M:5 c:wa5:1:s Q:wa5:0 q:5 P:5:0 Q:wa5:1 P:5:1 c:w:0:s c:w:1:s Q:w:0 Q:w:1 B:0 B:1 B:2 B:3 d:4:2:3 s:44:2 d:5:0:2 s:55:0 s:55:1 E:0 E:1 d:5:2:3 s:55:2 d:4:3:4 s:44:3 d:5:3:4 s:55:3 A:0 A:1 A:2 A:3"
 
 
 def tile_moe_adb_relu_kernel(tc, dy_words, dy_scales, wt, wbt, wat, a, gate, offs, out):
@@ -84,19 +84,22 @@ def tile_moe_adb_relu_kernel(tc, dy_words, dy_scales, wt, wbt, wat, a, gate, off
         planes = {}
 
         def round_weight(name, part, engine):
-            grouped[name, part] = ring.tile([P, HALF, PACK], BF16, name="grouped", tag="order", bufs=30, align_bytes=64)
+            if engine in "gS":
+                grouped[name, part] = ring.tile([P, HALF, PACK], BF16, name="handed", tag="handed", bufs=1, align_bytes=64)
+            else:
+                grouped[name, part] = ring.tile([P, HALF, PACK], BF16, name="grouped", tag="order", bufs=24, align_bytes=64)
             source = raw[name][:, :, part * HALF : (part + 1) * HALF]
             if engine == "g":
                 nc.gpsimd.tensor_scalar(grouped[name, part][:], source.rearrange("p j c -> p c j"), 1.0, 0.0, ALU.mult, ALU.add)
             else:
-                copy = nc.scalar.copy if engine == "s" else nc.vector.tensor_copy
+                copy = nc.scalar.copy if engine in "sS" else nc.vector.tensor_copy
                 copy(
                     grouped[name, part][:].rearrange("p (c i) j -> p c j i", i=LINE),
                     source.rearrange("p j (c i) -> p c j i", i=LINE),
                 )
 
         def quantise_weight(name, part):
-            codes[name, part] = ring.tile([P, HALF], U32, name="codes", tag="order", bufs=30, align_bytes=64)
+            codes[name, part] = ring.tile([P, HALF], U32, name="codes", tag="order", bufs=24, align_bytes=64)
             planes[name, part] = ring.tile([P, HALF], U8, name="planes", tag="planes", bufs=26, align_bytes=64)
             nc.vector.quantize_mx(
                 out=codes[name, part][:].bitcast(FP8X4),
@@ -129,14 +132,14 @@ def tile_moe_adb_relu_kernel(tc, dy_words, dy_scales, wt, wbt, wat, a, gate, off
                     start=True,
                     stop=True,
                 )
-            gated = ring.tile([P, H], F32, name="gated", tag="order", bufs=30, align_bytes=64)
+            gated = ring.tile([P, H], F32, name="gated", tag="order", bufs=24, align_bytes=64)
             nc.scalar.activation(gated[:], sums[:], COPY, scale=gate_cols[:, e : e + 1])
             turned[e] = psum.tile([P, PACK, C], F32, name="turned", tag="turned")
             for j in range(PACK):
                 nc.tensor.transpose(turned[e][:, j, :], gated[:, j:H:PACK], identity[:])
 
         def inner_gradient(e):
-            dh[e] = ring.tile([P, C, PACK], BF16, name="dh", tag="order", bufs=30, align_bytes=64)
+            dh[e] = ring.tile([P, C, PACK], BF16, name="dh", tag="order", bufs=24, align_bytes=64)
             lo = (e % 2) * C
             nc.vector.scalar_tensor_tensor(
                 out=dh[e][:],
@@ -148,7 +151,7 @@ def tile_moe_adb_relu_kernel(tc, dy_words, dy_scales, wt, wbt, wat, a, gate, off
             )
 
         def quantise_gradient(e):
-            dh_codes[e] = ring.tile([P, C], U32, name="dh_codes", tag="order", bufs=30, align_bytes=64)
+            dh_codes[e] = ring.tile([P, C], U32, name="dh_codes", tag="order", bufs=24, align_bytes=64)
             dh_planes[e] = ring.tile([P, C], U8, name="dh_planes", tag="dh_planes", bufs=6, align_bytes=64)
             nc.vector.quantize_mx(
                 out=dh_codes[e][:].bitcast(FP8X4),
@@ -156,12 +159,12 @@ def tile_moe_adb_relu_kernel(tc, dy_words, dy_scales, wt, wbt, wat, a, gate, off
                 in_=dh[e][:].rearrange("p s j -> p (s j)"),
             )
 
-        def adapter_product(e):
-            product[e] = psum.tile([P, K_TILES, C], F32, name="product", tag="product")
-            for kt in range(K_TILES):
+        def adapter_product(e, h):
+            product[e, h] = psum.tile([P, 2, C], F32, name="product", tag="product")
+            for kt in (2 * h, 2 * h + 1):
                 cols = slice(kt % 2 * P, (kt % 2 + 1) * P)
                 nc.tensor.matmul_mx(
-                    out=product[e][:, kt, :],
+                    out=product[e, h][:, kt % 2, :],
                     lhsT=codes[f"wa{e}", kt // 2][:, cols].bitcast(FP8X4),
                     lhsT_scale=planes[f"wa{e}", kt // 2][:, cols],
                     rhs=dh_codes[e][:].bitcast(FP8X4),
@@ -171,8 +174,8 @@ def tile_moe_adb_relu_kernel(tc, dy_words, dy_scales, wt, wbt, wat, a, gate, off
                 )
 
         def leave(e, lo, hi):
-            part = ring.tile([P, hi - lo, C], F32, name="dx", tag="order", bufs=30, align_bytes=64)
-            nc.scalar.copy(part[:], product[e][:, lo:hi, :])
+            part = ring.tile([P, hi - lo, C], F32, name="dx", tag="order", bufs=24, align_bytes=64)
+            nc.scalar.copy(part[:], product[e, lo // 2][:, lo % 2 : lo % 2 + hi - lo, :])
             for kt in range(lo, hi):
                 dx[e, kt] = part[:, kt - lo, :]
 
@@ -187,7 +190,7 @@ def tile_moe_adb_relu_kernel(tc, dy_words, dy_scales, wt, wbt, wat, a, gate, off
             cols = slice(kt % 2 * P, (kt % 2 + 1) * P)
             if kt % 2 == 0:
                 tails[kt // 2] = psum.tile([P, 2, T - WIDTH], F32, name="tail", tag="sums")
-            head = psum.tile([P, WIDTH], F32, name="head", tag=("base", "turned")[kt % 2])
+            head = psum.tile([P, WIDTH], F32, name="head", tag=("turned", "turned", "base", "base")[kt])
             heads[kt] = ((head[:], slice(0, WIDTH)), (tails[kt // 2][:, kt % 2, :], slice(WIDTH, T)))
             for bank, tokens in heads[kt]:
                 nc.tensor.matmul_mx(
@@ -203,18 +206,22 @@ def tile_moe_adb_relu_kernel(tc, dy_words, dy_scales, wt, wbt, wat, a, gate, off
         bases = {}
 
         def park(kt):
-            bases[kt] = ring.tile([P, T], F32, name="base", tag="base")
+            bases[kt] = ring.tile([P, T], F32, name="base", tag="order", bufs=24, align_bytes=64)
             for bank, tokens in heads[kt]:
                 nc.scalar.copy(bases[kt][:, tokens], bank)
 
         def finish(kt):
-            result = ring.tile([P, T], F32, name="result", tag="result", bufs=4)
+            result = ring.tile([P, T], F32, name="result", tag="order", bufs=24, align_bytes=64)
             if kt in bases:
                 nc.gpsimd.tensor_tensor(result[:], bases[kt][:], windows[kt][:], ALU.add)
             else:
                 for bank, tokens in heads[kt]:
                     nc.vector.tensor_tensor(result[:, tokens], bank, windows[kt][:, tokens], ALU.add)
-            nc.sync.dma_start(out[kt * P : (kt + 1) * P, :], result[:])
+                    if kt == K_TILES - 1:
+                        nc.sync.dma_start(out[kt * P : (kt + 1) * P, tokens], result[:, tokens])
+            if kt < K_TILES - 1:
+                queue = nc.scalar if kt in bases else nc.sync
+                queue.dma_start(out[kt * P : (kt + 1) * P, :], result[:])
 
         for step in STEPS.split():
             kind, *arg = step.split(":")
@@ -231,7 +238,7 @@ def tile_moe_adb_relu_kernel(tc, dy_words, dy_scales, wt, wbt, wat, a, gate, off
             elif kind == "q":
                 quantise_gradient(int(arg[0]))
             elif kind == "P":
-                adapter_product(int(arg[0]))
+                adapter_product(int(arg[0]), int(arg[1]))
             elif kind == "d":
                 leave(int(arg[0]), int(arg[1]), int(arg[2]))
             elif kind == "s":

@@ -22,9 +22,10 @@ WIDTH = 512
 LINE = 4
 K_TILES = K // P
 PAIR = 2 * C
+HANDED = (2, 3, 4)
 HALF = WIDTH // 2
 LOADS = "dy gate wb0 sc a0 wa0 wb1 wb2 wa1 a1 wb3 wa2 wb4 wa3 a2 wb5 wa4 wa5 w"
-STEPS = "g:0 c:wb0:0:v c:wb0:1:s Q:wb0:0 Q:wb0:1 G:0 g:1 c:wa0:0:v c:wa0:1:s Q:wa0:0 M:0 Q:wa0:1 q:0 c:wb1:0:v c:wb1:1:s P:0:0 P:0:1 Q:wb1:0 Q:wb1:1 g:2 d:0:0:2 d:0:2:4 s:00:0 s:00:1 s:00:2 s:00:3 c:wb2:0:s G:1 c:wb2:1:s Q:wb2:0 M:1 c:wa1:0:s Q:wb2:1 q:1 c:wa1:1:s Q:wa1:0 P:1:0 c:wb3:0:v G:2 Q:wa1:1 P:1:1 d:1:0:2 s:11:0 s:11:1 c:wb3:1:s M:2 Q:wb3:0 q:2 Q:wb3:1 c:wa2:0:s Q:wa2:0 P:2:0 d:1:2:4 s:11:2 s:11:3 c:wa2:1:s G:3 Q:wa2:1 P:2:1 d:2:0:2 s:22:0 s:22:1 c:wb4:0:s M:3 c:wb4:1:s Q:wb4:0 q:3 Q:wb4:1 c:wa3:0:s Q:wa3:0 P:3:0 d:2:2:4 s:22:2 s:22:3 c:wa3:1:s G:4 Q:wa3:1 P:3:1 d:3:0:2 s:33:0 s:33:1 c:wb5:0:s M:4 c:wb5:1:s Q:wb5:0 q:4 Q:wb5:1 c:wa4:0:s Q:wa4:0 P:4:0 d:3:2:4 s:33:2 s:33:3 c:wa4:1:s G:5 Q:wa4:1 P:4:1 d:4:0:2 s:44:0 s:44:1 c:wa5:0:s M:5 c:wa5:1:s Q:wa5:0 q:5 P:5:0 Q:wa5:1 P:5:1 c:w:0:s c:w:1:s Q:w:0 Q:w:1 B:0 B:1 B:2 B:3 d:4:2:3 s:44:2 d:5:0:2 s:55:0 s:55:1 E:0 E:1 d:5:2:3 s:55:2 d:4:3:4 s:44:3 d:5:3:4 s:55:3 A:0 A:1 A:2 A:3"
+STEPS = "g:0 c:wb0:0:v c:wb0:1:s Q:wb0:0 Q:wb0:1 G:0 g:1 c:wa0:0:v c:wa0:1:s Q:wa0:0 M:0 Q:wa0:1 q:0 c:wb1:0:v c:wb1:1:s P:0:0 P:0:1 Q:wb1:0 Q:wb1:1 g:2 d:0:0:2 d:0:2:4 s:00:0 s:00:1 s:00:2 s:00:3 c:wb2:0:s G:1 c:wb2:1:s Q:wb2:0 M:1 c:wa1:0:s Q:wb2:1 q:1 c:wa1:1:s Q:wa1:0 P:1:0 c:wb3:0:v G:2 Q:wa1:1 P:1:1 d:1:0:2 s:11:0 s:11:1 c:wb3:1:s c:wa2:0:s Q:wb3:0 Q:wb3:1 M:2 c:wa2:1:s Q:wa2:0 Q:wa2:1 q:2 P:2:0 P:2:1 c:wb4:0:g d:1:2:4 s:11:2 s:11:3 G:3 c:wb4:1:s d:2:0:2 s:22:0 s:22:1 c:wa3:0:s c:wa3:1:s Q:wb4:0 Q:wb4:1 M:3 Q:wa3:0 Q:wa3:1 q:3 P:3:0 P:3:1 c:wb5:0:g d:2:2:4 s:22:2 s:22:3 G:4 c:wb5:1:s d:3:0:2 s:33:0 s:33:1 c:wa4:0:s c:wa4:1:s Q:wb5:0 Q:wb5:1 M:4 Q:wa4:0 Q:wa4:1 q:4 P:4:0 P:4:1 c:wa5:0:g d:3:2:4 s:33:2 s:33:3 G:5 c:wa5:1:s d:4:0:1 s:44:0 c:w:0:s c:w:1:s M:5 Q:wa5:0 q:5 P:5:0 Q:w:0 B:0 B:1 Q:wa5:1 Q:w:1 d:4:1:2 s:44:1 d:5:0:2 s:55:0 s:55:1 P:5:1 E:0 B:2 B:3 d:4:2:4 s:44:2 s:44:3 E:1 d:5:2:4 s:55:2 s:55:3 E:2 A:0 A:1 A:2 A:3"
 
 
 def tile_moe_adb_relu_kernel(tc, dy_words, dy_scales, wt, wbt, wat, a, gate, offs, out):
@@ -139,7 +140,10 @@ def tile_moe_adb_relu_kernel(tc, dy_words, dy_scales, wt, wbt, wat, a, gate, off
                 nc.tensor.transpose(turned[e][:, j, :], gated[:, j:H:PACK], identity[:])
 
         def inner_gradient(e):
-            dh[e] = ring.tile([P, C, PACK], BF16, name="dh", tag="order", bufs=24, align_bytes=64)
+            if e in HANDED:
+                dh[e] = ring.tile([P, C, PACK], BF16, name="dh", tag="handed", bufs=1, align_bytes=64)
+            else:
+                dh[e] = ring.tile([P, C, PACK], BF16, name="dh", tag="order", bufs=24, align_bytes=64)
             lo = (e % 2) * C
             nc.vector.scalar_tensor_tensor(
                 out=dh[e][:],
@@ -160,7 +164,7 @@ def tile_moe_adb_relu_kernel(tc, dy_words, dy_scales, wt, wbt, wat, a, gate, off
             )
 
         def adapter_product(e, h):
-            product[e, h] = psum.tile([P, 2, C], F32, name="product", tag="product")
+            product[e, h] = psum.tile([P, 2, C], F32, name="product", tag="product", bufs=3)
             for kt in (2 * h, 2 * h + 1):
                 cols = slice(kt % 2 * P, (kt % 2 + 1) * P)
                 nc.tensor.matmul_mx(
@@ -190,7 +194,7 @@ def tile_moe_adb_relu_kernel(tc, dy_words, dy_scales, wt, wbt, wat, a, gate, off
             cols = slice(kt % 2 * P, (kt % 2 + 1) * P)
             if kt % 2 == 0:
                 tails[kt // 2] = psum.tile([P, 2, T - WIDTH], F32, name="tail", tag="sums")
-            head = psum.tile([P, WIDTH], F32, name="head", tag=("turned", "turned", "base", "base")[kt])
+            head = psum.tile([P, WIDTH], F32, name="head", tag="turned" if kt < 3 else "base", bufs=2 if kt < 3 else 1)
             heads[kt] = ((head[:], slice(0, WIDTH)), (tails[kt // 2][:, kt % 2, :], slice(WIDTH, T)))
             for bank, tokens in heads[kt]:
                 nc.tensor.matmul_mx(
@@ -212,16 +216,14 @@ def tile_moe_adb_relu_kernel(tc, dy_words, dy_scales, wt, wbt, wat, a, gate, off
 
         def finish(kt):
             result = ring.tile([P, T], F32, name="result", tag="order", bufs=24, align_bytes=64)
-            if kt in bases:
-                nc.gpsimd.tensor_tensor(result[:], bases[kt][:], windows[kt][:], ALU.add)
-            else:
-                for bank, tokens in heads[kt]:
-                    nc.vector.tensor_tensor(result[:, tokens], bank, windows[kt][:, tokens], ALU.add)
-                    if kt == K_TILES - 1:
-                        nc.sync.dma_start(out[kt * P : (kt + 1) * P, tokens], result[:, tokens])
-            if kt < K_TILES - 1:
+            pieces = [slice(0, T)] if kt < 2 else [tokens for bank, tokens in heads[kt]]
+            for n, tokens in enumerate(pieces):
+                if kt in bases:
+                    nc.gpsimd.tensor_tensor(result[:, tokens], bases[kt][:, tokens], windows[kt][:, tokens], ALU.add)
+                else:
+                    nc.vector.tensor_tensor(result[:, tokens], heads[kt][n][0], windows[kt][:, tokens], ALU.add)
                 queue = nc.scalar if kt in bases else nc.sync
-                queue.dma_start(out[kt * P : (kt + 1) * P, :], result[:])
+                queue.dma_start(out[kt * P : (kt + 1) * P, tokens], result[:, tokens])
 
         for step in STEPS.split():
             kind, *arg = step.split(":")

@@ -19,13 +19,14 @@ COPY = mybir.ActivationFunctionType.Copy
 P = 128
 PACK = 4
 WIDTH = 512
+HALF = WIDTH // 2
 LINE = 4
+PER_COLUMN = 16
+BANK = 512
 K_TILES = K // P
 PAIR = 2 * C
-HANDED = (2, 3, 4)
-HALF = WIDTH // 2
-LOADS = "dy gate wb0 sc a0 wa0 wb1 wb2 wa1 a1 wb3 wa2 wb4 wa3 a2 wb5 wa4 wa5 w"
-STEPS = "g:0 c:wb0:0:v c:wb0:1:s Q:wb0:0 Q:wb0:1 G:0 g:1 c:wa0:0:v c:wa0:1:s Q:wa0:0 M:0 Q:wa0:1 q:0 c:wb1:0:v c:wb1:1:s P:0:0 P:0:1 Q:wb1:0 Q:wb1:1 g:2 d:0:0:2 d:0:2:4 s:00:0 s:00:1 s:00:2 s:00:3 c:wb2:0:s G:1 c:wb2:1:s Q:wb2:0 M:1 c:wa1:0:s Q:wb2:1 q:1 c:wa1:1:s Q:wa1:0 P:1:0 c:wb3:0:v G:2 Q:wa1:1 P:1:1 d:1:0:2 s:11:0 s:11:1 c:wb3:1:s c:wa2:0:s Q:wb3:0 Q:wb3:1 M:2 c:wa2:1:s Q:wa2:0 Q:wa2:1 q:2 P:2:0 P:2:1 c:wb4:0:g d:1:2:4 s:11:2 s:11:3 G:3 c:wb4:1:s d:2:0:2 s:22:0 s:22:1 c:wa3:0:s c:wa3:1:s Q:wb4:0 Q:wb4:1 M:3 Q:wa3:0 Q:wa3:1 q:3 P:3:0 P:3:1 c:wb5:0:g d:2:2:4 s:22:2 s:22:3 G:4 c:wb5:1:s d:3:0:2 s:33:0 s:33:1 c:wa4:0:s c:wa4:1:s Q:wb5:0 Q:wb5:1 M:4 Q:wa4:0 Q:wa4:1 q:4 P:4:0 P:4:1 c:wa5:0:g d:3:2:4 s:33:2 s:33:3 G:5 c:wa5:1:s d:4:0:1 s:44:0 c:w:0:s c:w:1:s M:5 Q:wa5:0 q:5 P:5:0 Q:w:0 B:0 B:1 Q:wa5:1 Q:w:1 d:4:1:2 s:44:1 d:5:0:2 s:55:0 s:55:1 P:5:1 E:0 B:2 B:3 d:4:2:4 s:44:2 s:44:3 E:1 d:5:2:4 s:55:2 s:55:3 E:2 A:0 A:1 A:2 A:3"
+STAGED_BUFS = 32
+MATRICES = 2 * E + 1
 
 
 def tile_moe_adb_relu_kernel(tc, dy_words, dy_scales, wt, wbt, wat, a, gate, offs, out):
@@ -35,219 +36,297 @@ def tile_moe_adb_relu_kernel(tc, dy_words, dy_scales, wt, wbt, wat, a, gate, off
         ring = ctx.enter_context(tc.tile_pool(name="ring", bufs=2))
         psum = ctx.enter_context(tc.psum_pool(name="psum", bufs=2))
 
-        offsets = keep.tile([P, T // 16], U16, name="offsets")
+        offsets = keep.tile([P, T // PER_COLUMN], U16, name="offsets")
         words = keep.tile([P, T], I32, name="words", align_bytes=64)
         scales = keep.tile([P, T], U8, name="scales", align_bytes=64)
         slot_words = keep.tile([P, T], U32, name="slot_words", align_bytes=64)
         slot_scales = keep.tile([P, T], U8, name="slot_scales", align_bytes=64)
         gate_rows = keep.tile([P, C], F32, name="gate_rows")
-        gate_cols = keep.tile([P, 8], F32, name="gate_cols")
+        gate_cols = keep.tile([P, E], F32, name="gate_cols")
         identity = keep.tile([P, P], F32, name="identity")
-        dx = {}
         windows = [keep.tile([P, T], F32, name=f"window{kt}") for kt in range(K_TILES)]
+
+        def staged(shape, dtype, name):
+            return ring.tile(shape, dtype, name=name, tag="staged", bufs=STAGED_BUFS, align_bytes=64)
+
         raw = {}
         saved = {}
 
         def load_weight(name, matrix):
-            raw[name] = ring.tile([P, PACK, WIDTH], F32, name="raw_" + name, tag="raw", bufs=13)
-            nc.sync.dma_start(raw[name][:], matrix.rearrange("(p j) c -> p j c", j=PACK))
+            raw[name] = ring.tile([P, PACK, WIDTH], F32, name="raw", tag="raw", bufs=MATRICES)
+            nc.sync.dma_start(raw[name][:], matrix.rearrange("(p r) c -> p r c", r=PACK))
 
         def load_saved(pair):
-            saved[pair] = ring.tile([P, PACK, PAIR], F32, name=f"saved{pair}", tag="saved", bufs=3)
-            nc.sync.dma_start(saved[pair][:], a[:, pair * PAIR : (pair + 1) * PAIR].rearrange("(p j) s -> p j s", j=PACK))
+            saved[pair] = ring.tile([P, PACK, PAIR], F32, name="saved", tag="saved", bufs=E // 2)
+            nc.sync.dma_start(saved[pair][:], a[:, pair * PAIR : (pair + 1) * PAIR].rearrange("(p r) s -> p r s", r=PACK))
 
         nc.vector.memset(scales[:].bitcast(I32), 0)
-        matrices = {"w": wt}
-        for e in range(E):
-            matrices[f"wb{e}"] = wbt[e]
-            matrices[f"wa{e}"] = wat[e]
-        for name in LOADS.split():
-            if name == "dy":
-                nc.sync.dma_start(words[:], dy_words[0].rearrange("p t d -> p (t d)").bitcast(I32))
-                nc.sync.dma_start(offsets[:], offs)
-            elif name == "gate":
-                nc.sync.dma_start(gate_rows[:], gate.rearrange("r (e u) -> (r e) u", u=C)[0:P, :])
-            elif name == "sc":
-                for q in range(4):
-                    nc.sync.dma_start(scales[32 * q : 32 * q + 4, :].bitcast(I32), dy_scales[0, 4 * q : 4 * q + 4, :].bitcast(I32))
-            elif name[0] == "a":
-                load_saved(int(name[1]))
-            else:
-                load_weight(name, matrices[name])
+        nc.sync.dma_start(words[:], dy_words[0].rearrange("p t r -> p (t r)").bitcast(I32))
+        nc.sync.dma_start(offsets[:], offs)
+        nc.sync.dma_start(gate_rows[:], gate.rearrange("q (e u) -> (q e) u", u=C)[0:P, :])
+        load_weight(("wb", 0), wbt[0])
+        for quad in range(4):
+            nc.sync.dma_start(
+                scales[32 * quad : 32 * quad + 4, :].bitcast(I32),
+                dy_scales[0, 4 * quad : 4 * quad + 4, :].bitcast(I32),
+            )
+        load_saved(0)
+        load_weight(("wa", 0), wat[0])
+        load_weight(("wb", 1), wbt[1])
+        for e in range(1, E):
+            if e + 1 < E:
+                load_weight(("wb", e + 1), wbt[e + 1])
+            load_weight(("wa", e), wat[e])
+            if e % 2 == 0:
+                load_saved(e // 2)
+        load_weight(("w", 0), wt)
 
         make_identity(nc, identity[:])
         turned_gate = psum.tile([P, P], F32, name="turned_gate", tag="turned")
         nc.tensor.transpose(turned_gate[:], gate_rows[:], identity[:])
-        nc.scalar.activation(gate_cols[:], turned_gate[:, 0:8], COPY)
+        nc.scalar.activation(gate_cols[:], turned_gate[:, 0:E], COPY)
 
-        grouped = {}
+        rounded = {}
         codes = {}
         planes = {}
 
-        def round_weight(name, part, engine):
-            if engine in "gS":
-                grouped[name, part] = ring.tile([P, HALF, PACK], BF16, name="handed", tag="handed", bufs=1, align_bytes=64)
+        def round_half(half, engine, handed=False):
+            if handed:
+                rounded[half] = ring.tile([P, HALF, PACK], BF16, name="handed", tag="handed", bufs=1, align_bytes=64)
             else:
-                grouped[name, part] = ring.tile([P, HALF, PACK], BF16, name="grouped", tag="order", bufs=24, align_bytes=64)
-            source = raw[name][:, :, part * HALF : (part + 1) * HALF]
-            if engine == "g":
-                nc.gpsimd.tensor_scalar(grouped[name, part][:], source.rearrange("p j c -> p c j"), 1.0, 0.0, ALU.mult, ALU.add)
+                rounded[half] = staged([P, HALF, PACK], BF16, "rounded")
+            source = raw[half[:2]][:, :, half[2] * HALF : (half[2] + 1) * HALF]
+            if engine == "gpsimd":
+                nc.gpsimd.tensor_scalar(rounded[half][:], source.rearrange("p r c -> p c r"), 1.0, 0.0, ALU.mult, ALU.add)
             else:
-                copy = nc.scalar.copy if engine in "sS" else nc.vector.tensor_copy
+                copy = nc.scalar.copy if engine == "scalar" else nc.vector.tensor_copy
                 copy(
-                    grouped[name, part][:].rearrange("p (c i) j -> p c j i", i=LINE),
-                    source.rearrange("p j (c i) -> p c j i", i=LINE),
+                    rounded[half][:].rearrange("p (c i) r -> p c r i", i=LINE),
+                    source.rearrange("p r (c i) -> p c r i", i=LINE),
                 )
 
-        def quantise_weight(name, part):
-            codes[name, part] = ring.tile([P, HALF], U32, name="codes", tag="order", bufs=24, align_bytes=64)
-            planes[name, part] = ring.tile([P, HALF], U8, name="planes", tag="planes", bufs=26, align_bytes=64)
+        def quantise_half(half):
+            codes[half] = staged([P, HALF], U32, "codes")
+            planes[half] = ring.tile([P, HALF], U8, name="planes", tag="planes", bufs=2 * MATRICES, align_bytes=64)
             nc.vector.quantize_mx(
-                out=codes[name, part][:].bitcast(FP8X4),
-                scales=planes[name, part][:],
-                in_=grouped[name, part][:].rearrange("p c j -> p (c j)"),
+                out=codes[half][:].bitcast(FP8X4),
+                scales=planes[half][:],
+                in_=rounded[half][:].rearrange("p c r -> p (c r)"),
             )
 
         def gather(pair):
-            cols = slice(pair * PAIR, (pair + 1) * PAIR)
-            entries = offsets[:, pair * PAIR // 16 : (pair + 1) * PAIR // 16]
-            nc.vector.tensor_copy(slot_words[:, cols], words[:].bitcast(U32).indirect(entries))
-            nc.vector.tensor_copy(slot_scales[:, cols], scales[:].indirect(entries))
+            slots = slice(pair * PAIR, (pair + 1) * PAIR)
+            entries = offsets[:, slots.start // PER_COLUMN : slots.stop // PER_COLUMN]
+            nc.vector.tensor_copy(slot_words[:, slots], words[:].bitcast(U32).indirect(entries))
+            nc.vector.tensor_copy(slot_scales[:, slots], scales[:].indirect(entries))
 
         turned = {}
         dh = {}
-        product = {}
         dh_codes = {}
         dh_planes = {}
 
-        def inner_sums(e):
+        def gated_sums(e):
             slots = slice(e * C, (e + 1) * C)
             sums = psum.tile([P, H], F32, name="sums", tag="sums")
-            for part in range(2):
+            for side in range(2):
                 nc.tensor.matmul_mx(
-                    out=sums[:, part * HALF : (part + 1) * HALF],
+                    out=sums[:, side * HALF : (side + 1) * HALF],
                     lhsT=slot_words[:, slots].bitcast(FP8X4),
                     lhsT_scale=slot_scales[:, slots],
-                    rhs=codes[f"wb{e}", part][:].bitcast(FP8X4),
-                    rhs_scale=planes[f"wb{e}", part][:],
+                    rhs=codes["wb", e, side][:].bitcast(FP8X4),
+                    rhs_scale=planes["wb", e, side][:],
                     start=True,
                     stop=True,
                 )
-            gated = ring.tile([P, H], F32, name="gated", tag="order", bufs=24, align_bytes=64)
+            gated = staged([P, H], F32, "gated")
             nc.scalar.activation(gated[:], sums[:], COPY, scale=gate_cols[:, e : e + 1])
             turned[e] = psum.tile([P, PACK, C], F32, name="turned", tag="turned")
-            for j in range(PACK):
-                nc.tensor.transpose(turned[e][:, j, :], gated[:, j:H:PACK], identity[:])
+            for r in range(PACK):
+                nc.tensor.transpose(turned[e][:, r, :], gated[:, r:H:PACK], identity[:])
 
-        def inner_gradient(e):
-            if e in HANDED:
-                dh[e] = ring.tile([P, C, PACK], BF16, name="dh", tag="handed", bufs=1, align_bytes=64)
-            else:
-                dh[e] = ring.tile([P, C, PACK], BF16, name="dh", tag="order", bufs=24, align_bytes=64)
-            lo = (e % 2) * C
+        def mask(e):
+            dh[e] = staged([P, C, PACK], BF16, "dh")
+            first = (e % 2) * C
             nc.vector.scalar_tensor_tensor(
                 out=dh[e][:],
-                in0=saved[e // 2][:, :, lo : lo + C].rearrange("p j s -> p s j"),
+                in0=saved[e // 2][:, :, first : first + C].rearrange("p r u -> p u r"),
                 scalar=0.0,
-                in1=turned[e][:].rearrange("p j s -> p s j"),
+                in1=turned[e][:].rearrange("p r u -> p u r"),
                 op0=ALU.is_gt,
                 op1=ALU.mult,
             )
 
-        def quantise_gradient(e):
-            dh_codes[e] = ring.tile([P, C], U32, name="dh_codes", tag="order", bufs=24, align_bytes=64)
-            dh_planes[e] = ring.tile([P, C], U8, name="dh_planes", tag="dh_planes", bufs=6, align_bytes=64)
+        def quantise_dh(e):
+            dh_codes[e] = staged([P, C], U32, "dh_codes")
+            dh_planes[e] = ring.tile([P, C], U8, name="dh_planes", tag="dh_planes", bufs=E, align_bytes=64)
             nc.vector.quantize_mx(
                 out=dh_codes[e][:].bitcast(FP8X4),
                 scales=dh_planes[e][:],
-                in_=dh[e][:].rearrange("p s j -> p (s j)"),
+                in_=dh[e][:].rearrange("p u r -> p (u r)"),
             )
 
-        def adapter_product(e, h):
-            product[e, h] = psum.tile([P, 2, C], F32, name="product", tag="product", bufs=3)
-            for kt in (2 * h, 2 * h + 1):
-                cols = slice(kt % 2 * P, (kt % 2 + 1) * P)
+        product = {}
+        dx = {}
+
+        def adapter_product(e, side):
+            product[e, side] = psum.tile([P, 2, C], F32, name="product", tag="product", bufs=3)
+            for place in range(2):
+                cols = slice(place * P, (place + 1) * P)
                 nc.tensor.matmul_mx(
-                    out=product[e, h][:, kt % 2, :],
-                    lhsT=codes[f"wa{e}", kt // 2][:, cols].bitcast(FP8X4),
-                    lhsT_scale=planes[f"wa{e}", kt // 2][:, cols],
+                    out=product[e, side][:, place, :],
+                    lhsT=codes["wa", e, side][:, cols].bitcast(FP8X4),
+                    lhsT_scale=planes["wa", e, side][:, cols],
                     rhs=dh_codes[e][:].bitcast(FP8X4),
                     rhs_scale=dh_planes[e][:],
                     start=True,
                     stop=True,
                 )
 
-        def leave(e, lo, hi):
-            part = ring.tile([P, hi - lo, C], F32, name="dx", tag="order", bufs=24, align_bytes=64)
-            nc.scalar.copy(part[:], product[e, lo // 2][:, lo % 2 : lo % 2 + hi - lo, :])
-            for kt in range(lo, hi):
-                dx[e, kt] = part[:, kt - lo, :]
+        def leave_psum(e, first, count):
+            part = staged([P, count, C], F32, "dx")
+            nc.scalar.copy(part[:], product[e, first // 2][:, first % 2 : first % 2 + count, :])
+            for n in range(count):
+                dx[e, first + n] = part[:, n, :]
 
-        def scatter(first, last, kt):
-            entries = offsets[:, first * C // 16 : (last + 1) * C // 16]
-            nc.vector.tensor_copy(windows[kt][:].indirect(entries), dx[first, kt])
+        def scatter(e, kt):
+            entries = offsets[:, e * C // PER_COLUMN : (e + 1) * C // PER_COLUMN]
+            nc.vector.tensor_copy(windows[kt][:].indirect(entries), dx[e, kt])
 
-        heads = {}
+        def send_back(e, first, count):
+            leave_psum(e, first, count)
+            for kt in range(first, first + count):
+                scatter(e, kt)
+
+        pieces = {}
         tails = {}
+        parked = {}
 
         def frozen_product(kt):
             cols = slice(kt % 2 * P, (kt % 2 + 1) * P)
             if kt % 2 == 0:
-                tails[kt // 2] = psum.tile([P, 2, T - WIDTH], F32, name="tail", tag="sums")
-            head = psum.tile([P, WIDTH], F32, name="head", tag="turned" if kt < 3 else "base", bufs=2 if kt < 3 else 1)
-            heads[kt] = ((head[:], slice(0, WIDTH)), (tails[kt // 2][:, kt % 2, :], slice(WIDTH, T)))
-            for bank, tokens in heads[kt]:
+                tails[kt // 2] = psum.tile([P, 2, T - BANK], F32, name="tail", tag="sums")
+            if kt < K_TILES - 1:
+                head = psum.tile([P, BANK], F32, name="head", tag="turned")
+            else:
+                head = psum.tile([P, BANK], F32, name="head", tag="base", bufs=1)
+            pieces[kt, 0] = (head[:], slice(0, BANK))
+            pieces[kt, 1] = (tails[kt // 2][:, kt % 2, :], slice(BANK, T))
+            for n in range(2):
+                bank, tokens = pieces[kt, n]
                 nc.tensor.matmul_mx(
                     out=bank,
-                    lhsT=codes["w", kt // 2][:, cols].bitcast(FP8X4),
-                    lhsT_scale=planes["w", kt // 2][:, cols],
+                    lhsT=codes["w", 0, kt // 2][:, cols].bitcast(FP8X4),
+                    lhsT_scale=planes["w", 0, kt // 2][:, cols],
                     rhs=words[:, tokens].bitcast(FP8X4),
                     rhs_scale=scales[:, tokens],
                     start=True,
                     stop=True,
                 )
 
-        bases = {}
+        def park(kt, n):
+            bank, tokens = pieces[kt, n]
+            parked[kt, n] = staged([P, tokens.stop - tokens.start], F32, "parked")
+            nc.scalar.copy(parked[kt, n][:], bank)
 
-        def park(kt):
-            bases[kt] = ring.tile([P, T], F32, name="base", tag="order", bufs=24, align_bytes=64)
-            for bank, tokens in heads[kt]:
-                nc.scalar.copy(bases[kt][:, tokens], bank)
-
-        def finish(kt):
-            result = ring.tile([P, T], F32, name="result", tag="order", bufs=24, align_bytes=64)
-            pieces = [slice(0, T)] if kt < 2 else [tokens for bank, tokens in heads[kt]]
-            for n, tokens in enumerate(pieces):
-                if kt in bases:
-                    nc.gpsimd.tensor_tensor(result[:, tokens], bases[kt][:, tokens], windows[kt][:, tokens], ALU.add)
-                else:
-                    nc.vector.tensor_tensor(result[:, tokens], heads[kt][n][0], windows[kt][:, tokens], ALU.add)
-                queue = nc.scalar if kt in bases else nc.sync
-                queue.dma_start(out[kt * P : (kt + 1) * P, tokens], result[:, tokens])
-
-        for step in STEPS.split():
-            kind, *arg = step.split(":")
-            if kind == "c":
-                round_weight(arg[0], int(arg[1]), arg[2])
-            elif kind == "Q":
-                quantise_weight(arg[0], int(arg[1]))
-            elif kind == "g":
-                gather(int(arg[0]))
-            elif kind == "G":
-                inner_sums(int(arg[0]))
-            elif kind == "M":
-                inner_gradient(int(arg[0]))
-            elif kind == "q":
-                quantise_gradient(int(arg[0]))
-            elif kind == "P":
-                adapter_product(int(arg[0]), int(arg[1]))
-            elif kind == "d":
-                leave(int(arg[0]), int(arg[1]), int(arg[2]))
-            elif kind == "s":
-                scatter(int(arg[0][0]), int(arg[0][-1]), int(arg[1]))
-            elif kind == "B":
-                frozen_product(int(arg[0]))
-            elif kind == "E":
-                park(int(arg[0]))
+        def finish(kt, n):
+            bank, tokens = pieces[kt, n]
+            result = staged([P, tokens.stop - tokens.start], F32, "result")
+            if (kt, n) in parked:
+                nc.gpsimd.tensor_tensor(result[:], parked[kt, n][:], windows[kt][:, tokens], ALU.add)
+                nc.scalar.dma_start(out[kt * P : (kt + 1) * P, tokens], result[:])
             else:
-                finish(int(arg[0]))
+                nc.vector.tensor_tensor(result[:], bank, windows[kt][:, tokens], ALU.add)
+                nc.sync.dma_start(out[kt * P : (kt + 1) * P, tokens], result[:])
+
+        gather(0)
+        round_half(("wb", 0, 0), "vector")
+        round_half(("wb", 0, 1), "scalar")
+        quantise_half(("wb", 0, 0))
+        quantise_half(("wb", 0, 1))
+        gated_sums(0)
+        gather(1)
+        round_half(("wa", 0, 0), "vector")
+        round_half(("wa", 0, 1), "scalar")
+        quantise_half(("wa", 0, 0))
+        mask(0)
+        quantise_half(("wa", 0, 1))
+        quantise_dh(0)
+        round_half(("wb", 1, 0), "vector")
+        round_half(("wb", 1, 1), "scalar")
+        adapter_product(0, 0)
+        adapter_product(0, 1)
+        quantise_half(("wb", 1, 0))
+        quantise_half(("wb", 1, 1))
+        gather(2)
+
+        leave_psum(0, 0, 2)
+        leave_psum(0, 2, 2)
+        for kt in range(K_TILES):
+            scatter(0, kt)
+        round_half(("wb", 2, 0), "scalar")
+        gated_sums(1)
+        round_half(("wb", 2, 1), "scalar")
+        quantise_half(("wb", 2, 0))
+        mask(1)
+        round_half(("wa", 1, 0), "scalar")
+        quantise_half(("wb", 2, 1))
+        quantise_dh(1)
+        round_half(("wa", 1, 1), "scalar")
+        quantise_half(("wa", 1, 0))
+        adapter_product(1, 0)
+        round_half(("wb", 3, 0), "vector")
+        gated_sums(2)
+        quantise_half(("wa", 1, 1))
+        adapter_product(1, 1)
+
+        for e in range(1, E - 2):
+            ahead = e + 3 < E
+            send_back(e, 0, 2)
+            round_half(("wb", e + 2, 1), "scalar")
+            round_half(("wa", e + 1, 0), "scalar")
+            quantise_half(("wb", e + 2, 0))
+            quantise_half(("wb", e + 2, 1))
+            mask(e + 1)
+            round_half(("wa", e + 1, 1), "scalar", handed=ahead)
+            quantise_half(("wa", e + 1, 0))
+            quantise_dh(e + 1)
+            adapter_product(e + 1, 0)
+            quantise_half(("wa", e + 1, 1))
+            adapter_product(e + 1, 1)
+            if ahead:
+                round_half(("wb", e + 3, 0), "gpsimd", handed=True)
+            send_back(e, 2, 2)
+            gated_sums(e + 2)
+
+        before, last = E - 2, E - 1
+        round_half(("wa", last, 0), "scalar")
+        send_back(before, 0, 1)
+        round_half(("wa", last, 1), "scalar")
+        round_half(("w", 0, 0), "scalar")
+        mask(last)
+        quantise_half(("wa", last, 0))
+        quantise_dh(last)
+        adapter_product(last, 0)
+        quantise_half(("wa", last, 1))
+        adapter_product(last, 1)
+        quantise_half(("w", 0, 0))
+        frozen_product(0)
+        frozen_product(1)
+        send_back(before, 1, 1)
+        round_half(("w", 0, 1), "scalar")
+        quantise_half(("w", 0, 1))
+        frozen_product(2)
+        frozen_product(3)
+        send_back(last, 0, 2)
+        park(0, 0)
+        park(1, 0)
+        send_back(before, 2, 2)
+        park(0, 1)
+        park(1, 1)
+        send_back(last, 2, 2)
+        for n in range(2):
+            finish(0, n)
+            finish(1, n)
+        for kt in (2, 3):
+            finish(kt, 0)
+            finish(kt, 1)

@@ -27,6 +27,8 @@ K_TILES = K // P
 PAIR = 2 * C
 STAGED_BUFS = 32
 MATRICES = 2 * E + 1
+WHOLE_BUFS = 11
+HALF_BUFS = 4
 
 
 def tile_moe_adb_relu_kernel(tc, dy_words, dy_scales, wt, wbt, wat, a, gate, offs, out):
@@ -39,71 +41,56 @@ def tile_moe_adb_relu_kernel(tc, dy_words, dy_scales, wt, wbt, wat, a, gate, off
         offsets = keep.tile([P, T // PER_COLUMN], U16, name="offsets")
         words = keep.tile([P, T], I32, name="words", align_bytes=64)
         scales = keep.tile([P, T], U8, name="scales", align_bytes=64)
-        slot_words = keep.tile([P, T], U32, name="slot_words", align_bytes=64)
-        slot_scales = keep.tile([P, T], U8, name="slot_scales", align_bytes=64)
         gate_rows = keep.tile([P, C], F32, name="gate_rows")
         gate_cols = keep.tile([P, E], F32, name="gate_cols")
         identity = keep.tile([P, P], F32, name="identity")
         windows = [keep.tile([P, T], F32, name=f"window{kt}") for kt in range(K_TILES)]
 
-        def staged(shape, dtype, name):
+        def staged(shape, dtype, name, handed=None):
+            if handed:
+                return ring.tile(shape, dtype, name=name, tag=handed, bufs=1, align_bytes=64)
             return ring.tile(shape, dtype, name=name, tag="staged", bufs=STAGED_BUFS, align_bytes=64)
 
         raw = {}
         saved = {}
 
         def load_weight(name, matrix):
-            raw[name] = ring.tile([P, PACK, WIDTH], F32, name="raw", tag="raw", bufs=MATRICES)
-            nc.sync.dma_start(raw[name][:], matrix.rearrange("(p r) c -> p r c", r=PACK))
+            whole = ring.tile([P, PACK, WIDTH], F32, name="raw", tag="raw", bufs=WHOLE_BUFS)
+            nc.sync.dma_start(whole[:], matrix.rearrange("(p r) c -> p r c", r=PACK))
+            for side in range(2):
+                raw[name + (side,)] = whole[:, :, side * HALF : (side + 1) * HALF]
 
-        def load_saved(pair):
-            saved[pair] = ring.tile([P, PACK, PAIR], F32, name="saved", tag="saved", bufs=E // 2)
-            nc.sync.dma_start(saved[pair][:], a[:, pair * PAIR : (pair + 1) * PAIR].rearrange("(p r) s -> p r s", r=PACK))
+        def load_half(half, matrix):
+            part = ring.tile([P, PACK, HALF], F32, name="raw_half", tag="raw_half", bufs=HALF_BUFS)
+            cols = slice(half[2] * HALF, (half[2] + 1) * HALF)
+            nc.sync.dma_start(part[:], matrix[:, cols].rearrange("(p r) c -> p r c", r=PACK))
+            raw[half] = part[:]
 
-        nc.vector.memset(scales[:].bitcast(I32), 0)
-        nc.sync.dma_start(words[:], dy_words[0].rearrange("p t r -> p (t r)").bitcast(I32))
-        nc.sync.dma_start(offsets[:], offs)
-        nc.sync.dma_start(gate_rows[:], gate.rearrange("q (e u) -> (q e) u", u=C)[0:P, :])
-        load_weight(("wb", 0), wbt[0])
-        for quad in range(4):
-            nc.sync.dma_start(
-                scales[32 * quad : 32 * quad + 4, :].bitcast(I32),
-                dy_scales[0, 4 * quad : 4 * quad + 4, :].bitcast(I32),
-            )
-        load_saved(0)
-        load_weight(("wa", 0), wat[0])
-        load_weight(("wb", 1), wbt[1])
-        for e in range(1, E):
-            if e + 1 < E:
-                load_weight(("wb", e + 1), wbt[e + 1])
-            load_weight(("wa", e), wat[e])
-            if e % 2 == 0:
-                load_saved(e // 2)
-        load_weight(("w", 0), wt)
-
-        make_identity(nc, identity[:])
-        turned_gate = psum.tile([P, P], F32, name="turned_gate", tag="turned")
-        nc.tensor.transpose(turned_gate[:], gate_rows[:], identity[:])
-        nc.scalar.activation(gate_cols[:], turned_gate[:, 0:E], COPY)
+        def load_saved(first, count):
+            part = keep.tile([P, PACK, count * C], F32, name=f"saved{first}")
+            nc.sync.dma_start(part[:], a[:, first * C : (first + count) * C].rearrange("(p r) s -> p r s", r=PACK))
+            for n in range(count):
+                saved[first + n] = part[:, :, n * C : (n + 1) * C]
 
         rounded = {}
         codes = {}
         planes = {}
 
-        def round_half(half, engine, handed=False):
-            if handed:
-                rounded[half] = ring.tile([P, HALF, PACK], BF16, name="handed", tag="handed", bufs=1, align_bytes=64)
-            else:
-                rounded[half] = staged([P, HALF, PACK], BF16, "rounded")
-            source = raw[half[:2]][:, :, half[2] * HALF : (half[2] + 1) * HALF]
+        def lines(written, read):
+            return (
+                written.rearrange("p (c i) r -> p c r i", i=LINE),
+                read.rearrange("p r (c i) -> p c r i", i=LINE),
+            )
+
+        def round_half(half, engine, handed=None):
+            rounded[half] = staged([P, HALF, PACK], BF16, "rounded", handed)
+            written, read = lines(rounded[half][:], raw[half])
             if engine == "gpsimd":
-                nc.gpsimd.tensor_scalar(rounded[half][:], source.rearrange("p r c -> p c r"), 1.0, 0.0, ALU.mult, ALU.add)
+                nc.gpsimd.tensor_copy(rounded[half][:], raw[half].rearrange("p r c -> p c r"))
+            elif engine == "scalar":
+                nc.scalar.copy(written, read)
             else:
-                copy = nc.scalar.copy if engine == "scalar" else nc.vector.tensor_copy
-                copy(
-                    rounded[half][:].rearrange("p (c i) r -> p c r i", i=LINE),
-                    source.rearrange("p r (c i) -> p c r i", i=LINE),
-                )
+                nc.vector.tensor_copy(written, read)
 
         def quantise_half(half):
             codes[half] = staged([P, HALF], U32, "codes")
@@ -114,46 +101,60 @@ def tile_moe_adb_relu_kernel(tc, dy_words, dy_scales, wt, wbt, wat, a, gate, off
                 in_=rounded[half][:].rearrange("p c r -> p (c r)"),
             )
 
-        def gather(pair):
-            slots = slice(pair * PAIR, (pair + 1) * PAIR)
-            entries = offsets[:, slots.start // PER_COLUMN : slots.stop // PER_COLUMN]
-            nc.vector.tensor_copy(slot_words[:, slots], words[:].bitcast(U32).indirect(entries))
-            nc.vector.tensor_copy(slot_scales[:, slots], scales[:].indirect(entries))
+        slot_words = {}
+        slot_scales = {}
 
+        def gather(pair, words_tag, scales_tag):
+            entries = offsets[:, pair * PAIR // PER_COLUMN : (pair + 1) * PAIR // PER_COLUMN]
+            slot_words[pair] = staged([P, PAIR], U32, "slot_words", words_tag)
+            nc.vector.tensor_copy(slot_words[pair][:], words[:].bitcast(U32).indirect(entries))
+            slot_scales[pair] = staged([P, PAIR], U8, "slot_scales", scales_tag)
+            nc.vector.tensor_copy(slot_scales[pair][:], scales[:].indirect(entries))
+
+        sums = {}
         turned = {}
+        positive = {}
         dh = {}
         dh_codes = {}
         dh_planes = {}
 
-        def gated_sums(e):
-            slots = slice(e * C, (e + 1) * C)
-            sums = psum.tile([P, H], F32, name="sums", tag="sums")
+        def first_product(e):
+            slots = slice(e % 2 * C, (e % 2 + 1) * C)
+            sums[e] = psum.tile([P, H], F32, name="sums", tag="sums")
             for side in range(2):
                 nc.tensor.matmul_mx(
-                    out=sums[:, side * HALF : (side + 1) * HALF],
-                    lhsT=slot_words[:, slots].bitcast(FP8X4),
-                    lhsT_scale=slot_scales[:, slots],
+                    out=sums[e][:, side * HALF : (side + 1) * HALF],
+                    lhsT=slot_words[e // 2][:, slots].bitcast(FP8X4),
+                    lhsT_scale=slot_scales[e // 2][:, slots],
                     rhs=codes["wb", e, side][:].bitcast(FP8X4),
                     rhs_scale=planes["wb", e, side][:],
                     start=True,
                     stop=True,
                 )
-            gated = staged([P, H], F32, "gated")
-            nc.scalar.activation(gated[:], sums[:], COPY, scale=gate_cols[:, e : e + 1])
-            turned[e] = psum.tile([P, PACK, C], F32, name="turned", tag="turned")
-            for r in range(PACK):
-                nc.tensor.transpose(turned[e][:, r, :], gated[:, r:H:PACK], identity[:])
+
+        def gate_and_turn(e):
+            gated = staged([P, 2, P, 2], BF16, "gated")
+            nc.scalar.activation(
+                gated[:], sums[e][:].rearrange("u (p h j) -> u h p j", h=2, j=2), COPY, scale=gate_cols[:, e : e + 1]
+            )
+            pairs = gated[:].rearrange("u h p j -> u (h p j)").bitcast(F32)
+            turned[e] = psum.tile([P, 2, C], F32, name="turned", tag="turned")
+            for h in range(2):
+                nc.tensor.transpose(turned[e][:, h, :], pairs[:, h * P : (h + 1) * P], identity[:])
+
+        def compare(e, engine, handed=None):
+            positive[e] = staged([P, C, PACK], BF16, "positive", handed)
+            written, read = lines(positive[e][:], saved[e])
+            engine.tensor_scalar(written, read, 0.0, 1.0, ALU.is_gt, ALU.mult)
 
         def mask(e):
             dh[e] = staged([P, C, PACK], BF16, "dh")
-            first = (e % 2) * C
-            nc.vector.scalar_tensor_tensor(
-                out=dh[e][:],
-                in0=saved[e // 2][:, :, first : first + C].rearrange("p r u -> p u r"),
-                scalar=0.0,
-                in1=turned[e][:].rearrange("p r u -> p u r"),
-                op0=ALU.is_gt,
-                op1=ALU.mult,
+            values = turned[e][:].rearrange("p h u -> p (h u)").bitcast(BF16).rearrange("p (h u j) -> p u h j", h=2, j=2)
+            nc.vector.tensor_tensor(
+                dh[e][:].rearrange("p u (h j) -> p u h j", j=2),
+                values,
+                positive[e][:].rearrange("p u (h j) -> p u h j", j=2),
+                ALU.mult,
             )
 
         def quantise_dh(e):
@@ -215,8 +216,8 @@ def tile_moe_adb_relu_kernel(tc, dy_words, dy_scales, wt, wbt, wat, a, gate, off
                 bank, tokens = pieces[kt, n]
                 nc.tensor.matmul_mx(
                     out=bank,
-                    lhsT=codes["w", 0, kt // 2][:, cols].bitcast(FP8X4),
-                    lhsT_scale=planes["w", 0, kt // 2][:, cols],
+                    lhsT=codes["wb", E, kt // 2][:, cols].bitcast(FP8X4),
+                    lhsT_scale=planes["wb", E, kt // 2][:, cols],
                     rhs=words[:, tokens].bitcast(FP8X4),
                     rhs_scale=scales[:, tokens],
                     start=True,
@@ -228,105 +229,175 @@ def tile_moe_adb_relu_kernel(tc, dy_words, dy_scales, wt, wbt, wat, a, gate, off
             parked[kt, n] = staged([P, tokens.stop - tokens.start], F32, "parked")
             nc.scalar.copy(parked[kt, n][:], bank)
 
-        def finish(kt, n):
-            bank, tokens = pieces[kt, n]
-            result = staged([P, tokens.stop - tokens.start], F32, "result")
-            if (kt, n) in parked:
-                nc.gpsimd.tensor_tensor(result[:], parked[kt, n][:], windows[kt][:, tokens], ALU.add)
-                nc.scalar.dma_start(out[kt * P : (kt + 1) * P, tokens], result[:])
-            else:
-                nc.vector.tensor_tensor(result[:], bank, windows[kt][:, tokens], ALU.add)
-                nc.sync.dma_start(out[kt * P : (kt + 1) * P, tokens], result[:])
+        results = {}
 
-        gather(0)
-        round_half(("wb", 0, 0), "vector")
-        round_half(("wb", 0, 1), "scalar")
+        def add(kt, n):
+            bank, tokens = pieces[kt, n]
+            results[kt, n] = staged([P, tokens.stop - tokens.start], F32, "result")
+            if (kt, n) in parked:
+                nc.gpsimd.tensor_tensor(results[kt, n][:], parked[kt, n][:], windows[kt][:, tokens], ALU.add)
+            else:
+                nc.vector.tensor_tensor(results[kt, n][:], bank, windows[kt][:, tokens], ALU.add)
+
+        def store(kt, n):
+            queue = nc.sync if (kt, n) in parked else nc.scalar
+            queue.dma_start(out[kt * P : (kt + 1) * P, pieces[kt, n][1]], results[kt, n][:])
+
+        def gate_columns():
+            make_identity(nc, identity[:])
+            turned_gate = psum.tile([P, P], F32, name="turned_gate", tag="turned")
+            nc.tensor.transpose(turned_gate[:], gate_rows[:], identity[:])
+            nc.scalar.activation(gate_cols[:], turned_gate[:, 0:E], COPY)
+
+        def load_small():
+            nc.gpsimd.memset(scales[:].bitcast(I32), 0)
+            nc.sync.dma_start(words[:], dy_words[0].rearrange("p t r -> p (t r)").bitcast(I32))
+            nc.sync.dma_start(offsets[:], offs)
+            for quad in range(4):
+                nc.sync.dma_start(
+                    scales[32 * quad : 32 * quad + 4, :].bitcast(I32),
+                    dy_scales[0, 4 * quad : 4 * quad + 4, :].bitcast(I32),
+                )
+            nc.sync.dma_start(gate_rows[:], gate.rearrange("q (e u) -> (q e) u", u=C)[0:P, :])
+
+        load_small()
+        load_half(("wb", 0, 0), wbt[0])
+        load_half(("wb", 0, 1), wbt[0])
+        load_half(("wa", 0, 0), wat[0])
+        load_saved(0, 2)
+        load_half(("wa", 0, 1), wat[0])
+        load_weight(("wb", 1), wbt[1])
+        load_weight(("wb", 2), wbt[2])
+        load_weight(("wa", 1), wat[1])
+        load_saved(2, 2)
+        load_weight(("wb", 3), wbt[3])
+        load_weight(("wa", 2), wat[2])
+        load_weight(("wb", 4), wbt[4])
+        load_weight(("wa", 3), wat[3])
+        load_saved(4, 1)
+        load_weight(("wb", 5), wbt[5])
+        load_weight(("wa", 4), wat[4])
+        load_saved(5, 1)
+        load_weight(("wa", 5), wat[5])
+        load_weight(("wb", E), wt)
+        gate_columns()
+
+        gather(0, "words0", "scales0")
+        round_half(("wb", 0, 0), "scalar", handed="scales2")
+        gather(1, "words1", "scales1")
+        round_half(("wb", 0, 1), "vector", handed="words2")
         quantise_half(("wb", 0, 0))
         quantise_half(("wb", 0, 1))
-        gated_sums(0)
-        gather(1)
-        round_half(("wa", 0, 0), "vector")
-        round_half(("wa", 0, 1), "scalar")
-        quantise_half(("wa", 0, 0))
+        first_product(0)
+        gather(2, "words2", "scales2")
+        gate_and_turn(0)
+        round_half(("wa", 0, 0), "scalar")
+        compare(0, nc.vector)
         mask(0)
-        quantise_half(("wa", 0, 1))
+        compare(1, nc.vector)
         quantise_dh(0)
-        round_half(("wb", 1, 0), "vector")
-        round_half(("wb", 1, 1), "scalar")
+        quantise_half(("wa", 0, 0))
         adapter_product(0, 0)
+        round_half(("wa", 0, 1), "vector")
+        leave_psum(0, 0, 2)
+        quantise_half(("wa", 0, 1))
         adapter_product(0, 1)
+        scatter(0, 0)
+        scatter(0, 1)
+        round_half(("wb", 1, 0), "scalar")
+        round_half(("wb", 1, 1), "vector")
         quantise_half(("wb", 1, 0))
         quantise_half(("wb", 1, 1))
-        gather(2)
-
-        leave_psum(0, 0, 2)
-        leave_psum(0, 2, 2)
-        for kt in range(K_TILES):
-            scatter(0, kt)
+        first_product(1)
+        send_back(0, 2, 2)
         round_half(("wb", 2, 0), "scalar")
-        gated_sums(1)
-        round_half(("wb", 2, 1), "scalar")
-        quantise_half(("wb", 2, 0))
-        mask(1)
-        round_half(("wa", 1, 0), "scalar")
-        quantise_half(("wb", 2, 1))
-        quantise_dh(1)
+        gate_and_turn(1)
         round_half(("wa", 1, 1), "scalar")
+        round_half(("wa", 1, 0), "vector")
+        mask(1)
+        round_half(("wb", 2, 1), "scalar", handed="handed")
         quantise_half(("wa", 1, 0))
+        quantise_dh(1)
         adapter_product(1, 0)
-        round_half(("wb", 3, 0), "vector")
-        gated_sums(2)
+        quantise_half(("wb", 2, 0))
+        compare(2, nc.vector)
         quantise_half(("wa", 1, 1))
         adapter_product(1, 1)
-
-        for e in range(1, E - 2):
-            ahead = e + 3 < E
+        quantise_half(("wb", 2, 1))
+        first_product(2)
+        round_half(("wb", 3, 1), "gpsimd", handed="handed")
+        send_back(1, 0, 2)
+        gate_and_turn(2)
+        send_back(1, 2, 1)
+        round_half(("wb", 3, 0), "scalar")
+        mask(2)
+        send_back(1, 3, 1)
+        round_half(("wa", 2, 0), "scalar")
+        round_half(("wa", 2, 1), "scalar")
+        last = E - 1
+        before = last - 1
+        for e in range(2, last):
+            if e == 3:
+                quantise_half(("wa", e, 0))
+            quantise_dh(e)
+            if e != 3:
+                quantise_half(("wa", e, 0))
+            adapter_product(e, 0)
+            quantise_half(("wb", e + 1, 0))
+            compare(e + 1, nc.vector)
+            quantise_half(("wa", e, 1))
+            adapter_product(e, 1)
+            quantise_half(("wb", e + 1, 1))
+            first_product(e + 1)
+            round_half(("wb", e + 2, 1) if e < before else ("wa", last, 1), "gpsimd", handed="handed")
+            if e > 2:
+                send_back(e - 1, 3, 1)
             send_back(e, 0, 2)
-            round_half(("wb", e + 2, 1), "scalar")
-            round_half(("wa", e + 1, 0), "scalar")
-            quantise_half(("wb", e + 2, 0))
-            quantise_half(("wb", e + 2, 1))
+            round_half(("wb", e + 2, 0) if e < before else ("wa", last, 0), "scalar")
+            if e == 2:
+                gate_and_turn(e + 1)
+                send_back(e, 2, 1)
+                round_half(("wa", e + 1, 0), "scalar")
+                mask(e + 1)
+                round_half(("wa", e + 1, 1), "scalar")
+                continue
+            gate_and_turn(e + 1)
             mask(e + 1)
-            round_half(("wa", e + 1, 1), "scalar", handed=ahead)
-            quantise_half(("wa", e + 1, 0))
-            quantise_dh(e + 1)
-            adapter_product(e + 1, 0)
-            quantise_half(("wa", e + 1, 1))
-            adapter_product(e + 1, 1)
-            if ahead:
-                round_half(("wb", e + 3, 0), "gpsimd", handed=True)
-            send_back(e, 2, 2)
-            gated_sums(e + 2)
-
-        before, last = E - 2, E - 1
-        round_half(("wa", last, 0), "scalar")
-        send_back(before, 0, 1)
-        round_half(("wa", last, 1), "scalar")
-        round_half(("w", 0, 0), "scalar")
-        mask(last)
+            if e < before:
+                send_back(e, 2, 1)
+                round_half(("wa", e + 1, 0), "scalar")
+                round_half(("wa", e + 1, 1), "scalar")
+        round_half(("wb", E, 0), "scalar")
         quantise_half(("wa", last, 0))
         quantise_dh(last)
         adapter_product(last, 0)
         quantise_half(("wa", last, 1))
         adapter_product(last, 1)
-        quantise_half(("w", 0, 0))
+        send_back(before, 2, 1)
+        leave_psum(last, 0, 2)
+        quantise_half(("wb", E, 0))
         frozen_product(0)
         frozen_product(1)
-        send_back(before, 1, 1)
-        round_half(("w", 0, 1), "scalar")
-        quantise_half(("w", 0, 1))
+        scatter(last, 0)
+        scatter(last, 1)
+        round_half(("wb", E, 1), "scalar")
+        park(0, 0)
+        quantise_half(("wb", E, 1))
         frozen_product(2)
         frozen_product(3)
-        send_back(last, 0, 2)
-        park(0, 0)
-        park(1, 0)
-        send_back(before, 2, 2)
+        send_back(last, 2, 1)
         park(0, 1)
+        park(1, 0)
+        send_back(before, 3, 1)
         park(1, 1)
-        send_back(last, 2, 2)
-        for n in range(2):
-            finish(0, n)
-            finish(1, n)
-        for kt in (2, 3):
-            finish(kt, 0)
-            finish(kt, 1)
+        for kt in range(2):
+            add(kt, 0)
+            add(kt, 1)
+        add(2, 0)
+        send_back(last, 3, 1)
+        add(2, 1)
+        add(3, 0)
+        add(3, 1)
+        for kt in (0, 2, 1, 3):
+            store(kt, 0)
+            store(kt, 1)

@@ -27,8 +27,8 @@ K_TILES = K // P
 PAIR = 2 * C
 STAGED_BUFS = 32
 MATRICES = 2 * E + 1
-WHOLE_BUFS = 11
-HALF_BUFS = 4
+WHOLE_BUFS = 13
+HALF_BUFS = 1
 
 
 def tile_moe_adb_relu_kernel(tc, dy_words, dy_scales, wt, wbt, wat, a, gate, offs, out):
@@ -142,10 +142,10 @@ def tile_moe_adb_relu_kernel(tc, dy_words, dy_scales, wt, wbt, wat, a, gate, off
             for h in range(2):
                 nc.tensor.transpose(turned[e][:, h, :], pairs[:, h * P : (h + 1) * P], identity[:])
 
-        def compare(e, engine, handed=None):
-            positive[e] = staged([P, C, PACK], BF16, "positive", handed)
+        def compare(e):
+            positive[e] = ring.tile([P, C, PACK], BF16, name="positive", tag="positive", bufs=E, align_bytes=64)
             written, read = lines(positive[e][:], saved[e])
-            engine.tensor_scalar(written, read, 0.0, 1.0, ALU.is_gt, ALU.mult)
+            nc.vector.tensor_scalar(written, read, 0.0, 1.0, ALU.is_gt, ALU.mult)
 
         def mask(e):
             dh[e] = staged([P, C, PACK], BF16, "dh")
@@ -261,143 +261,91 @@ def tile_moe_adb_relu_kernel(tc, dy_words, dy_scales, wt, wbt, wat, a, gate, off
             nc.sync.dma_start(gate_rows[:], gate.rearrange("q (e u) -> (q e) u", u=C)[0:P, :])
 
         load_small()
-        load_half(("wb", 0, 0), wbt[0])
-        load_half(("wb", 0, 1), wbt[0])
-        load_half(("wa", 0, 0), wat[0])
-        load_saved(0, 2)
-        load_half(("wa", 0, 1), wat[0])
-        load_weight(("wb", 1), wbt[1])
-        load_weight(("wb", 2), wbt[2])
-        load_weight(("wa", 1), wat[1])
-        load_saved(2, 2)
-        load_weight(("wb", 3), wbt[3])
-        load_weight(("wa", 2), wat[2])
-        load_weight(("wb", 4), wbt[4])
-        load_weight(("wa", 3), wat[3])
-        load_saved(4, 1)
-        load_weight(("wb", 5), wbt[5])
-        load_weight(("wa", 4), wat[4])
-        load_saved(5, 1)
-        load_weight(("wa", 5), wat[5])
-        load_weight(("wb", E), wt)
+        load_weight(("wb", 0), wbt[0])
+        load_saved(0, E)
+        for e in range(E):
+            load_weight(("wa", e), wat[e])
+            load_weight(("wb", e + 1), wbt[e + 1] if e + 1 < E else wt)
         gate_columns()
 
         gather(0, "words0", "scales0")
-        round_half(("wb", 0, 0), "scalar", handed="scales2")
         gather(1, "words1", "scales1")
+        round_half(("wb", 0, 0), "scalar", handed="scales2")
         round_half(("wb", 0, 1), "vector", handed="words2")
-        quantise_half(("wb", 0, 0))
         quantise_half(("wb", 0, 1))
+        quantise_half(("wb", 0, 0))
         first_product(0)
         gather(2, "words2", "scales2")
         gate_and_turn(0)
-        round_half(("wa", 0, 0), "scalar")
-        compare(0, nc.vector)
+        compare(0)
+        compare(1)
         mask(0)
-        compare(1, nc.vector)
+        compare(2)
         quantise_dh(0)
+        compare(3)
+        round_half(("wa", 0, 1), "scalar")
+        round_half(("wa", 0, 0), "vector")
+        compare(4)
         quantise_half(("wa", 0, 0))
         adapter_product(0, 0)
-        round_half(("wa", 0, 1), "vector")
-        leave_psum(0, 0, 2)
+        compare(5)
         quantise_half(("wa", 0, 1))
         adapter_product(0, 1)
-        scatter(0, 0)
-        scatter(0, 1)
-        round_half(("wb", 1, 0), "scalar")
         round_half(("wb", 1, 1), "vector")
-        quantise_half(("wb", 1, 0))
+        send_back(0, 0, 1)
+        round_half(("wb", 1, 0), "scalar", handed="handed0")
         quantise_half(("wb", 1, 1))
+        quantise_half(("wb", 1, 0))
         first_product(1)
+        round_half(("wa", 1, 1), "gpsimd", handed="handed0")
+        send_back(0, 1, 1)
         send_back(0, 2, 2)
-        round_half(("wb", 2, 0), "scalar")
         gate_and_turn(1)
-        round_half(("wa", 1, 1), "scalar")
-        round_half(("wa", 1, 0), "vector")
+        round_half(("wa", 1, 0), "scalar")
         mask(1)
-        round_half(("wb", 2, 1), "scalar", handed="handed")
+        round_half(("wb", 2, 0), "scalar")
         quantise_half(("wa", 1, 0))
         quantise_dh(1)
         adapter_product(1, 0)
-        quantise_half(("wb", 2, 0))
-        compare(2, nc.vector)
         quantise_half(("wa", 1, 1))
         adapter_product(1, 1)
-        quantise_half(("wb", 2, 1))
-        first_product(2)
-        round_half(("wb", 3, 1), "gpsimd", handed="handed")
-        send_back(1, 0, 2)
-        gate_and_turn(2)
-        send_back(1, 2, 1)
-        round_half(("wb", 3, 0), "scalar")
-        mask(2)
-        send_back(1, 3, 1)
-        round_half(("wa", 2, 0), "scalar")
-        round_half(("wa", 2, 1), "scalar")
+        round_half(("wb", 2, 1), "vector", handed="handed1")
         last = E - 1
         before = last - 1
-        for e in range(2, last):
-            if e == 3:
-                quantise_half(("wa", e, 0))
-            quantise_dh(e)
-            if e != 3:
-                quantise_half(("wa", e, 0))
-            adapter_product(e, 0)
+        for e in range(1, last):
             quantise_half(("wb", e + 1, 0))
-            compare(e + 1, nc.vector)
-            quantise_half(("wa", e, 1))
-            adapter_product(e, 1)
             quantise_half(("wb", e + 1, 1))
             first_product(e + 1)
-            round_half(("wb", e + 2, 1) if e < before else ("wa", last, 1), "gpsimd", handed="handed")
-            if e > 2:
-                send_back(e - 1, 3, 1)
+            round_half(("wa", e + 1, 1), "gpsimd", handed=f"handed{e % 2}")
             send_back(e, 0, 2)
-            round_half(("wb", e + 2, 0) if e < before else ("wa", last, 0), "scalar")
-            if e == 2:
-                gate_and_turn(e + 1)
-                send_back(e, 2, 1)
-                round_half(("wa", e + 1, 0), "scalar")
-                mask(e + 1)
-                round_half(("wa", e + 1, 1), "scalar")
-                continue
+            send_back(e, 2, 1)
+            round_half(("wa", e + 1, 0), "scalar")
             gate_and_turn(e + 1)
             mask(e + 1)
+            round_half(("wb", e + 2, 0), "scalar")
+            quantise_half(("wa", e + 1, 0))
+            quantise_dh(e + 1)
+            adapter_product(e + 1, 0)
+            quantise_half(("wa", e + 1, 1))
+            adapter_product(e + 1, 1)
             if e < before:
-                send_back(e, 2, 1)
-                round_half(("wa", e + 1, 0), "scalar")
-                round_half(("wa", e + 1, 1), "scalar")
-        round_half(("wb", E, 0), "scalar")
-        quantise_half(("wa", last, 0))
-        quantise_dh(last)
-        adapter_product(last, 0)
-        quantise_half(("wa", last, 1))
-        adapter_product(last, 1)
-        send_back(before, 2, 1)
-        leave_psum(last, 0, 2)
+                send_back(e, 3, 1)
+                round_half(("wb", e + 2, 1), "scalar", handed=f"handed{(e + 1) % 2}")
         quantise_half(("wb", E, 0))
         frozen_product(0)
         frozen_product(1)
-        scatter(last, 0)
-        scatter(last, 1)
+        send_back(before, 3, 1)
         round_half(("wb", E, 1), "scalar")
-        park(0, 0)
         quantise_half(("wb", E, 1))
+        send_back(last, 0, 2)
+        park(0, 0)
         frozen_product(2)
         frozen_product(3)
-        send_back(last, 2, 1)
+        send_back(last, 2, 2)
         park(0, 1)
         park(1, 0)
-        send_back(before, 3, 1)
-        park(1, 1)
-        for kt in range(2):
+        for kt in range(K_TILES):
             add(kt, 0)
             add(kt, 1)
-        add(2, 0)
-        send_back(last, 3, 1)
-        add(2, 1)
-        add(3, 0)
-        add(3, 1)
-        for kt in (0, 2, 1, 3):
-            store(kt, 0)
-            store(kt, 1)
+        for kt, n in ((0, 0), (0, 1), (1, 1), (1, 0), (2, 0), (2, 1), (3, 0), (3, 1)):
+            store(kt, n)

@@ -104,12 +104,28 @@ def tile_moe_adb_relu_kernel(tc, dy_words, dy_scales, wt, wbt, wat, a, gate, off
         slot_words = {}
         slot_scales = {}
 
-        def gather(pair, words_tag, scales_tag):
-            entries = offsets[:, pair * PAIR // PER_COLUMN : (pair + 1) * PAIR // PER_COLUMN]
-            slot_words[pair] = staged([P, PAIR], U32, "slot_words", words_tag)
-            nc.vector.tensor_copy(slot_words[pair][:], words[:].bitcast(U32).indirect(entries))
-            slot_scales[pair] = staged([P, PAIR], U8, "slot_scales", scales_tag)
-            nc.vector.tensor_copy(slot_scales[pair][:], scales[:].indirect(entries))
+        def pair_entries(pair):
+            return offsets[:, pair * PAIR // PER_COLUMN : (pair + 1) * PAIR // PER_COLUMN]
+
+        def gather_words(pair, handed):
+            slot_words[pair] = staged([P, PAIR], U32, "slot_words", handed)
+            nc.vector.tensor_copy(slot_words[pair][:], words[:].bitcast(U32).indirect(pair_entries(pair)))
+
+        def gather_scales(pair, handed):
+            slot_scales[pair] = staged([P, PAIR], U8, "slot_scales", handed)
+            nc.vector.tensor_copy(slot_scales[pair][:], scales[:].indirect(pair_entries(pair)))
+
+        def gather_both_scales():
+            later = staged([P, 2 * PAIR], U8, "later_scales", "scales12")
+            nc.vector.tensor_copy(later[:], scales[:].indirect(offsets[:, PAIR // PER_COLUMN :]))
+            slot_scales[1] = later[:, 0:PAIR]
+            slot_scales[2] = later[:, PAIR : 2 * PAIR]
+
+        def gather_both_words():
+            later = staged([P, 2 * PAIR], U32, "later_words", "words12")
+            nc.vector.tensor_copy(later[:], words[:].bitcast(U32).indirect(offsets[:, PAIR // PER_COLUMN :]))
+            slot_words[1] = later[:, 0:PAIR]
+            slot_words[2] = later[:, PAIR : 2 * PAIR]
 
         sums = {}
         turned = {}
@@ -143,7 +159,7 @@ def tile_moe_adb_relu_kernel(tc, dy_words, dy_scales, wt, wbt, wat, a, gate, off
                 nc.tensor.transpose(turned[e][:, h, :], pairs[:, h * P : (h + 1) * P], identity[:])
 
         def compare(e):
-            positive[e] = ring.tile([P, C, PACK], BF16, name="positive", tag="positive", bufs=E, align_bytes=64)
+            positive[e] = staged([P, C, PACK], BF16, "positive")
             written, read = lines(positive[e][:], saved[e])
             nc.vector.tensor_scalar(written, read, 0.0, 1.0, ALU.is_gt, ALU.mult)
 
@@ -198,6 +214,17 @@ def tile_moe_adb_relu_kernel(tc, dy_words, dy_scales, wt, wbt, wat, a, gate, off
             for kt in range(first, first + count):
                 scatter(e, kt)
 
+        both = {}
+
+        def leave_for_both(e, kt):
+            if kt not in both:
+                both[kt] = staged([P, 2, C], F32, "both")
+            nc.scalar.copy(both[kt][:, e % 2, :], product[e, kt // 2][:, kt % 2, :])
+
+        def scatter_both(kt):
+            entries = offsets[:, (E - 2) * C // PER_COLUMN : E * C // PER_COLUMN]
+            nc.vector.tensor_copy(windows[kt][:].indirect(entries), both[kt][:].rearrange("p n u -> p (n u)"))
+
         pieces = {}
         tails = {}
         parked = {}
@@ -206,7 +233,7 @@ def tile_moe_adb_relu_kernel(tc, dy_words, dy_scales, wt, wbt, wat, a, gate, off
             cols = slice(kt % 2 * P, (kt % 2 + 1) * P)
             if kt % 2 == 0:
                 tails[kt // 2] = psum.tile([P, 2, T - BANK], F32, name="tail", tag="sums")
-            if kt < K_TILES - 1:
+            if kt != 2:
                 head = psum.tile([P, BANK], F32, name="head", tag="turned")
             else:
                 head = psum.tile([P, BANK], F32, name="head", tag="base", bufs=1)
@@ -251,6 +278,7 @@ def tile_moe_adb_relu_kernel(tc, dy_words, dy_scales, wt, wbt, wat, a, gate, off
 
         def load_small():
             nc.gpsimd.memset(scales[:].bitcast(I32), 0)
+            nc.sync.dma_start(gate_rows[:], gate.rearrange("q (e u) -> (q e) u", u=C)[0:P, :])
             nc.sync.dma_start(words[:], dy_words[0].rearrange("p t r -> p (t r)").bitcast(I32))
             nc.sync.dma_start(offsets[:], offs)
             for quad in range(4):
@@ -258,71 +286,77 @@ def tile_moe_adb_relu_kernel(tc, dy_words, dy_scales, wt, wbt, wat, a, gate, off
                     scales[32 * quad : 32 * quad + 4, :].bitcast(I32),
                     dy_scales[0, 4 * quad : 4 * quad + 4, :].bitcast(I32),
                 )
-            nc.sync.dma_start(gate_rows[:], gate.rearrange("q (e u) -> (q e) u", u=C)[0:P, :])
 
         load_small()
         load_weight(("wb", 0), wbt[0])
-        load_saved(0, E)
+        load_saved(0, 2)
         for e in range(E):
             load_weight(("wa", e), wat[e])
             load_weight(("wb", e + 1), wbt[e + 1] if e + 1 < E else wt)
+            if e in (1, 3):
+                load_saved(e + 1, 2)
         gate_columns()
 
-        gather(0, "words0", "scales0")
-        gather(1, "words1", "scales1")
-        round_half(("wb", 0, 0), "scalar", handed="scales2")
-        round_half(("wb", 0, 1), "vector", handed="words2")
-        quantise_half(("wb", 0, 1))
+        gather_words(0, "words0")
+        gather_scales(0, "scales0")
+        gather_both_words()
+        round_half(("wb", 0, 1), "scalar", handed="scales12")
+        round_half(("wb", 0, 0), "vector")
         quantise_half(("wb", 0, 0))
+        quantise_half(("wb", 0, 1))
         first_product(0)
-        gather(2, "words2", "scales2")
-        gate_and_turn(0)
+        gather_both_scales()
         compare(0)
-        compare(1)
-        mask(0)
-        compare(2)
-        quantise_dh(0)
-        compare(3)
+        gate_and_turn(0)
         round_half(("wa", 0, 1), "scalar")
         round_half(("wa", 0, 0), "vector")
-        compare(4)
+        compare(1)
+        mask(0)
         quantise_half(("wa", 0, 0))
+        quantise_dh(0)
         adapter_product(0, 0)
-        compare(5)
         quantise_half(("wa", 0, 1))
         adapter_product(0, 1)
-        round_half(("wb", 1, 1), "vector")
-        send_back(0, 0, 1)
         round_half(("wb", 1, 0), "scalar", handed="handed0")
+        round_half(("wb", 1, 1), "vector")
+        leave_psum(0, 0, 2)
         quantise_half(("wb", 1, 1))
         quantise_half(("wb", 1, 0))
         first_product(1)
         round_half(("wa", 1, 1), "gpsimd", handed="handed0")
-        send_back(0, 1, 1)
+        scatter(0, 0)
+        scatter(0, 1)
         send_back(0, 2, 2)
         gate_and_turn(1)
         round_half(("wa", 1, 0), "scalar")
         mask(1)
         round_half(("wb", 2, 0), "scalar")
+        round_half(("wb", 2, 1), "scalar", handed="handed1")
         quantise_half(("wa", 1, 0))
         quantise_dh(1)
         adapter_product(1, 0)
         quantise_half(("wa", 1, 1))
         adapter_product(1, 1)
-        round_half(("wb", 2, 1), "vector", handed="handed1")
+        compare(2)
         last = E - 1
         before = last - 1
         for e in range(1, last):
             quantise_half(("wb", e + 1, 0))
             quantise_half(("wb", e + 1, 1))
             first_product(e + 1)
+            if e > 1:
+                compare(e + 1)
             round_half(("wa", e + 1, 1), "gpsimd", handed=f"handed{e % 2}")
             send_back(e, 0, 2)
             send_back(e, 2, 1)
-            round_half(("wa", e + 1, 0), "scalar")
+            if e > 1:
+                round_half(("wa", e + 1, 0), "scalar")
             gate_and_turn(e + 1)
+            if e == 1:
+                round_half(("wa", e + 1, 0), "scalar")
             mask(e + 1)
-            round_half(("wb", e + 2, 0), "scalar")
+            if e == before:
+                round_half(("wb", E, 0), "scalar")
             quantise_half(("wa", e + 1, 0))
             quantise_dh(e + 1)
             adapter_product(e + 1, 0)
@@ -330,6 +364,7 @@ def tile_moe_adb_relu_kernel(tc, dy_words, dy_scales, wt, wbt, wat, a, gate, off
             adapter_product(e + 1, 1)
             if e < before:
                 send_back(e, 3, 1)
+                round_half(("wb", e + 2, 0), "scalar")
                 round_half(("wb", e + 2, 1), "scalar", handed=f"handed{(e + 1) % 2}")
         quantise_half(("wb", E, 0))
         frozen_product(0)
@@ -341,11 +376,18 @@ def tile_moe_adb_relu_kernel(tc, dy_words, dy_scales, wt, wbt, wat, a, gate, off
         park(0, 0)
         frozen_product(2)
         frozen_product(3)
-        send_back(last, 2, 2)
+        send_back(last, 2, 1)
         park(0, 1)
-        park(1, 0)
-        for kt in range(K_TILES):
+        park(2, 0)
+        add(0, 0)
+        add(1, 0)
+        send_back(last, 3, 1)
+        park(2, 1)
+        add(0, 1)
+        add(1, 1)
+        for kt in (2, 3):
             add(kt, 0)
             add(kt, 1)
-        for kt, n in ((0, 0), (0, 1), (1, 1), (1, 0), (2, 0), (2, 1), (3, 0), (3, 1)):
-            store(kt, n)
+        for kt in range(K_TILES):
+            store(kt, 0)
+            store(kt, 1)

@@ -21,14 +21,16 @@ PACK = 4
 WIDTH = 512
 HALF = WIDTH // 2
 LINE = 4
+QUADRANT = 32
+SCALE_ROWS = 4
 PER_COLUMN = 16
 BANK = 512
 K_TILES = K // P
-PAIR = 2 * C
+PAIR = 2
 STAGED_BUFS = 32
 MATRICES = 2 * E + 1
-WHOLE_BUFS = 13
-HALF_BUFS = 1
+LAST = E - 1
+FROZEN = E
 
 
 def tile_moe_adb_relu_kernel(tc, dy_words, dy_scales, wt, wbt, wat, a, gate, offs, out):
@@ -54,43 +56,77 @@ def tile_moe_adb_relu_kernel(tc, dy_words, dy_scales, wt, wbt, wat, a, gate, off
         raw = {}
         saved = {}
 
-        def load_weight(name, matrix):
-            whole = ring.tile([P, PACK, WIDTH], F32, name="raw", tag="raw", bufs=WHOLE_BUFS)
-            nc.sync.dma_start(whole[:], matrix.rearrange("(p r) c -> p r c", r=PACK))
+        def load_whole(matrix, source):
+            whole = ring.tile([P, PACK, WIDTH], F32, name="whole", tag="whole", bufs=MATRICES - 1)
+            nc.sync.dma_start(whole[:], source.rearrange("(p r) c -> p r c", r=PACK))
             for side in range(2):
-                raw[name + (side,)] = whole[:, :, side * HALF : (side + 1) * HALF]
+                raw[matrix + (side,)] = whole[:, :, side * HALF : (side + 1) * HALF]
 
-        def load_half(half, matrix):
-            part = ring.tile([P, PACK, HALF], F32, name="raw_half", tag="raw_half", bufs=HALF_BUFS)
+        def load_half(half, source):
+            part = ring.tile([P, PACK, HALF], F32, name="part", tag="part", bufs=2)
             cols = slice(half[2] * HALF, (half[2] + 1) * HALF)
-            nc.sync.dma_start(part[:], matrix[:, cols].rearrange("(p r) c -> p r c", r=PACK))
+            nc.sync.dma_start(part[:], source[:, cols].rearrange("(p r) c -> p r c", r=PACK))
             raw[half] = part[:]
 
-        def load_saved(first, count):
-            part = keep.tile([P, PACK, count * C], F32, name=f"saved{first}")
-            nc.sync.dma_start(part[:], a[:, first * C : (first + count) * C].rearrange("(p r) s -> p r s", r=PACK))
-            for n in range(count):
-                saved[first + n] = part[:, :, n * C : (n + 1) * C]
+        def load_saved(first):
+            both = keep.tile([P, PACK, PAIR * C], F32, name=f"saved{first}")
+            nc.sync.dma_start(both[:], a[:, first * C : (first + PAIR) * C].rearrange("(p r) s -> p r s", r=PACK))
+            for place in range(PAIR):
+                saved[first + place] = both[:, :, place * C : (place + 1) * C]
 
-        rounded = {}
-        codes = {}
-        planes = {}
+        nc.gpsimd.memset(scales[:].bitcast(I32), 0)
+        nc.gpsimd.memset(gate_rows[:], 0.0)
+        nc.sync.dma_start(words[:], dy_words[0].rearrange("p t r -> p (t r)").bitcast(I32))
+        nc.sync.dma_start(offsets[:], offs)
+        for row in range(SCALE_ROWS):
+            nc.sync.dma_start(scales[row:P:QUADRANT, :].bitcast(I32), dy_scales[0, row::SCALE_ROWS, :].bitcast(I32))
+        load_whole(("n", 0), wbt[0])
+        nc.sync.dma_start(gate_rows[0:E, :], gate[0].rearrange("(e u) -> e u", u=C))
+        load_saved(0)
+        for e in range(E):
+            load_whole(("i", e), wat[e])
+            if e + 1 == LAST:
+                load_half(("n", LAST, 1), wbt[LAST])
+                load_half(("n", LAST, 0), wbt[LAST])
+            else:
+                load_whole(("n", e + 1), wbt[e + 1] if e < LAST else wt)
+            if (e + 1) % PAIR == 0 and e < LAST:
+                load_saved(e + 1)
 
-        def lines(written, read):
+        make_identity(nc, identity[:])
+        turned_gate = psum.tile([P, P], F32, name="turned_gate", tag="turned")
+        nc.tensor.transpose(turned_gate[:], gate_rows[:], identity[:])
+        nc.scalar.activation(gate_cols[:], turned_gate[:, 0:E], COPY)
+
+        slot_words = {}
+        slot_scales = {}
+
+        def entries(first, count):
+            return offsets[:, first * C // PER_COLUMN : (first + count) * C // PER_COLUMN]
+
+        def gather(table, dtype, gathered, first, count, tag):
+            part = staged([P, count * C], dtype, "gathered", tag)
+            nc.vector.tensor_copy(part[:], table.indirect(entries(first, count)))
+            for place in range(count):
+                gathered[first + place] = part[:, place * C : (place + 1) * C]
+
+        def by_lines(written, read):
             return (
                 written.rearrange("p (c i) r -> p c r i", i=LINE),
                 read.rearrange("p r (c i) -> p c r i", i=LINE),
             )
 
+        rounded = {}
+        codes = {}
+        planes = {}
+
         def round_half(half, engine, handed=None):
             rounded[half] = staged([P, HALF, PACK], BF16, "rounded", handed)
-            written, read = lines(rounded[half][:], raw[half])
             if engine == "gpsimd":
                 nc.gpsimd.tensor_copy(rounded[half][:], raw[half].rearrange("p r c -> p c r"))
-            elif engine == "scalar":
-                nc.scalar.copy(written, read)
             else:
-                nc.vector.tensor_copy(written, read)
+                copy = nc.scalar.copy if engine == "scalar" else nc.vector.tensor_copy
+                copy(*by_lines(rounded[half][:], raw[half]))
 
         def quantise_half(half):
             codes[half] = staged([P, HALF], U32, "codes")
@@ -101,32 +137,6 @@ def tile_moe_adb_relu_kernel(tc, dy_words, dy_scales, wt, wbt, wat, a, gate, off
                 in_=rounded[half][:].rearrange("p c r -> p (c r)"),
             )
 
-        slot_words = {}
-        slot_scales = {}
-
-        def pair_entries(pair):
-            return offsets[:, pair * PAIR // PER_COLUMN : (pair + 1) * PAIR // PER_COLUMN]
-
-        def gather_words(pair, handed):
-            slot_words[pair] = staged([P, PAIR], U32, "slot_words", handed)
-            nc.vector.tensor_copy(slot_words[pair][:], words[:].bitcast(U32).indirect(pair_entries(pair)))
-
-        def gather_scales(pair, handed):
-            slot_scales[pair] = staged([P, PAIR], U8, "slot_scales", handed)
-            nc.vector.tensor_copy(slot_scales[pair][:], scales[:].indirect(pair_entries(pair)))
-
-        def gather_both_scales():
-            later = staged([P, 2 * PAIR], U8, "later_scales", "scales12")
-            nc.vector.tensor_copy(later[:], scales[:].indirect(offsets[:, PAIR // PER_COLUMN :]))
-            slot_scales[1] = later[:, 0:PAIR]
-            slot_scales[2] = later[:, PAIR : 2 * PAIR]
-
-        def gather_both_words():
-            later = staged([P, 2 * PAIR], U32, "later_words", "words12")
-            nc.vector.tensor_copy(later[:], words[:].bitcast(U32).indirect(offsets[:, PAIR // PER_COLUMN :]))
-            slot_words[1] = later[:, 0:PAIR]
-            slot_words[2] = later[:, PAIR : 2 * PAIR]
-
         sums = {}
         turned = {}
         positive = {}
@@ -135,15 +145,14 @@ def tile_moe_adb_relu_kernel(tc, dy_words, dy_scales, wt, wbt, wat, a, gate, off
         dh_planes = {}
 
         def first_product(e):
-            slots = slice(e % 2 * C, (e % 2 + 1) * C)
             sums[e] = psum.tile([P, H], F32, name="sums", tag="sums")
             for side in range(2):
                 nc.tensor.matmul_mx(
                     out=sums[e][:, side * HALF : (side + 1) * HALF],
-                    lhsT=slot_words[e // 2][:, slots].bitcast(FP8X4),
-                    lhsT_scale=slot_scales[e // 2][:, slots],
-                    rhs=codes["wb", e, side][:].bitcast(FP8X4),
-                    rhs_scale=planes["wb", e, side][:],
+                    lhsT=slot_words[e].bitcast(FP8X4),
+                    lhsT_scale=slot_scales[e],
+                    rhs=codes["n", e, side][:].bitcast(FP8X4),
+                    rhs_scale=planes["n", e, side][:],
                     start=True,
                     stop=True,
                 )
@@ -160,15 +169,15 @@ def tile_moe_adb_relu_kernel(tc, dy_words, dy_scales, wt, wbt, wat, a, gate, off
 
         def compare(e):
             positive[e] = staged([P, C, PACK], BF16, "positive")
-            written, read = lines(positive[e][:], saved[e])
+            written, read = by_lines(positive[e][:], saved[e])
             nc.vector.tensor_scalar(written, read, 0.0, 1.0, ALU.is_gt, ALU.mult)
 
         def mask(e):
             dh[e] = staged([P, C, PACK], BF16, "dh")
-            values = turned[e][:].rearrange("p h u -> p (h u)").bitcast(BF16).rearrange("p (h u j) -> p u h j", h=2, j=2)
+            values = turned[e][:].rearrange("p h u -> p (h u)").bitcast(BF16)
             nc.vector.tensor_tensor(
                 dh[e][:].rearrange("p u (h j) -> p u h j", j=2),
-                values,
+                values.rearrange("p (h u j) -> p u h j", h=2, j=2),
                 positive[e][:].rearrange("p u (h j) -> p u h j", j=2),
                 ALU.mult,
             )
@@ -183,211 +192,169 @@ def tile_moe_adb_relu_kernel(tc, dy_words, dy_scales, wt, wbt, wat, a, gate, off
             )
 
         product = {}
-        dx = {}
 
-        def adapter_product(e, side):
+        def second_product(e, side):
             product[e, side] = psum.tile([P, 2, C], F32, name="product", tag="product", bufs=3)
             for place in range(2):
                 cols = slice(place * P, (place + 1) * P)
                 nc.tensor.matmul_mx(
                     out=product[e, side][:, place, :],
-                    lhsT=codes["wa", e, side][:, cols].bitcast(FP8X4),
-                    lhsT_scale=planes["wa", e, side][:, cols],
+                    lhsT=codes["i", e, side][:, cols].bitcast(FP8X4),
+                    lhsT_scale=planes["i", e, side][:, cols],
                     rhs=dh_codes[e][:].bitcast(FP8X4),
                     rhs_scale=dh_planes[e][:],
                     start=True,
                     stop=True,
                 )
 
+        def finish_adapter(e):
+            quantise_half(("i", e, 0))
+            quantise_dh(e)
+            second_product(e, 0)
+            quantise_half(("i", e, 1))
+            second_product(e, 1)
+
+        dx = {}
+
         def leave_psum(e, first, count):
             part = staged([P, count, C], F32, "dx")
             nc.scalar.copy(part[:], product[e, first // 2][:, first % 2 : first % 2 + count, :])
-            for n in range(count):
-                dx[e, first + n] = part[:, n, :]
+            for place in range(count):
+                dx[e, first + place] = part[:, place, :]
 
         def scatter(e, kt):
-            entries = offsets[:, e * C // PER_COLUMN : (e + 1) * C // PER_COLUMN]
-            nc.vector.tensor_copy(windows[kt][:].indirect(entries), dx[e, kt])
+            nc.vector.tensor_copy(windows[kt][:].indirect(entries(e, 1)), dx[e, kt])
 
         def send_back(e, first, count):
             leave_psum(e, first, count)
             for kt in range(first, first + count):
                 scatter(e, kt)
 
-        both = {}
-
-        def leave_for_both(e, kt):
-            if kt not in both:
-                both[kt] = staged([P, 2, C], F32, "both")
-            nc.scalar.copy(both[kt][:, e % 2, :], product[e, kt // 2][:, kt % 2, :])
-
-        def scatter_both(kt):
-            entries = offsets[:, (E - 2) * C // PER_COLUMN : E * C // PER_COLUMN]
-            nc.vector.tensor_copy(windows[kt][:].indirect(entries), both[kt][:].rearrange("p n u -> p (n u)"))
-
-        pieces = {}
-        tails = {}
+        tokens = (slice(0, BANK), slice(BANK, T))
+        base = {}
+        short = {}
         parked = {}
+        result = {}
 
         def frozen_product(kt):
             cols = slice(kt % 2 * P, (kt % 2 + 1) * P)
             if kt % 2 == 0:
-                tails[kt // 2] = psum.tile([P, 2, T - BANK], F32, name="tail", tag="sums")
-            if kt != 2:
-                head = psum.tile([P, BANK], F32, name="head", tag="turned")
+                short[kt // 2] = psum.tile([P, 2, T - BANK], F32, name="short", tag="sums")
+            if kt == 2:
+                long = psum.tile([P, BANK], F32, name="long", tag="spare", bufs=1)
             else:
-                head = psum.tile([P, BANK], F32, name="head", tag="base", bufs=1)
-            pieces[kt, 0] = (head[:], slice(0, BANK))
-            pieces[kt, 1] = (tails[kt // 2][:, kt % 2, :], slice(BANK, T))
+                long = psum.tile([P, BANK], F32, name="long", tag="turned")
+            base[kt, 0] = long[:]
+            base[kt, 1] = short[kt // 2][:, kt % 2, :]
             for n in range(2):
-                bank, tokens = pieces[kt, n]
                 nc.tensor.matmul_mx(
-                    out=bank,
-                    lhsT=codes["wb", E, kt // 2][:, cols].bitcast(FP8X4),
-                    lhsT_scale=planes["wb", E, kt // 2][:, cols],
-                    rhs=words[:, tokens].bitcast(FP8X4),
-                    rhs_scale=scales[:, tokens],
+                    out=base[kt, n],
+                    lhsT=codes["n", FROZEN, kt // 2][:, cols].bitcast(FP8X4),
+                    lhsT_scale=planes["n", FROZEN, kt // 2][:, cols],
+                    rhs=words[:, tokens[n]].bitcast(FP8X4),
+                    rhs_scale=scales[:, tokens[n]],
                     start=True,
                     stop=True,
                 )
 
         def park(kt, n):
-            bank, tokens = pieces[kt, n]
-            parked[kt, n] = staged([P, tokens.stop - tokens.start], F32, "parked")
-            nc.scalar.copy(parked[kt, n][:], bank)
-
-        results = {}
+            parked[kt, n] = staged([P, tokens[n].stop - tokens[n].start], F32, "parked")
+            nc.scalar.copy(parked[kt, n][:], base[kt, n])
 
         def add(kt, n):
-            bank, tokens = pieces[kt, n]
-            results[kt, n] = staged([P, tokens.stop - tokens.start], F32, "result")
+            result[kt, n] = staged([P, tokens[n].stop - tokens[n].start], F32, "result")
             if (kt, n) in parked:
-                nc.gpsimd.tensor_tensor(results[kt, n][:], parked[kt, n][:], windows[kt][:, tokens], ALU.add)
+                nc.gpsimd.tensor_tensor(result[kt, n][:], parked[kt, n][:], windows[kt][:, tokens[n]], ALU.add)
             else:
-                nc.vector.tensor_tensor(results[kt, n][:], bank, windows[kt][:, tokens], ALU.add)
+                nc.vector.tensor_tensor(result[kt, n][:], base[kt, n], windows[kt][:, tokens[n]], ALU.add)
 
         def store(kt, n):
             queue = nc.sync if (kt, n) in parked else nc.scalar
-            queue.dma_start(out[kt * P : (kt + 1) * P, pieces[kt, n][1]], results[kt, n][:])
+            queue.dma_start(out[kt * P : (kt + 1) * P, tokens[n]], result[kt, n][:])
 
-        def gate_columns():
-            make_identity(nc, identity[:])
-            turned_gate = psum.tile([P, P], F32, name="turned_gate", tag="turned")
-            nc.tensor.transpose(turned_gate[:], gate_rows[:], identity[:])
-            nc.scalar.activation(gate_cols[:], turned_gate[:, 0:E], COPY)
+        def for_gpsimd(e):
+            return f"for_gpsimd{e % 2}"
 
-        def load_small():
-            nc.gpsimd.memset(scales[:].bitcast(I32), 0)
-            nc.sync.dma_start(gate_rows[:], gate.rearrange("q (e u) -> (q e) u", u=C)[0:P, :])
-            nc.sync.dma_start(words[:], dy_words[0].rearrange("p t r -> p (t r)").bitcast(I32))
-            nc.sync.dma_start(offsets[:], offs)
-            for quad in range(4):
-                nc.sync.dma_start(
-                    scales[32 * quad : 32 * quad + 4, :].bitcast(I32),
-                    dy_scales[0, 4 * quad : 4 * quad + 4, :].bitcast(I32),
-                )
-
-        load_small()
-        load_weight(("wb", 0), wbt[0])
-        load_saved(0, 2)
-        for e in range(E):
-            load_weight(("wa", e), wat[e])
-            load_weight(("wb", e + 1), wbt[e + 1] if e + 1 < E else wt)
-            if e in (1, 3):
-                load_saved(e + 1, 2)
-        gate_columns()
-
-        gather_words(0, "words0")
-        gather_scales(0, "scales0")
-        gather_both_words()
-        round_half(("wb", 0, 1), "scalar", handed="scales12")
-        round_half(("wb", 0, 0), "vector")
-        quantise_half(("wb", 0, 0))
-        quantise_half(("wb", 0, 1))
+        gather(words[:].bitcast(U32), U32, slot_words, 0, PAIR, "first_words")
+        gather(scales[:], U8, slot_scales, 0, PAIR, "first_scales")
+        gather(words[:].bitcast(U32), U32, slot_words, PAIR, E - PAIR, "later_words")
+        round_half(("n", 0, 1), "scalar", handed="later_scales")
+        round_half(("n", 0, 0), "vector")
+        quantise_half(("n", 0, 0))
+        quantise_half(("n", 0, 1))
         first_product(0)
-        gather_both_scales()
+        gather(scales[:], U8, slot_scales, PAIR, E - PAIR, "later_scales")
         compare(0)
         gate_and_turn(0)
-        round_half(("wa", 0, 1), "scalar")
-        round_half(("wa", 0, 0), "vector")
+        round_half(("i", 0, 1), "scalar")
+        round_half(("i", 0, 0), "vector")
         compare(1)
         mask(0)
-        quantise_half(("wa", 0, 0))
-        quantise_dh(0)
-        adapter_product(0, 0)
-        quantise_half(("wa", 0, 1))
-        adapter_product(0, 1)
-        round_half(("wb", 1, 0), "scalar", handed="handed0")
-        round_half(("wb", 1, 1), "vector")
+        finish_adapter(0)
+
+        round_half(("n", 1, 0), "scalar", handed=for_gpsimd(0))
+        round_half(("n", 1, 1), "vector")
         leave_psum(0, 0, 2)
-        quantise_half(("wb", 1, 1))
-        quantise_half(("wb", 1, 0))
+        quantise_half(("n", 1, 1))
+        quantise_half(("n", 1, 0))
         first_product(1)
-        round_half(("wa", 1, 1), "gpsimd", handed="handed0")
+        round_half(("i", 1, 1), "gpsimd", handed=for_gpsimd(0))
         scatter(0, 0)
         scatter(0, 1)
         send_back(0, 2, 2)
         gate_and_turn(1)
-        round_half(("wa", 1, 0), "scalar")
+        round_half(("i", 1, 0), "scalar")
         mask(1)
-        round_half(("wb", 2, 0), "scalar")
-        round_half(("wb", 2, 1), "scalar", handed="handed1")
-        quantise_half(("wa", 1, 0))
-        quantise_dh(1)
-        adapter_product(1, 0)
-        quantise_half(("wa", 1, 1))
-        adapter_product(1, 1)
+        round_half(("n", 2, 0), "scalar")
+        round_half(("n", 2, 1), "scalar", handed=for_gpsimd(1))
+        finish_adapter(1)
         compare(2)
-        last = E - 1
-        before = last - 1
-        for e in range(1, last):
-            quantise_half(("wb", e + 1, 0))
-            quantise_half(("wb", e + 1, 1))
+
+        for e in range(1, LAST):
+            quantise_half(("n", e + 1, 0))
+            quantise_half(("n", e + 1, 1))
             first_product(e + 1)
-            if e > 1:
+            if e + 1 not in positive:
                 compare(e + 1)
-            round_half(("wa", e + 1, 1), "gpsimd", handed=f"handed{e % 2}")
+            round_half(("i", e + 1, 1), "gpsimd", handed=for_gpsimd(e))
             send_back(e, 0, 2)
             send_back(e, 2, 1)
-            if e > 1:
-                round_half(("wa", e + 1, 0), "scalar")
-            gate_and_turn(e + 1)
             if e == 1:
-                round_half(("wa", e + 1, 0), "scalar")
+                gate_and_turn(e + 1)
+                round_half(("i", e + 1, 0), "scalar")
+            else:
+                round_half(("i", e + 1, 0), "scalar")
+                gate_and_turn(e + 1)
             mask(e + 1)
-            if e == before:
-                round_half(("wb", E, 0), "scalar")
-            quantise_half(("wa", e + 1, 0))
-            quantise_dh(e + 1)
-            adapter_product(e + 1, 0)
-            quantise_half(("wa", e + 1, 1))
-            adapter_product(e + 1, 1)
-            if e < before:
+            if e + 1 < LAST:
+                finish_adapter(e + 1)
                 send_back(e, 3, 1)
-                round_half(("wb", e + 2, 0), "scalar")
-                round_half(("wb", e + 2, 1), "scalar", handed=f"handed{(e + 1) % 2}")
-        quantise_half(("wb", E, 0))
+                round_half(("n", e + 2, 0), "scalar")
+                round_half(("n", e + 2, 1), "scalar", handed=for_gpsimd(e + 1))
+
+        round_half(("n", FROZEN, 0), "scalar")
+        finish_adapter(LAST)
+        quantise_half(("n", FROZEN, 0))
         frozen_product(0)
         frozen_product(1)
-        send_back(before, 3, 1)
-        round_half(("wb", E, 1), "scalar")
-        quantise_half(("wb", E, 1))
-        send_back(last, 0, 2)
+        send_back(LAST - 1, 3, 1)
+        round_half(("n", FROZEN, 1), "scalar")
+        quantise_half(("n", FROZEN, 1))
+        send_back(LAST, 0, 2)
         park(0, 0)
         frozen_product(2)
         frozen_product(3)
-        send_back(last, 2, 1)
+        send_back(LAST, 2, 1)
         park(0, 1)
         park(2, 0)
         add(0, 0)
         add(1, 0)
-        send_back(last, 3, 1)
-        park(2, 1)
-        add(0, 1)
         add(1, 1)
-        for kt in (2, 3):
-            add(kt, 0)
-            add(kt, 1)
-        for kt in range(K_TILES):
-            store(kt, 0)
-            store(kt, 1)
+        send_back(LAST, 3, 1)
+        add(0, 1)
+        add(2, 1)
+        add(2, 0)
+        add(3, 0)
+        add(3, 1)
+        for kt, n in result:
+            store(kt, n)

@@ -78,9 +78,9 @@ def tile_moe_adb_relu_kernel(tc, dy_words, dy_scales, wt, wbt, wat, a, gate, off
         nc.gpsimd.memset(gate_rows[:], 0.0)
         nc.sync.dma_start(words[:], dy_words[0].rearrange("p t r -> p (t r)").bitcast(I32))
         nc.sync.dma_start(offsets[:], offs)
+        load_whole(("n", 0), wbt[0])
         for row in range(SCALE_ROWS):
             nc.sync.dma_start(scales[row:P:QUADRANT, :].bitcast(I32), dy_scales[0, row::SCALE_ROWS, :].bitcast(I32))
-        load_whole(("n", 0), wbt[0])
         nc.sync.dma_start(gate_rows[0:E, :], gate[0].rearrange("(e u) -> e u", u=C))
         load_saved(0)
         for e in range(E):
@@ -276,10 +276,10 @@ def tile_moe_adb_relu_kernel(tc, dy_words, dy_scales, wt, wbt, wat, a, gate, off
             return f"for_gpsimd{e % 2}"
 
         gather(words[:].bitcast(U32), U32, slot_words, 0, PAIR, "first_words")
-        gather(scales[:], U8, slot_scales, 0, PAIR, "first_scales")
         gather(words[:].bitcast(U32), U32, slot_words, PAIR, E - PAIR, "later_words")
         round_half(("n", 0, 1), "scalar", handed="later_scales")
         round_half(("n", 0, 0), "vector")
+        gather(scales[:], U8, slot_scales, 0, PAIR, None)
         quantise_half(("n", 0, 0))
         quantise_half(("n", 0, 1))
         first_product(0)

@@ -21,6 +21,7 @@ PACK = 4
 WIDTH = 512
 HALF = WIDTH // 2
 LINE = 4
+AXI = 256
 QUADRANT = 32
 SCALE_ROWS = 4
 PER_COLUMN = 16
@@ -41,8 +42,8 @@ def tile_moe_adb_relu_kernel(tc, dy_words, dy_scales, wt, wbt, wat, a, gate, off
         psum = ctx.enter_context(tc.psum_pool(name="psum", bufs=2))
 
         offsets = keep.tile([P, T // PER_COLUMN], U16, name="offsets")
-        words = keep.tile([P, T], I32, name="words", align_bytes=64)
-        scales = keep.tile([P, T], U8, name="scales", align_bytes=64)
+        words = keep.tile([P, T], I32, name="words", align_bytes=AXI)
+        scales = keep.tile([P, T], U8, name="scales", align_bytes=AXI)
         gate_rows = keep.tile([P, C], F32, name="gate_rows")
         gate_cols = keep.tile([P, E], F32, name="gate_cols")
         identity = keep.tile([P, P], F32, name="identity")
@@ -51,25 +52,25 @@ def tile_moe_adb_relu_kernel(tc, dy_words, dy_scales, wt, wbt, wat, a, gate, off
         def staged(shape, dtype, name, handed=None):
             if handed:
                 return ring.tile(shape, dtype, name=name, tag=handed, bufs=1, align_bytes=64)
-            return ring.tile(shape, dtype, name=name, tag="staged", bufs=STAGED_BUFS, align_bytes=64)
+            return ring.tile(shape, dtype, name=name, tag="staged", bufs=STAGED_BUFS, align_bytes=AXI)
 
         raw = {}
         saved = {}
 
         def load_whole(matrix, source):
-            whole = ring.tile([P, PACK, WIDTH], F32, name="whole", tag="whole", bufs=MATRICES - 1)
+            whole = ring.tile([P, PACK, WIDTH], F32, name="whole", tag="whole", bufs=MATRICES - 1, align_bytes=AXI)
             nc.sync.dma_start(whole[:], source.rearrange("(p r) c -> p r c", r=PACK))
             for side in range(2):
                 raw[matrix + (side,)] = whole[:, :, side * HALF : (side + 1) * HALF]
 
         def load_half(half, source):
-            part = ring.tile([P, PACK, HALF], F32, name="part", tag="part", bufs=2)
+            part = ring.tile([P, PACK, HALF], F32, name="part", tag="part", bufs=2, align_bytes=AXI)
             cols = slice(half[2] * HALF, (half[2] + 1) * HALF)
             nc.sync.dma_start(part[:], source[:, cols].rearrange("(p r) c -> p r c", r=PACK))
             raw[half] = part[:]
 
         def load_saved(first):
-            both = keep.tile([P, PACK, PAIR * C], F32, name=f"saved{first}")
+            both = keep.tile([P, PACK, PAIR * C], F32, name=f"saved{first}", align_bytes=AXI)
             nc.sync.dma_start(both[:], a[:, first * C : (first + PAIR) * C].rearrange("(p r) s -> p r s", r=PACK))
             for place in range(PAIR):
                 saved[first + place] = both[:, :, place * C : (place + 1) * C]

@@ -18,20 +18,18 @@ COPY = mybir.ActivationFunctionType.Copy
 
 P = 128
 PACK = 4
-WIDTH = 512
-HALF = WIDTH // 2
+TILES = 4
 LINE = 4
 AXI = 256
 QUADRANT = 32
 SCALE_ROWS = 4
 PER_COLUMN = 16
 BANK = 512
-K_TILES = K // P
+BANKS = 8
 PAIR = 2
 STAGED_BUFS = 32
-MATRICES = 2 * E + 1
+PLANE_BUFS = 40
 LAST = E - 1
-FROZEN = E
 
 
 def tile_moe_adb_relu_kernel(tc, dy_words, dy_scales, wt, wbt, wat, a, gate, offs, out):
@@ -39,7 +37,7 @@ def tile_moe_adb_relu_kernel(tc, dy_words, dy_scales, wt, wbt, wat, a, gate, off
     with ExitStack() as ctx:
         keep = ctx.enter_context(tc.tile_pool(name="keep", bufs=1))
         ring = ctx.enter_context(tc.tile_pool(name="ring", bufs=2))
-        psum = ctx.enter_context(tc.psum_pool(name="psum", bufs=2))
+        psum = ctx.enter_context(tc.psum_pool(name="psum", bufs=BANKS))
 
         offsets = keep.tile([P, T // PER_COLUMN], U16, name="offsets")
         words = keep.tile([P, T], I32, name="words", align_bytes=AXI)
@@ -47,27 +45,24 @@ def tile_moe_adb_relu_kernel(tc, dy_words, dy_scales, wt, wbt, wat, a, gate, off
         gate_rows = keep.tile([P, C], F32, name="gate_rows")
         gate_cols = keep.tile([P, E], F32, name="gate_cols")
         identity = keep.tile([P, P], F32, name="identity")
-        windows = [keep.tile([P, T], F32, name=f"window{kt}") for kt in range(K_TILES)]
+        windows = [keep.tile([P, T], F32, name=f"window{kt}") for kt in range(TILES)]
 
-        def staged(shape, dtype, name, handed=None):
-            if handed:
-                return ring.tile(shape, dtype, name=name, tag=handed, bufs=1, align_bytes=64)
+        def staged(shape, dtype, name):
             return ring.tile(shape, dtype, name=name, tag="staged", bufs=STAGED_BUFS, align_bytes=AXI)
+
+        def bank(shape, name):
+            return psum.tile(shape, F32, name=name, tag="bank")
 
         raw = {}
         saved = {}
 
-        def load_whole(matrix, source):
-            whole = ring.tile([P, PACK, WIDTH], F32, name="whole", tag="whole", bufs=MATRICES - 1, align_bytes=AXI)
-            nc.sync.dma_start(whole[:], source.rearrange("(p r) c -> p r c", r=PACK))
-            for side in range(2):
-                raw[matrix + (side,)] = whole[:, :, side * HALF : (side + 1) * HALF]
-
-        def load_half(half, source):
-            part = ring.tile([P, PACK, HALF], F32, name="part", tag="part", bufs=2, align_bytes=AXI)
-            cols = slice(half[2] * HALF, (half[2] + 1) * HALF)
+        def load_part(matrix, first, count):
+            source = {"wbt": wbt[matrix[1]], "wat": wat[matrix[1]], "wt": wt}[matrix[0]]
+            part = keep.tile([P, PACK, count * P], F32, name=f"{matrix[0]}{matrix[1]}_{first}", align_bytes=AXI)
+            cols = slice(first * P, (first + count) * P)
             nc.sync.dma_start(part[:], source[:, cols].rearrange("(p r) c -> p r c", r=PACK))
-            raw[half] = part[:]
+            for place in range(count):
+                raw[matrix, first + place] = part[:, :, place * P : count * P]
 
         def load_saved(first):
             both = keep.tile([P, PACK, PAIR * C], F32, name=f"saved{first}", align_bytes=AXI)
@@ -79,25 +74,38 @@ def tile_moe_adb_relu_kernel(tc, dy_words, dy_scales, wt, wbt, wat, a, gate, off
         nc.gpsimd.memset(gate_rows[:], 0.0)
         nc.sync.dma_start(words[:], dy_words[0].rearrange("p t r -> p (t r)").bitcast(I32))
         nc.sync.dma_start(offsets[:], offs)
-        load_whole(("n", 0), wbt[0])
+        load_part(("wbt", 0), 0, TILES)
         for row in range(SCALE_ROWS):
             nc.sync.dma_start(scales[row:P:QUADRANT, :].bitcast(I32), dy_scales[0, row::SCALE_ROWS, :].bitcast(I32))
         nc.sync.dma_start(gate_rows[0:E, :], gate[0].rearrange("(e u) -> e u", u=C))
-        load_saved(0)
-        for e in range(E):
-            load_whole(("i", e), wat[e])
-            if e + 1 == LAST:
-                load_half(("n", LAST, 1), wbt[LAST])
-                load_half(("n", LAST, 0), wbt[LAST])
-            else:
-                load_whole(("n", e + 1), wbt[e + 1] if e < LAST else wt)
-            if (e + 1) % PAIR == 0 and e < LAST:
-                load_saved(e + 1)
+        for e in range(LAST):
+            if e > 0:
+                load_part(("wbt", e), 0, TILES)
+            if e % PAIR == 0:
+                load_saved(e)
+            load_part(("wat", e), 0, TILES if e < LAST - 1 else 2)
+        load_part(("wbt", LAST), 0, TILES)
+        load_part(("wat", LAST - 1), 2, 2)
+        load_part(("wat", LAST), 0, 2)
+        load_part(("wt", 0), 0, 2)
+        load_part(("wat", LAST), 2, 2)
+        load_part(("wt", 0), 2, 1)
+        load_part(("wt", 0), 3, 1)
 
-        make_identity(nc, identity[:])
-        turned_gate = psum.tile([P, P], F32, name="turned_gate", tag="turned")
-        nc.tensor.transpose(turned_gate[:], gate_rows[:], identity[:])
-        nc.scalar.activation(gate_cols[:], turned_gate[:, 0:E], COPY)
+        on_vector = nc.vector.tensor_copy
+        on_scalar = nc.scalar.copy
+        gate_wide = {}
+
+        def spread_gate():
+            make_identity(nc, identity[:])
+            turned = bank([P, P], "turned")
+            nc.tensor.transpose(turned[:], gate_rows[:], identity[:])
+            nc.scalar.copy(gate_cols[:], turned[:, 0:E])
+            for first in range(0, E, BANK // C):
+                wide = bank([P, min(BANK // C, E - first), C], "wide")
+                for e in range(first, min(first + BANK // C, E)):
+                    gate_wide[e] = wide[:, e - first, :]
+                    nc.tensor.transpose(gate_wide[e], gate_cols[:, e : e + 1].to_broadcast([P, P]), identity[:])
 
         slot_words = {}
         slot_scales = {}
@@ -105,8 +113,8 @@ def tile_moe_adb_relu_kernel(tc, dy_words, dy_scales, wt, wbt, wat, a, gate, off
         def entries(first, count):
             return offsets[:, first * C // PER_COLUMN : (first + count) * C // PER_COLUMN]
 
-        def gather(table, dtype, gathered, first, count, tag):
-            part = staged([P, count * C], dtype, "gathered", tag)
+        def gather(table, dtype, gathered, first, count):
+            part = staged([P, count * C], dtype, "gathered")
             nc.vector.tensor_copy(part[:], table.indirect(entries(first, count)))
             for place in range(count):
                 gathered[first + place] = part[:, place * C : (place + 1) * C]
@@ -121,67 +129,62 @@ def tile_moe_adb_relu_kernel(tc, dy_words, dy_scales, wt, wbt, wat, a, gate, off
         codes = {}
         planes = {}
 
-        def round_half(half, engine, handed=None):
-            rounded[half] = staged([P, HALF, PACK], BF16, "rounded", handed)
-            if engine == "gpsimd":
-                nc.gpsimd.tensor_copy(rounded[half][:], raw[half].rearrange("p r c -> p c r"))
-            else:
-                copy = nc.scalar.copy if engine == "scalar" else nc.vector.tensor_copy
-                copy(*by_lines(rounded[half][:], raw[half]))
+        def round_part(matrix, first, count, engine):
+            rounded[matrix, first] = staged([P, count, P, PACK], BF16, "rounded")
+            written = rounded[matrix, first][:].rearrange("p s m r -> p (s m) r")
+            engine(*by_lines(written, raw[matrix, first][:, :, 0 : count * P]))
 
-        def quantise_half(half):
-            codes[half] = staged([P, HALF], U32, "codes")
-            planes[half] = ring.tile([P, HALF], U8, name="planes", tag="planes", bufs=2 * MATRICES, align_bytes=64)
+        def round_dealt(e, first, engine, tiles=range(TILES)):
+            matrix = ("wbt", e)
+            if tiles.start == 0:
+                rounded[matrix, first] = staged([P, 2, P, PACK], BF16, "rounded")
+            places = slice(tiles.start * P // PACK, tiles.stop * P // PACK)
+            read = raw[matrix, tiles.start][:, :, 0 : len(tiles) * P].rearrange("p r (m s) -> p m r s", s=PACK)
+            engine(rounded[matrix, first][:, :, places, :].rearrange("p s m r -> p m r s"), read[:, :, :, first : first + 2])
+
+        def quantise_part(matrix, first, count):
+            packed = staged([P, count * P], U32, "codes")
+            plane = ring.tile([P, count * P], U8, name="plane", tag="plane", bufs=PLANE_BUFS, align_bytes=64)
             nc.vector.quantize_mx(
-                out=codes[half][:].bitcast(FP8X4),
-                scales=planes[half][:],
-                in_=rounded[half][:].rearrange("p c r -> p (c r)"),
+                out=packed[:].bitcast(FP8X4),
+                scales=plane[:],
+                in_=rounded[matrix, first][:].rearrange("p s m r -> p (s m r)"),
+            )
+            for place in range(count):
+                codes[matrix, first + place] = packed[:, place * P : (place + 1) * P]
+                planes[matrix, first + place] = plane[:, place * P : (place + 1) * P]
+
+        def multiply(sums, matrix, st, moving, moving_scales):
+            nc.tensor.matmul_mx(
+                out=sums,
+                lhsT=codes[matrix, st].bitcast(FP8X4),
+                lhsT_scale=planes[matrix, st],
+                rhs=moving.bitcast(FP8X4),
+                rhs_scale=moving_scales,
+                start=True,
+                stop=True,
             )
 
         sums = {}
-        turned = {}
-        positive = {}
+        factor = {}
         dh = {}
         dh_codes = {}
         dh_planes = {}
 
         def first_product(e):
-            sums[e] = psum.tile([P, H], F32, name="sums", tag="sums")
-            for side in range(2):
-                nc.tensor.matmul_mx(
-                    out=sums[e][:, side * HALF : (side + 1) * HALF],
-                    lhsT=slot_words[e].bitcast(FP8X4),
-                    lhsT_scale=slot_scales[e],
-                    rhs=codes["n", e, side][:].bitcast(FP8X4),
-                    rhs_scale=planes["n", e, side][:],
-                    start=True,
-                    stop=True,
-                )
+            sums[e] = bank([P, PACK, C], "sums")
+            for r in range(PACK):
+                multiply(sums[e][:, r, :], ("wbt", e), r, slot_words[e], slot_scales[e])
 
-        def gate_and_turn(e):
-            gated = staged([P, 2, P, 2], BF16, "gated")
-            nc.scalar.activation(
-                gated[:], sums[e][:].rearrange("u (p h j) -> u h p j", h=2, j=2), COPY, scale=gate_cols[:, e : e + 1]
-            )
-            pairs = gated[:].rearrange("u h p j -> u (h p j)").bitcast(F32)
-            turned[e] = psum.tile([P, 2, C], F32, name="turned", tag="turned")
-            for h in range(2):
-                nc.tensor.transpose(turned[e][:, h, :], pairs[:, h * P : (h + 1) * P], identity[:])
+        def make_factor(e):
+            factor[e] = staged([P, PACK, C], F32, "factor")
+            spread = gate_wide[e].unsqueeze(1).to_broadcast([P, PACK, C])
+            nc.vector.scalar_tensor_tensor(factor[e][:], saved[e], 0.0, spread, ALU.is_gt, ALU.mult)
 
-        def compare(e):
-            positive[e] = staged([P, C, PACK], BF16, "positive")
-            written, read = by_lines(positive[e][:], saved[e])
-            nc.vector.tensor_scalar(written, read, 0.0, 1.0, ALU.is_gt, ALU.mult)
-
-        def mask(e):
+        def make_dh(e):
             dh[e] = staged([P, C, PACK], BF16, "dh")
-            values = turned[e][:].rearrange("p h u -> p (h u)").bitcast(BF16)
-            nc.vector.tensor_tensor(
-                dh[e][:].rearrange("p u (h j) -> p u h j", j=2),
-                values.rearrange("p (h u j) -> p u h j", h=2, j=2),
-                positive[e][:].rearrange("p u (h j) -> p u h j", j=2),
-                ALU.mult,
-            )
+            written, read = by_lines(dh[e][:], sums[e][:])
+            nc.vector.tensor_tensor(written, read, factor[e][:].rearrange("p r (c i) -> p c r i", i=LINE), ALU.mult)
 
         def quantise_dh(e):
             dh_codes[e] = staged([P, C], U32, "dh_codes")
@@ -192,170 +195,128 @@ def tile_moe_adb_relu_kernel(tc, dy_words, dy_scales, wt, wbt, wat, a, gate, off
                 in_=dh[e][:].rearrange("p u r -> p (u r)"),
             )
 
-        product = {}
+        products = {}
 
-        def second_product(e, side):
-            product[e, side] = psum.tile([P, 2, C], F32, name="product", tag="product", bufs=3)
-            for place in range(2):
-                cols = slice(place * P, (place + 1) * P)
-                nc.tensor.matmul_mx(
-                    out=product[e, side][:, place, :],
-                    lhsT=codes["i", e, side][:, cols].bitcast(FP8X4),
-                    lhsT_scale=planes["i", e, side][:, cols],
-                    rhs=dh_codes[e][:].bitcast(FP8X4),
-                    rhs_scale=dh_planes[e][:],
-                    start=True,
-                    stop=True,
-                )
-
-        def finish_adapter(e):
-            quantise_half(("i", e, 0))
-            quantise_dh(e)
-            second_product(e, 0)
-            quantise_half(("i", e, 1))
-            second_product(e, 1)
+        def second_product(e, first, count):
+            product = bank([P, count, C], "product")
+            for place in range(count):
+                products[e, first + place] = (product, place)
+                multiply(product[:, place, :], ("wat", e), first + place, dh_codes[e][:], dh_planes[e][:])
 
         dx = {}
 
-        def leave_psum(e, first, count):
+        def leave_psum(e, first, count, engine):
             part = staged([P, count, C], F32, "dx")
-            nc.scalar.copy(part[:], product[e, first // 2][:, first % 2 : first % 2 + count, :])
-            for place in range(count):
-                dx[e, first + place] = part[:, place, :]
+            product, place = products[e, first]
+            engine(part[:], product[:, place : place + count, :])
+            for kt in range(first, first + count):
+                dx[e, kt] = part[:, kt - first, :]
 
-        def scatter(e, kt):
-            nc.vector.tensor_copy(windows[kt][:].indirect(entries(e, 1)), dx[e, kt])
+        def scatter(e, kt, by_vector=False):
+            window = windows[kt][:].indirect(entries(e, 1))
+            if by_vector:
+                nc.vector.tensor_copy(window, dx[e, kt])
+            else:
+                nc.scalar.activation(window, dx[e, kt], COPY)
 
         def send_back(e, first, count):
-            leave_psum(e, first, count)
+            leave_psum(e, first, count, on_scalar)
             for kt in range(first, first + count):
                 scatter(e, kt)
 
         tokens = (slice(0, BANK), slice(BANK, T))
         base = {}
         short = {}
-        parked = {}
-        result = {}
 
         def frozen_product(kt):
-            cols = slice(kt % 2 * P, (kt % 2 + 1) * P)
             if kt % 2 == 0:
-                short[kt // 2] = psum.tile([P, 2, T - BANK], F32, name="short", tag="sums")
-            if kt == 2:
-                long = psum.tile([P, BANK], F32, name="long", tag="spare", bufs=1)
-            else:
-                long = psum.tile([P, BANK], F32, name="long", tag="turned")
+                short[kt // 2] = bank([P, 2, T - BANK], "short")
+            long = bank([P, BANK], "long")
             base[kt, 0] = long[:]
             base[kt, 1] = short[kt // 2][:, kt % 2, :]
             for n in range(2):
-                nc.tensor.matmul_mx(
-                    out=base[kt, n],
-                    lhsT=codes["n", FROZEN, kt // 2][:, cols].bitcast(FP8X4),
-                    lhsT_scale=planes["n", FROZEN, kt // 2][:, cols],
-                    rhs=words[:, tokens[n]].bitcast(FP8X4),
-                    rhs_scale=scales[:, tokens[n]],
-                    start=True,
-                    stop=True,
-                )
+                multiply(base[kt, n], ("wt", 0), kt, words[:, tokens[n]], scales[:, tokens[n]])
 
-        def park(kt, n):
-            parked[kt, n] = staged([P, tokens[n].stop - tokens[n].start], F32, "parked")
-            nc.scalar.copy(parked[kt, n][:], base[kt, n])
+        def add_and_store(kt, n):
+            result = staged([P, tokens[n].stop - tokens[n].start], F32, "result")
+            nc.vector.tensor_tensor(result[:], base[kt, n], windows[kt][:, tokens[n]], ALU.add)
+            nc.sync.dma_start(out[kt * P : (kt + 1) * P, tokens[n]], result[:])
 
-        def add(kt, n):
-            result[kt, n] = staged([P, tokens[n].stop - tokens[n].start], F32, "result")
-            if (kt, n) in parked:
-                nc.gpsimd.tensor_tensor(result[kt, n][:], parked[kt, n][:], windows[kt][:, tokens[n]], ALU.add)
-            else:
-                nc.vector.tensor_tensor(result[kt, n][:], base[kt, n], windows[kt][:, tokens[n]], ALU.add)
+        def prepare(matrix, first):
+            round_part(matrix, first, 1, on_vector)
+            round_part(matrix, first + 1, 1, on_vector)
+            quantise_part(matrix, first, 1)
+            quantise_part(matrix, first + 1, 1)
 
-        def store(kt, n):
-            queue = nc.sync if (kt, n) in parked else nc.scalar
-            queue.dma_start(out[kt * P : (kt + 1) * P, tokens[n]], result[kt, n][:])
-
-        def for_gpsimd(e):
-            return f"for_gpsimd{e % 2}"
-
-        gather(words[:].bitcast(U32), U32, slot_words, 0, PAIR, "first_words")
-        gather(words[:].bitcast(U32), U32, slot_words, PAIR, E - PAIR, "later_words")
-        round_half(("n", 0, 1), "scalar", handed="later_scales")
-        round_half(("n", 0, 0), "vector")
-        gather(scales[:], U8, slot_scales, 0, PAIR, None)
-        quantise_half(("n", 0, 0))
-        quantise_half(("n", 0, 1))
+        gather(words[:].bitcast(U32), U32, slot_words, 0, PAIR)
+        gather(words[:].bitcast(U32), U32, slot_words, PAIR, E - PAIR)
+        round_dealt(0, 2, on_scalar)
+        round_dealt(0, 0, on_vector)
+        spread_gate()
+        gather(scales[:], U8, slot_scales, 0, PAIR)
+        quantise_part(("wbt", 0), 0, 2)
+        quantise_part(("wbt", 0), 2, 2)
         first_product(0)
-        gather(scales[:], U8, slot_scales, PAIR, E - PAIR, "later_scales")
-        compare(0)
-        gate_and_turn(0)
-        round_half(("i", 0, 1), "scalar")
-        round_half(("i", 0, 0), "vector")
-        compare(1)
-        mask(0)
-        finish_adapter(0)
-
-        round_half(("n", 1, 0), "scalar", handed=for_gpsimd(0))
-        round_half(("n", 1, 1), "vector")
-        leave_psum(0, 0, 2)
-        quantise_half(("n", 1, 1))
-        quantise_half(("n", 1, 0))
-        first_product(1)
-        round_half(("i", 1, 1), "gpsimd", handed=for_gpsimd(0))
-        scatter(0, 0)
-        scatter(0, 1)
+        gather(scales[:], U8, slot_scales, PAIR, E - PAIR)
+        make_factor(0)
+        make_dh(0)
+        make_factor(1)
+        quantise_dh(0)
+        round_part(("wat", 0), 2, 2, on_scalar)
+        prepare(("wat", 0), 0)
+        second_product(0, 0, 2)
+        send_back(0, 0, 2)
+        quantise_part(("wat", 0), 2, 2)
+        second_product(0, 2, 2)
         send_back(0, 2, 2)
-        gate_and_turn(1)
-        round_half(("i", 1, 0), "scalar")
-        mask(1)
-        round_half(("n", 2, 0), "scalar")
-        round_half(("n", 2, 1), "scalar", handed=for_gpsimd(1))
-        finish_adapter(1)
-        compare(2)
-
         for e in range(1, LAST):
-            quantise_half(("n", e + 1, 0))
-            quantise_half(("n", e + 1, 1))
-            first_product(e + 1)
-            if e + 1 not in positive:
-                compare(e + 1)
-            round_half(("i", e + 1, 1), "gpsimd", handed=for_gpsimd(e))
-            send_back(e, 0, 2)
-            send_back(e, 2, 1)
-            if e == 1:
-                gate_and_turn(e + 1)
-                round_half(("i", e + 1, 0), "scalar")
+            round_dealt(e, 0, on_vector)
+            round_dealt(e, 2, on_vector)
+            quantise_part(("wbt", e), 0, 2)
+            quantise_part(("wbt", e), 2, 2)
+            first_product(e)
+            if e > 1:
+                make_factor(e)
+            if e % PAIR == 0:
+                make_dh(e)
+            round_part(("wat", e), 0, 2, on_vector)
+            if e % PAIR == 1:
+                make_dh(e)
+                quantise_part(("wat", e), 0, 2)
+                quantise_dh(e)
             else:
-                round_half(("i", e + 1, 0), "scalar")
-                gate_and_turn(e + 1)
-            mask(e + 1)
-            if e + 1 < LAST:
-                finish_adapter(e + 1)
-                send_back(e, 3, 1)
-                round_half(("n", e + 2, 0), "scalar")
-                round_half(("n", e + 2, 1), "scalar", handed=for_gpsimd(e + 1))
-
-        round_half(("n", FROZEN, 0), "scalar")
-        finish_adapter(LAST)
-        quantise_half(("n", FROZEN, 0))
+                quantise_dh(e)
+                quantise_part(("wat", e), 0, 2)
+            second_product(e, 0, 2)
+            send_back(e, 0, 2)
+            if e < LAST - 1:
+                prepare(("wat", e), 2)
+                second_product(e, 2, 2)
+                send_back(e, 2, 2)
+        round_dealt(LAST, 0, on_vector)
+        round_dealt(LAST, 2, on_vector)
+        quantise_part(("wbt", LAST), 0, 2)
+        quantise_part(("wbt", LAST), 2, 2)
+        first_product(LAST)
+        prepare(("wat", LAST - 1), 2)
+        second_product(LAST - 1, 2, 2)
+        send_back(LAST - 1, 2, 2)
+        make_factor(LAST)
+        round_part(("wat", LAST), 0, 2, on_vector)
+        make_dh(LAST)
+        quantise_part(("wat", LAST), 0, 2)
+        quantise_dh(LAST)
+        second_product(LAST, 0, 2)
+        send_back(LAST, 0, 2)
+        prepare(("wt", 0), 0)
         frozen_product(0)
         frozen_product(1)
-        send_back(LAST - 1, 3, 1)
-        round_half(("n", FROZEN, 1), "scalar")
-        quantise_half(("n", FROZEN, 1))
-        send_back(LAST, 0, 2)
-        park(0, 0)
+        prepare(("wat", LAST), 2)
+        second_product(LAST, 2, 2)
+        send_back(LAST, 2, 2)
+        prepare(("wt", 0), 2)
         frozen_product(2)
         frozen_product(3)
-        send_back(LAST, 2, 1)
-        park(0, 1)
-        park(2, 0)
-        add(0, 0)
-        add(1, 0)
-        add(1, 1)
-        send_back(LAST, 3, 1)
-        add(0, 1)
-        add(2, 1)
-        add(2, 0)
-        add(3, 0)
-        add(3, 1)
-        for kt, n in result:
-            store(kt, n)
+        for kt in range(TILES):
+            for n in range(2):
+                add_and_store(kt, n)

@@ -224,6 +224,12 @@ def tile_moe_adb_relu_kernel(tc, dy_words, dy_scales, wt, wbt, wat, a, gate, off
             for kt in range(first, first + count):
                 scatter(e, kt)
 
+        def send_back_singly(e, first):
+            leave_psum(e, first, 1, on_scalar)
+            leave_psum(e, first + 1, 1, on_scalar)
+            scatter(e, first)
+            scatter(e, first + 1)
+
         tokens = (slice(0, BANK), slice(BANK, T))
         base = {}
         short = {}
@@ -260,60 +266,71 @@ def tile_moe_adb_relu_kernel(tc, dy_words, dy_scales, wt, wbt, wat, a, gate, off
         gather(scales[:], U8, slot_scales, PAIR, E - PAIR)
         make_factor(0)
         make_dh(0)
-        make_factor(1)
-        quantise_dh(0)
         round_part(("wat", 0), 2, 2, on_scalar)
-        prepare(("wat", 0), 0)
+        round_part(("wat", 0), 0, 2, on_vector)
+        quantise_dh(0)
+        quantise_part(("wat", 0), 0, 2)
         second_product(0, 0, 2)
-        send_back(0, 0, 2)
+        make_factor(1)
         quantise_part(("wat", 0), 2, 2)
         second_product(0, 2, 2)
-        send_back(0, 2, 2)
         for e in range(1, LAST):
+            last = e == LAST - 1
+            shared = 0 if last else 2
+            send_back_singly(e - 1, 0)
             round_dealt(e, 0, on_vector)
             round_dealt(e, 2, on_vector)
             quantise_part(("wbt", e), 0, 2)
             quantise_part(("wbt", e), 2, 2)
             first_product(e)
-            if e > 1:
-                make_factor(e)
             if e % PAIR == 0:
+                make_factor(e)
                 make_dh(e)
-            round_part(("wat", e), 0, 2, on_vector)
-            if e % PAIR == 1:
-                make_dh(e)
-                quantise_part(("wat", e), 0, 2)
-                quantise_dh(e)
+                if not last:
+                    make_factor(e + 1)
+                    round_part(("wat", e), 0, 2, on_vector)
+                    quantise_dh(e)
             else:
+                round_part(("wat", e), 0, 2, on_vector)
+                make_dh(e)
+            round_part(("wat", e), shared, 1, on_vector)
+            leave_psum(e - 1, 2, 2, on_scalar)
+            round_part(("wat", e), shared + 1, 1, on_scalar)
+            scatter(e - 1, 2)
+            scatter(e - 1, 3)
+            if e % PAIR == 1 or last:
                 quantise_dh(e)
+            if not last:
                 quantise_part(("wat", e), 0, 2)
-            second_product(e, 0, 2)
-            send_back(e, 0, 2)
-            if e < LAST - 1:
-                prepare(("wat", e), 2)
-                second_product(e, 2, 2)
-                send_back(e, 2, 2)
+                second_product(e, 0, 2)
+            quantise_part(("wat", e), shared, 1)
+            quantise_part(("wat", e), shared + 1, 1)
+            second_product(e, shared, 2)
+        make_factor(LAST)
         round_dealt(LAST, 0, on_vector)
         round_dealt(LAST, 2, on_vector)
         quantise_part(("wbt", LAST), 0, 2)
+        leave_psum(LAST - 1, 0, 2, on_scalar)
+        round_part(("wat", LAST - 1), 2, 2, on_scalar)
+        scatter(LAST - 1, 0)
+        scatter(LAST - 1, 1)
         quantise_part(("wbt", LAST), 2, 2)
         first_product(LAST)
-        prepare(("wat", LAST - 1), 2)
-        second_product(LAST - 1, 2, 2)
-        send_back(LAST - 1, 2, 2)
-        make_factor(LAST)
         round_part(("wat", LAST), 0, 2, on_vector)
+        quantise_part(("wat", LAST - 1), 2, 2)
+        second_product(LAST - 1, 2, 2)
         make_dh(LAST)
         quantise_part(("wat", LAST), 0, 2)
         quantise_dh(LAST)
+        send_back_singly(LAST - 1, 2)
         second_product(LAST, 0, 2)
-        send_back(LAST, 0, 2)
         prepare(("wt", 0), 0)
         frozen_product(0)
         frozen_product(1)
+        send_back_singly(LAST, 0)
         prepare(("wat", LAST), 2)
         second_product(LAST, 2, 2)
-        send_back(LAST, 2, 2)
+        send_back_singly(LAST, 2)
         prepare(("wt", 0), 2)
         frozen_product(2)
         frozen_product(3)

@@ -27,8 +27,8 @@ PER_COLUMN = 16
 BANK = 512
 BANKS = 8
 PAIR = 2
-STAGED_BUFS = 32
-PLANE_BUFS = 40
+STAGED_BUFS = 22
+PLANE_BUFS = 36
 LAST = E - 1
 
 
@@ -134,13 +134,17 @@ def tile_moe_adb_relu_kernel(tc, dy_words, dy_scales, wt, wbt, wat, a, gate, off
             written = rounded[matrix, first][:].rearrange("p s m r -> p (s m) r")
             engine(*by_lines(written, raw[matrix, first][:, :, 0 : count * P]))
 
-        def round_dealt(e, first, engine, tiles=range(TILES)):
-            matrix = ("wbt", e)
-            if tiles.start == 0:
-                rounded[matrix, first] = staged([P, 2, P, PACK], BF16, "rounded")
-            places = slice(tiles.start * P // PACK, tiles.stop * P // PACK)
-            read = raw[matrix, tiles.start][:, :, 0 : len(tiles) * P].rearrange("p r (m s) -> p m r s", s=PACK)
-            engine(rounded[matrix, first][:, :, places, :].rearrange("p s m r -> p m r s"), read[:, :, :, first : first + 2])
+        def round_dealt(e):
+            whole = staged([P, TILES, P, PACK], BF16, "rounded")
+            read = raw[("wbt", e), 0].rearrange("p r (m s) -> p m r s", s=TILES)
+            nc.vector.tensor_copy(whole[:].rearrange("p s m r -> p m r s"), read)
+            for first in (0, 2):
+                rounded[("wbt", e), first] = whole[:, first : first + 2, :, :]
+
+        def round_dealt_pair(e, first, engine):
+            rounded[("wbt", e), first] = staged([P, 2, P, PACK], BF16, "rounded")
+            read = raw[("wbt", e), 0].rearrange("p r (m s) -> p m r s", s=TILES)[:, :, :, first : first + 2]
+            engine(rounded[("wbt", e), first][:].rearrange("p s m r -> p m r s"), read)
 
         def quantise_part(matrix, first, count):
             packed = staged([P, count * P], U32, "codes")
@@ -232,21 +236,32 @@ def tile_moe_adb_relu_kernel(tc, dy_words, dy_scales, wt, wbt, wat, a, gate, off
 
         tokens = (slice(0, BANK), slice(BANK, T))
         base = {}
-        short = {}
 
-        def frozen_product(kt):
-            if kt % 2 == 0:
-                short[kt // 2] = bank([P, 2, T - BANK], "short")
-            long = bank([P, BANK], "long")
-            base[kt, 0] = long[:]
-            base[kt, 1] = short[kt // 2][:, kt % 2, :]
-            for n in range(2):
-                multiply(base[kt, n], ("wt", 0), kt, words[:, tokens[n]], scales[:, tokens[n]])
+        def frozen_long(kt):
+            base[kt, 0] = bank([P, BANK], "long")[:]
+            multiply(base[kt, 0], ("wt", 0), kt, words[:, tokens[0]], scales[:, tokens[0]])
 
-        def add_and_store(kt, n):
-            result = staged([P, tokens[n].stop - tokens[n].start], F32, "result")
-            nc.vector.tensor_tensor(result[:], base[kt, n], windows[kt][:, tokens[n]], ALU.add)
-            nc.sync.dma_start(out[kt * P : (kt + 1) * P, tokens[n]], result[:])
+        def frozen_short(first):
+            both = bank([P, 2, T - BANK], "short")
+            for place in range(2):
+                base[first + place, 1] = both[:, place, :]
+                multiply(both[:, place, :], ("wt", 0), first + place, words[:, tokens[1]], scales[:, tokens[1]])
+
+        def add(kt, result, first, count):
+            n = first // BANK
+            sums_of_piece = base[kt, n][:, first - n * BANK : first - n * BANK + count]
+            nc.vector.tensor_tensor(result, sums_of_piece, windows[kt][:, first : first + count], ALU.add)
+
+        def finish_whole(kt):
+            result = staged([P, T], F32, "result")
+            for cols in tokens:
+                add(kt, result[:, cols], cols.start, cols.stop - cols.start)
+            nc.sync.dma_start(out[kt * P : (kt + 1) * P, :], result[:])
+
+        def finish_piece(kt, first, count):
+            result = staged([P, count], F32, "result")
+            add(kt, result[:], first, count)
+            nc.sync.dma_start(out[kt * P : (kt + 1) * P, first : first + count], result[:])
 
         def prepare(matrix, first):
             round_part(matrix, first, 1, on_vector)
@@ -256,8 +271,8 @@ def tile_moe_adb_relu_kernel(tc, dy_words, dy_scales, wt, wbt, wat, a, gate, off
 
         gather(words[:].bitcast(U32), U32, slot_words, 0, PAIR)
         gather(words[:].bitcast(U32), U32, slot_words, PAIR, E - PAIR)
-        round_dealt(0, 2, on_scalar)
-        round_dealt(0, 0, on_vector)
+        round_dealt_pair(0, 2, on_scalar)
+        round_dealt_pair(0, 0, on_vector)
         spread_gate()
         gather(scales[:], U8, slot_scales, 0, PAIR)
         quantise_part(("wbt", 0), 0, 2)
@@ -265,75 +280,117 @@ def tile_moe_adb_relu_kernel(tc, dy_words, dy_scales, wt, wbt, wat, a, gate, off
         first_product(0)
         gather(scales[:], U8, slot_scales, PAIR, E - PAIR)
         make_factor(0)
+        make_factor(1)
         make_dh(0)
         round_part(("wat", 0), 2, 2, on_scalar)
-        round_part(("wat", 0), 0, 2, on_vector)
+        round_part(("wat", 0), 0, 1, on_vector)
         quantise_dh(0)
-        quantise_part(("wat", 0), 0, 2)
+        round_part(("wat", 0), 1, 1, on_vector)
+        quantise_part(("wat", 0), 0, 1)
+        quantise_part(("wat", 0), 1, 1)
         second_product(0, 0, 2)
-        make_factor(1)
         quantise_part(("wat", 0), 2, 2)
         second_product(0, 2, 2)
-        for e in range(1, LAST):
-            last = e == LAST - 1
-            shared = 0 if last else 2
+        for e in range(1, LAST - 1):
             send_back_singly(e - 1, 0)
-            round_dealt(e, 0, on_vector)
-            round_dealt(e, 2, on_vector)
+            round_dealt(e)
+            if e % PAIR == 0:
+                make_factor(e)
+            elif e > 1:
+                quantise_part(("wat", e - 1), 3, 1)
+                second_product(e - 1, 2, 2)
             quantise_part(("wbt", e), 0, 2)
             quantise_part(("wbt", e), 2, 2)
             first_product(e)
             if e % PAIR == 0:
-                make_factor(e)
+                make_factor(e + 1)
                 make_dh(e)
-                if not last:
-                    make_factor(e + 1)
-                    round_part(("wat", e), 0, 2, on_vector)
-                    quantise_dh(e)
+                round_part(("wat", e), 0, 2, on_vector)
+                quantise_dh(e)
             else:
                 round_part(("wat", e), 0, 2, on_vector)
                 make_dh(e)
-            round_part(("wat", e), shared, 1, on_vector)
+            round_part(("wat", e), 2, 1, on_vector)
             leave_psum(e - 1, 2, 2, on_scalar)
-            round_part(("wat", e), shared + 1, 1, on_scalar)
+            round_part(("wat", e), 3, 1, on_scalar)
             scatter(e - 1, 2)
             scatter(e - 1, 3)
-            if e % PAIR == 1 or last:
+            if e % PAIR == 1:
                 quantise_dh(e)
-            if not last:
-                quantise_part(("wat", e), 0, 2)
-                second_product(e, 0, 2)
-            quantise_part(("wat", e), shared, 1)
-            quantise_part(("wat", e), shared + 1, 1)
-            second_product(e, shared, 2)
+            quantise_part(("wat", e), 0, 2)
+            second_product(e, 0, 2)
+            quantise_part(("wat", e), 2, 1)
+            if e % PAIR == 1:
+                quantise_part(("wat", e), 3, 1)
+                second_product(e, 2, 2)
+        e = LAST - 1
+        send_back_singly(e - 1, 0)
+        round_dealt(e)
+        make_factor(e)
+        quantise_part(("wbt", e), 0, 2)
+        quantise_part(("wbt", e), 2, 2)
+        first_product(e)
         make_factor(LAST)
-        round_dealt(LAST, 0, on_vector)
-        round_dealt(LAST, 2, on_vector)
+        round_part(("wat", e), 0, 1, on_vector)
+        leave_psum(e - 1, 2, 2, on_scalar)
+        round_part(("wat", e), 1, 1, on_scalar)
+        scatter(e - 1, 2)
+        scatter(e - 1, 3)
+        make_dh(e)
+        quantise_part(("wat", e), 0, 1)
+        quantise_dh(e)
+        quantise_part(("wat", e), 1, 1)
+        second_product(e, 0, 2)
+        round_dealt(LAST)
+        round_part(("wat", e), 2, 1, on_vector)
         quantise_part(("wbt", LAST), 0, 2)
-        leave_psum(LAST - 1, 0, 2, on_scalar)
-        round_part(("wat", LAST - 1), 2, 2, on_scalar)
-        scatter(LAST - 1, 0)
-        scatter(LAST - 1, 1)
+        leave_psum(e, 0, 2, on_scalar)
+        round_part(("wat", e), 3, 1, on_scalar)
+        scatter(e, 0)
+        scatter(e, 1)
         quantise_part(("wbt", LAST), 2, 2)
         first_product(LAST)
-        round_part(("wat", LAST), 0, 2, on_vector)
-        quantise_part(("wat", LAST - 1), 2, 2)
-        second_product(LAST - 1, 2, 2)
+        quantise_part(("wat", e), 2, 1)
+        quantise_part(("wat", e), 3, 1)
+        second_product(e, 2, 2)
+        round_part(("wat", LAST), 0, 1, on_vector)
         make_dh(LAST)
-        quantise_part(("wat", LAST), 0, 2)
+        round_part(("wat", LAST), 1, 1, on_vector)
         quantise_dh(LAST)
-        send_back_singly(LAST - 1, 2)
+        quantise_part(("wat", LAST), 0, 1)
+        quantise_part(("wat", LAST), 1, 1)
         second_product(LAST, 0, 2)
-        prepare(("wt", 0), 0)
-        frozen_product(0)
-        frozen_product(1)
-        send_back_singly(LAST, 0)
-        prepare(("wat", LAST), 2)
+        leave_psum(e, 2, 1, on_scalar)
+        leave_psum(e, 3, 1, on_scalar)
+        scatter(e, 2)
+        scatter(e, 3)
+        round_part(("wt", 0), 0, 1, on_vector)
+        round_part(("wt", 0), 1, 1, on_vector)
+        quantise_part(("wt", 0), 0, 1)
+        frozen_long(0)
+        round_part(("wat", LAST), 2, 1, on_vector)
+        quantise_part(("wt", 0), 1, 1)
+        frozen_short(0)
+        leave_psum(LAST, 0, 1, on_scalar)
+        leave_psum(LAST, 1, 1, on_scalar)
+        scatter(LAST, 0)
+        scatter(LAST, 1)
+        round_part(("wat", LAST), 3, 1, on_vector)
+        quantise_part(("wat", LAST), 2, 1)
+        round_part(("wt", 0), 2, 1, on_vector)
+        quantise_part(("wat", LAST), 3, 1)
         second_product(LAST, 2, 2)
-        send_back_singly(LAST, 2)
-        prepare(("wt", 0), 2)
-        frozen_product(2)
-        frozen_product(3)
-        for kt in range(TILES):
-            for n in range(2):
-                add_and_store(kt, n)
+        frozen_long(1)
+        round_part(("wt", 0), 3, 1, on_vector)
+        quantise_part(("wt", 0), 2, 1)
+        frozen_long(2)
+        quantise_part(("wt", 0), 3, 1)
+        frozen_short(2)
+        frozen_long(3)
+        leave_psum(LAST, 2, 2, on_vector)
+        scatter(LAST, 2)
+        scatter(LAST, 3)
+        for kt in range(TILES - 1):
+            finish_whole(kt)
+        finish_piece(TILES - 1, 0, BANK)
+        finish_piece(TILES - 1, BANK, T - BANK)

@@ -19,7 +19,7 @@ COPY = mybir.ActivationFunctionType.Copy
 P = 128
 PACK = 4
 TILES = 4
-LINE = 4
+RUN = 2
 AXI = 256
 QUADRANT = 32
 SCALE_ROWS = 4
@@ -27,7 +27,7 @@ PER_COLUMN = 16
 BANK = 512
 BANKS = 8
 PAIR = 2
-STAGED_BUFS = 22
+STAGED_BUFS = 28
 PLANE_BUFS = 36
 LAST = E - 1
 
@@ -64,11 +64,11 @@ def tile_moe_adb_relu_kernel(tc, dy_words, dy_scales, wt, wbt, wat, a, gate, off
             for place in range(count):
                 raw[matrix, first + place] = part[:, :, place * P : count * P]
 
-        def load_saved(first):
-            both = keep.tile([P, PACK, PAIR * C], F32, name=f"saved{first}", align_bytes=AXI)
-            nc.sync.dma_start(both[:], a[:, first * C : (first + PAIR) * C].rearrange("(p r) s -> p r s", r=PACK))
-            for place in range(PAIR):
-                saved[first + place] = both[:, :, place * C : (place + 1) * C]
+        def load_saved(first, count):
+            part = keep.tile([P, PACK, count * C], F32, name=f"saved{first}", align_bytes=AXI)
+            nc.sync.dma_start(part[:], a[:, first * C : (first + count) * C].rearrange("(p r) s -> p r s", r=PACK))
+            for place in range(count):
+                saved[first + place] = part[:, :, place * C : (place + 1) * C]
 
         nc.gpsimd.memset(scales[:].bitcast(I32), 0)
         nc.gpsimd.memset(gate_rows[:], 0.0)
@@ -78,19 +78,24 @@ def tile_moe_adb_relu_kernel(tc, dy_words, dy_scales, wt, wbt, wat, a, gate, off
         for row in range(SCALE_ROWS):
             nc.sync.dma_start(scales[row:P:QUADRANT, :].bitcast(I32), dy_scales[0, row::SCALE_ROWS, :].bitcast(I32))
         nc.sync.dma_start(gate_rows[0:E, :], gate[0].rearrange("(e u) -> e u", u=C))
-        for e in range(LAST):
-            if e > 0:
-                load_part(("wbt", e), 0, TILES)
-            if e % PAIR == 0:
-                load_saved(e)
-            load_part(("wat", e), 0, TILES if e < LAST - 1 else 2)
-        load_part(("wbt", LAST), 0, TILES)
-        load_part(("wat", LAST - 1), 2, 2)
-        load_part(("wat", LAST), 0, 2)
+        load_saved(0, 2)
+        load_part(("wat", 0), 0, 4)
+        load_part(("wbt", 1), 0, 4)
+        load_part(("wat", 1), 0, 4)
+        load_part(("wbt", 2), 0, 4)
+        load_saved(2, 2)
+        load_part(("wat", 2), 0, 4)
+        load_part(("wbt", 3), 0, 4)
+        load_part(("wat", 3), 0, 4)
+        load_part(("wbt", 4), 0, 4)
+        load_saved(4, 2)
+        load_part(("wat", 4), 0, 2)
+        load_part(("wbt", 5), 0, 4)
+        load_part(("wat", 4), 2, 2)
+        load_part(("wat", 5), 0, 2)
         load_part(("wt", 0), 0, 2)
-        load_part(("wat", LAST), 2, 2)
-        load_part(("wt", 0), 2, 1)
-        load_part(("wt", 0), 3, 1)
+        load_part(("wat", 5), 2, 2)
+        load_part(("wt", 0), 2, 2)
 
         on_vector = nc.vector.tensor_copy
         on_scalar = nc.scalar.copy
@@ -121,8 +126,8 @@ def tile_moe_adb_relu_kernel(tc, dy_words, dy_scales, wt, wbt, wat, a, gate, off
 
         def by_lines(written, read):
             return (
-                written.rearrange("p (c i) r -> p c r i", i=LINE),
-                read.rearrange("p r (c i) -> p c r i", i=LINE),
+                written.rearrange("p (c i) r -> p c r i", i=RUN),
+                read.rearrange("p r (c i) -> p c r i", i=RUN),
             )
 
         rounded = {}
@@ -134,14 +139,7 @@ def tile_moe_adb_relu_kernel(tc, dy_words, dy_scales, wt, wbt, wat, a, gate, off
             written = rounded[matrix, first][:].rearrange("p s m r -> p (s m) r")
             engine(*by_lines(written, raw[matrix, first][:, :, 0 : count * P]))
 
-        def round_dealt(e):
-            whole = staged([P, TILES, P, PACK], BF16, "rounded")
-            read = raw[("wbt", e), 0].rearrange("p r (m s) -> p m r s", s=TILES)
-            nc.vector.tensor_copy(whole[:].rearrange("p s m r -> p m r s"), read)
-            for first in (0, 2):
-                rounded[("wbt", e), first] = whole[:, first : first + 2, :, :]
-
-        def round_dealt_pair(e, first, engine):
+        def round_dealt(e, first, engine):
             rounded[("wbt", e), first] = staged([P, 2, P, PACK], BF16, "rounded")
             read = raw[("wbt", e), 0].rearrange("p r (m s) -> p m r s", s=TILES)[:, :, :, first : first + 2]
             engine(rounded[("wbt", e), first][:].rearrange("p s m r -> p m r s"), read)
@@ -188,7 +186,7 @@ def tile_moe_adb_relu_kernel(tc, dy_words, dy_scales, wt, wbt, wat, a, gate, off
         def make_dh(e):
             dh[e] = staged([P, C, PACK], BF16, "dh")
             written, read = by_lines(dh[e][:], sums[e][:])
-            nc.vector.tensor_tensor(written, read, factor[e][:].rearrange("p r (c i) -> p c r i", i=LINE), ALU.mult)
+            nc.vector.tensor_tensor(written, read, factor[e][:].rearrange("p r (c i) -> p c r i", i=RUN), ALU.mult)
 
         def quantise_dh(e):
             dh_codes[e] = staged([P, C], U32, "dh_codes")
@@ -271,8 +269,8 @@ def tile_moe_adb_relu_kernel(tc, dy_words, dy_scales, wt, wbt, wat, a, gate, off
 
         gather(words[:].bitcast(U32), U32, slot_words, 0, PAIR)
         gather(words[:].bitcast(U32), U32, slot_words, PAIR, E - PAIR)
-        round_dealt_pair(0, 2, on_scalar)
-        round_dealt_pair(0, 0, on_vector)
+        round_dealt(0, 2, on_scalar)
+        round_dealt(0, 0, on_vector)
         spread_gate()
         gather(scales[:], U8, slot_scales, 0, PAIR)
         quantise_part(("wbt", 0), 0, 2)
@@ -293,16 +291,13 @@ def tile_moe_adb_relu_kernel(tc, dy_words, dy_scales, wt, wbt, wat, a, gate, off
         second_product(0, 2, 2)
         for e in range(1, LAST - 1):
             send_back_singly(e - 1, 0)
-            round_dealt(e)
-            if e % PAIR == 0:
-                make_factor(e)
-            elif e > 1:
-                quantise_part(("wat", e - 1), 3, 1)
-                second_product(e - 1, 2, 2)
+            round_dealt(e, 0, on_vector)
+            round_dealt(e, 2, on_vector)
             quantise_part(("wbt", e), 0, 2)
             quantise_part(("wbt", e), 2, 2)
             first_product(e)
             if e % PAIR == 0:
+                make_factor(e)
                 make_factor(e + 1)
                 make_dh(e)
                 round_part(("wat", e), 0, 2, on_vector)
@@ -312,7 +307,7 @@ def tile_moe_adb_relu_kernel(tc, dy_words, dy_scales, wt, wbt, wat, a, gate, off
                 make_dh(e)
             round_part(("wat", e), 2, 1, on_vector)
             leave_psum(e - 1, 2, 2, on_scalar)
-            round_part(("wat", e), 3, 1, on_scalar)
+            round_part(("wat", e), 3, 1, on_scalar if True else on_vector)
             scatter(e - 1, 2)
             scatter(e - 1, 3)
             if e % PAIR == 1:
@@ -320,16 +315,16 @@ def tile_moe_adb_relu_kernel(tc, dy_words, dy_scales, wt, wbt, wat, a, gate, off
             quantise_part(("wat", e), 0, 2)
             second_product(e, 0, 2)
             quantise_part(("wat", e), 2, 1)
-            if e % PAIR == 1:
-                quantise_part(("wat", e), 3, 1)
-                second_product(e, 2, 2)
+            quantise_part(("wat", e), 3, 1)
+            second_product(e, 2, 2)
         e = LAST - 1
         send_back_singly(e - 1, 0)
-        round_dealt(e)
-        make_factor(e)
+        round_dealt(e, 0, on_vector)
+        round_dealt(e, 2, on_vector)
         quantise_part(("wbt", e), 0, 2)
         quantise_part(("wbt", e), 2, 2)
         first_product(e)
+        make_factor(e)
         make_factor(LAST)
         round_part(("wat", e), 0, 1, on_vector)
         leave_psum(e - 1, 2, 2, on_scalar)
@@ -341,8 +336,8 @@ def tile_moe_adb_relu_kernel(tc, dy_words, dy_scales, wt, wbt, wat, a, gate, off
         quantise_dh(e)
         quantise_part(("wat", e), 1, 1)
         second_product(e, 0, 2)
-        round_dealt(LAST)
-        round_part(("wat", e), 2, 1, on_vector)
+        round_dealt(LAST, 0, on_vector)
+        round_dealt(LAST, 2, on_vector)
         quantise_part(("wbt", LAST), 0, 2)
         leave_psum(e, 0, 2, on_scalar)
         round_part(("wat", e), 3, 1, on_scalar)
@@ -350,8 +345,9 @@ def tile_moe_adb_relu_kernel(tc, dy_words, dy_scales, wt, wbt, wat, a, gate, off
         scatter(e, 1)
         quantise_part(("wbt", LAST), 2, 2)
         first_product(LAST)
-        quantise_part(("wat", e), 2, 1)
+        round_part(("wat", e), 2, 1, on_vector)
         quantise_part(("wat", e), 3, 1)
+        quantise_part(("wat", e), 2, 1)
         second_product(e, 2, 2)
         round_part(("wat", LAST), 0, 1, on_vector)
         make_dh(LAST)
@@ -390,7 +386,9 @@ def tile_moe_adb_relu_kernel(tc, dy_words, dy_scales, wt, wbt, wat, a, gate, off
         leave_psum(LAST, 2, 2, on_vector)
         scatter(LAST, 2)
         scatter(LAST, 3)
-        for kt in range(TILES - 1):
+        finish_piece(0, 0, BANK)
+        finish_piece(0, BANK, T - BANK)
+        for kt in range(1, TILES - 1):
             finish_whole(kt)
         finish_piece(TILES - 1, 0, BANK)
         finish_piece(TILES - 1, BANK, T - BANK)

@@ -28,7 +28,7 @@ BANK = 512
 BANKS = 8
 PAIR = 2
 STAGED_BUFS = 28
-PLANE_BUFS = 36
+PLANE_BUFS = 44
 LAST = E - 1
 
 
@@ -51,7 +51,7 @@ def tile_moe_adb_relu_kernel(tc, dy_words, dy_scales, wt, wbt, wat, a, gate, off
             return ring.tile(shape, dtype, name=name, tag="staged", bufs=STAGED_BUFS, align_bytes=AXI)
 
         def bank(shape, name):
-            return psum.tile(shape, F32, name=name, tag="bank")
+            return psum.tile(shape, F32, name=name, tag="bank", bufs=BANKS - 2)
 
         raw = {}
         saved = {}
@@ -84,16 +84,18 @@ def tile_moe_adb_relu_kernel(tc, dy_words, dy_scales, wt, wbt, wat, a, gate, off
         load_part(("wat", 1), 0, 4)
         load_part(("wbt", 2), 0, 4)
         load_saved(2, 2)
-        load_part(("wat", 2), 0, 4)
+        load_part(("wat", 2), 0, 2)
+        load_part(("wat", 2), 2, 2)
         load_part(("wbt", 3), 0, 4)
         load_part(("wat", 3), 0, 4)
         load_part(("wbt", 4), 0, 4)
-        load_saved(4, 2)
+        load_saved(4, 1)
         load_part(("wat", 4), 0, 2)
         load_part(("wbt", 5), 0, 4)
         load_part(("wat", 4), 2, 2)
-        load_part(("wat", 5), 0, 2)
+        load_saved(5, 1)
         load_part(("wt", 0), 0, 2)
+        load_part(("wat", 5), 0, 2)
         load_part(("wat", 5), 2, 2)
         load_part(("wt", 0), 2, 2)
 
@@ -107,7 +109,7 @@ def tile_moe_adb_relu_kernel(tc, dy_words, dy_scales, wt, wbt, wat, a, gate, off
             nc.tensor.transpose(turned[:], gate_rows[:], identity[:])
             nc.scalar.copy(gate_cols[:], turned[:, 0:E])
             for first in range(0, E, BANK // C):
-                wide = bank([P, min(BANK // C, E - first), C], "wide")
+                wide = psum.tile([P, min(BANK // C, E - first), C], F32, name="wide", tag="wide", bufs=2)
                 for e in range(first, min(first + BANK // C, E)):
                     gate_wide[e] = wide[:, e - first, :]
                     nc.tensor.transpose(gate_wide[e], gate_cols[:, e : e + 1].to_broadcast([P, P]), identity[:])
@@ -134,18 +136,35 @@ def tile_moe_adb_relu_kernel(tc, dy_words, dy_scales, wt, wbt, wat, a, gate, off
         codes = {}
         planes = {}
 
-        def round_part(matrix, first, count, engine):
-            rounded[matrix, first] = staged([P, count, P, PACK], BF16, "rounded")
-            written = rounded[matrix, first][:].rearrange("p s m r -> p (s m) r")
-            engine(*by_lines(written, raw[matrix, first][:, :, 0 : count * P]))
+        def on_gpsimd(written, read):
+            nc.gpsimd.tensor_scalar(written, read, 1.0, 0.0, ALU.mult, ALU.add)
 
-        def round_dealt(e, first, engine):
-            rounded[("wbt", e), first] = staged([P, 2, P, PACK], BF16, "rounded")
+        def relay(shape, dtype):
+            return ring.tile(shape, dtype, name="relay", tag="relay", bufs=1, align_bytes=AXI)
+
+        def round_part(matrix, first, count, engine, relayed=False):
+            shape = [P, count, P, PACK]
+            rounded[matrix, first] = relay(shape, BF16) if relayed else staged(shape, BF16, "rounded")
+            written = rounded[matrix, first][:].rearrange("p s m r -> p (s m) r")
+            read = raw[matrix, first][:, :, 0 : count * P]
+            if engine is on_gpsimd:
+                engine(written, read.rearrange("p r c -> p c r"))
+            else:
+                engine(*by_lines(written, read))
+
+        def round_behind(matrix, st, spent):
+            rounded[matrix, st] = rounded[spent][:, 0:1]
+            written = rounded[matrix, st].rearrange("p s m r -> p (s m) r")
+            on_gpsimd(written, raw[matrix, st][:, :, 0:P].rearrange("p r c -> p c r"))
+
+        def round_dealt(e, first, engine, relayed=False):
+            shape = [P, 2, P, PACK]
+            rounded[("wbt", e), first] = relay(shape, BF16) if relayed else staged(shape, BF16, "rounded")
             read = raw[("wbt", e), 0].rearrange("p r (m s) -> p m r s", s=TILES)[:, :, :, first : first + 2]
             engine(rounded[("wbt", e), first][:].rearrange("p s m r -> p m r s"), read)
 
-        def quantise_part(matrix, first, count):
-            packed = staged([P, count * P], U32, "codes")
+        def quantise_part(matrix, first, count, relayed=False):
+            packed = relay([P, count * P], U32) if relayed else staged([P, count * P], U32, "codes")
             plane = ring.tile([P, count * P], U8, name="plane", tag="plane", bufs=PLANE_BUFS, align_bytes=64)
             nc.vector.quantize_mx(
                 out=packed[:].bitcast(FP8X4),
@@ -155,6 +174,17 @@ def tile_moe_adb_relu_kernel(tc, dy_words, dy_scales, wt, wbt, wat, a, gate, off
             for place in range(count):
                 codes[matrix, first + place] = packed[:, place * P : (place + 1) * P]
                 planes[matrix, first + place] = plane[:, place * P : (place + 1) * P]
+
+        def quantise_one(matrix, first, place):
+            packed = staged([P, P], U32, "codes")
+            plane = ring.tile([P, P], U8, name="plane", tag="plane", bufs=PLANE_BUFS, align_bytes=64)
+            nc.vector.quantize_mx(
+                out=packed[:].bitcast(FP8X4),
+                scales=plane[:],
+                in_=rounded[matrix, first][:, place].rearrange("p m r -> p (m r)"),
+            )
+            codes[matrix, first + place] = packed[:]
+            planes[matrix, first + place] = plane[:]
 
         def multiply(sums, matrix, st, moving, moving_scales):
             nc.tensor.matmul_mx(
@@ -245,6 +275,10 @@ def tile_moe_adb_relu_kernel(tc, dy_words, dy_scales, wt, wbt, wat, a, gate, off
                 base[first + place, 1] = both[:, place, :]
                 multiply(both[:, place, :], ("wt", 0), first + place, words[:, tokens[1]], scales[:, tokens[1]])
 
+        def frozen_short_alone(kt):
+            base[kt, 1] = bank([P, T - BANK], "short")[:]
+            multiply(base[kt, 1], ("wt", 0), kt, words[:, tokens[1]], scales[:, tokens[1]])
+
         def add(kt, result, first, count):
             n = first // BANK
             sums_of_piece = base[kt, n][:, first - n * BANK : first - n * BANK + count]
@@ -267,6 +301,9 @@ def tile_moe_adb_relu_kernel(tc, dy_words, dy_scales, wt, wbt, wat, a, gate, off
             quantise_part(matrix, first, 1)
             quantise_part(matrix, first + 1, 1)
 
+        V, S, G = on_vector, on_scalar, on_gpsimd
+        R, Q = round_part, quantise_part
+        W = ("wt", 0)
         gather(words[:].bitcast(U32), U32, slot_words, 0, PAIR)
         gather(words[:].bitcast(U32), U32, slot_words, PAIR, E - PAIR)
         round_dealt(0, 2, on_scalar)
@@ -289,106 +326,118 @@ def tile_moe_adb_relu_kernel(tc, dy_words, dy_scales, wt, wbt, wat, a, gate, off
         second_product(0, 0, 2)
         quantise_part(("wat", 0), 2, 2)
         second_product(0, 2, 2)
-        for e in range(1, LAST - 1):
+        for e in range(1, 4):
             send_back_singly(e - 1, 0)
-            round_dealt(e, 0, on_vector)
-            round_dealt(e, 2, on_vector)
-            quantise_part(("wbt", e), 0, 2)
-            quantise_part(("wbt", e), 2, 2)
+            round_dealt(e, 0, V)
+            round_dealt(e, 2, V)
+            Q(("wbt", e), 0, 2)
+            Q(("wbt", e), 2, 2)
             first_product(e)
-            if e % PAIR == 0:
+            if e == 2:
+                round_behind(("wat", e), 1, (("wbt", e), 2))
                 make_factor(e)
                 make_factor(e + 1)
                 make_dh(e)
-                round_part(("wat", e), 0, 2, on_vector)
+                R(("wat", e), 0, 1, V)
                 quantise_dh(e)
+                R(("wat", e), 2, 1, V)
+                leave_psum(e - 1, 2, 2, S)
+                R(("wat", e), 3, 1, S)
+                scatter(e - 1, 2)
+                scatter(e - 1, 3)
+                Q(("wat", e), 0, 1)
+                Q(("wat", e), 1, 1)
             else:
-                round_part(("wat", e), 0, 2, on_vector)
+                R(("wat", e), 0, 2, V)
                 make_dh(e)
-            round_part(("wat", e), 2, 1, on_vector)
-            leave_psum(e - 1, 2, 2, on_scalar)
-            round_part(("wat", e), 3, 1, on_scalar if True else on_vector)
-            scatter(e - 1, 2)
-            scatter(e - 1, 3)
-            if e % PAIR == 1:
+                R(("wat", e), 2, 1, V)
+                leave_psum(e - 1, 2, 2, S)
+                R(("wat", e), 3, 1, S)
+                scatter(e - 1, 2)
+                scatter(e - 1, 3)
                 quantise_dh(e)
-            quantise_part(("wat", e), 0, 2)
+                Q(("wat", e), 0, 2)
             second_product(e, 0, 2)
-            quantise_part(("wat", e), 2, 1)
-            quantise_part(("wat", e), 3, 1)
+            Q(("wat", e), 2, 1)
+            Q(("wat", e), 3, 1)
             second_product(e, 2, 2)
-        e = LAST - 1
-        send_back_singly(e - 1, 0)
-        round_dealt(e, 0, on_vector)
-        round_dealt(e, 2, on_vector)
-        quantise_part(("wbt", e), 0, 2)
-        quantise_part(("wbt", e), 2, 2)
-        first_product(e)
-        make_factor(e)
-        make_factor(LAST)
-        round_part(("wat", e), 0, 1, on_vector)
-        leave_psum(e - 1, 2, 2, on_scalar)
-        round_part(("wat", e), 1, 1, on_scalar)
-        scatter(e - 1, 2)
-        scatter(e - 1, 3)
-        make_dh(e)
-        quantise_part(("wat", e), 0, 1)
-        quantise_dh(e)
-        quantise_part(("wat", e), 1, 1)
-        second_product(e, 0, 2)
-        round_dealt(LAST, 0, on_vector)
-        round_dealt(LAST, 2, on_vector)
-        quantise_part(("wbt", LAST), 0, 2)
-        leave_psum(e, 0, 2, on_scalar)
-        round_part(("wat", e), 3, 1, on_scalar)
-        scatter(e, 0)
-        scatter(e, 1)
-        quantise_part(("wbt", LAST), 2, 2)
-        first_product(LAST)
-        round_part(("wat", e), 2, 1, on_vector)
-        quantise_part(("wat", e), 3, 1)
-        quantise_part(("wat", e), 2, 1)
-        second_product(e, 2, 2)
-        round_part(("wat", LAST), 0, 1, on_vector)
-        make_dh(LAST)
-        round_part(("wat", LAST), 1, 1, on_vector)
-        quantise_dh(LAST)
-        quantise_part(("wat", LAST), 0, 1)
-        quantise_part(("wat", LAST), 1, 1)
-        second_product(LAST, 0, 2)
-        leave_psum(e, 2, 1, on_scalar)
-        leave_psum(e, 3, 1, on_scalar)
-        scatter(e, 2)
-        scatter(e, 3)
-        round_part(("wt", 0), 0, 1, on_vector)
-        round_part(("wt", 0), 1, 1, on_vector)
-        quantise_part(("wt", 0), 0, 1)
+        send_back_singly(3, 0)
+        round_dealt(4, 0, V)
+        round_dealt(4, 2, V)
+        Q(("wbt", 4), 0, 2)
+        Q(("wbt", 4), 2, 2)
+        first_product(4)
+        round_behind(("wat", 4), 1, (("wbt", 4), 2))
+        make_factor(4)
+        R(("wat", 4), 0, 1, S)
+        leave_psum(3, 2, 2, V)
+        scatter(3, 2)
+        scatter(3, 3)
+        make_dh(4)
+        Q(("wat", 4), 1, 1)
+        quantise_dh(4)
+        second_product(4, 1, 1)
+        Q(("wat", 4), 0, 1)
+        second_product(4, 0, 1)
+        round_dealt(5, 0, V)
+        round_dealt(5, 2, V)
+        Q(("wbt", 5), 0, 2)
+        leave_psum(4, 1, 1, S)
+        leave_psum(4, 0, 1, S)
+        R(("wat", 4), 3, 1, S)
+        scatter(4, 1)
+        scatter(4, 0)
+        R(("wat", 4), 2, 1, V)
+        Q(("wbt", 5), 2, 2)
+        first_product(5)
+        Q(("wat", 4), 3, 1)
+        Q(("wat", 4), 2, 1)
+        second_product(4, 2, 2)
+        make_factor(5)
+        R(W, 0, 1, V)
+        make_dh(5)
+        leave_psum(4, 2, 1, S)
+        leave_psum(4, 3, 1, S)
+        scatter(4, 2)
+        scatter(4, 3)
+        R(("wat", 5), 0, 1, V)
+        quantise_dh(5)
+        R(("wat", 5), 1, 1, V)
+        Q(("wat", 5), 0, 1)
+        second_product(5, 0, 1)
+        Q(W, 0, 1)
+        Q(("wat", 5), 1, 1)
+        second_product(5, 1, 1)
         frozen_long(0)
-        round_part(("wat", LAST), 2, 1, on_vector)
-        quantise_part(("wt", 0), 1, 1)
+        R(W, 1, 1, V)
+        leave_psum(5, 0, 1, S)
+        leave_psum(5, 1, 1, S)
+        scatter(5, 0)
+        scatter(5, 1)
+        R(("wat", 5), 2, 1, V)
+        Q(W, 1, 1)
         frozen_short(0)
-        leave_psum(LAST, 0, 1, on_scalar)
-        leave_psum(LAST, 1, 1, on_scalar)
-        scatter(LAST, 0)
-        scatter(LAST, 1)
-        round_part(("wat", LAST), 3, 1, on_vector)
-        quantise_part(("wat", LAST), 2, 1)
-        round_part(("wt", 0), 2, 1, on_vector)
-        quantise_part(("wat", LAST), 3, 1)
-        second_product(LAST, 2, 2)
+        R(("wat", 5), 3, 1, V)
+        Q(("wat", 5), 2, 1)
+        second_product(5, 2, 1)
+        R(W, 2, 1, V)
+        Q(("wat", 5), 3, 1)
+        second_product(5, 3, 1)
         frozen_long(1)
-        round_part(("wt", 0), 3, 1, on_vector)
-        quantise_part(("wt", 0), 2, 1)
+        Q(W, 2, 1)
         frozen_long(2)
-        quantise_part(("wt", 0), 3, 1)
-        frozen_short(2)
-        frozen_long(3)
-        leave_psum(LAST, 2, 2, on_vector)
-        scatter(LAST, 2)
-        scatter(LAST, 3)
+        round_behind(W, 3, (W, 2))
         finish_piece(0, 0, BANK)
         finish_piece(0, BANK, T - BANK)
-        for kt in range(1, TILES - 1):
-            finish_whole(kt)
-        finish_piece(TILES - 1, 0, BANK)
-        finish_piece(TILES - 1, BANK, T - BANK)
+        frozen_short_alone(2)
+        leave_psum(5, 2, 1, S)
+        leave_psum(5, 3, 1, S)
+        scatter(5, 2)
+        scatter(5, 3)
+        finish_whole(1)
+        Q(W, 3, 1)
+        frozen_long(3)
+        frozen_short_alone(3)
+        finish_whole(2)
+        finish_piece(3, 0, BANK)
+        finish_piece(3, BANK, T - BANK)

@@ -84,18 +84,16 @@ def tile_moe_adb_relu_kernel(tc, dy_words, dy_scales, wt, wbt, wat, a, gate, off
         load_part(("wat", 1), 0, 4)
         load_part(("wbt", 2), 0, 4)
         load_saved(2, 2)
-        load_part(("wat", 2), 0, 2)
-        load_part(("wat", 2), 2, 2)
+        load_part(("wat", 2), 0, 4)
         load_part(("wbt", 3), 0, 4)
         load_part(("wat", 3), 0, 4)
         load_part(("wbt", 4), 0, 4)
-        load_saved(4, 1)
+        load_saved(4, 2)
         load_part(("wat", 4), 0, 2)
         load_part(("wbt", 5), 0, 4)
         load_part(("wat", 4), 2, 2)
-        load_saved(5, 1)
-        load_part(("wt", 0), 0, 2)
         load_part(("wat", 5), 0, 2)
+        load_part(("wt", 0), 0, 2)
         load_part(("wat", 5), 2, 2)
         load_part(("wt", 0), 2, 2)
 
@@ -326,56 +324,84 @@ def tile_moe_adb_relu_kernel(tc, dy_words, dy_scales, wt, wbt, wat, a, gate, off
         second_product(0, 0, 2)
         quantise_part(("wat", 0), 2, 2)
         second_product(0, 2, 2)
-        for e in range(1, 4):
-            send_back_singly(e - 1, 0)
-            round_dealt(e, 0, V)
-            round_dealt(e, 2, V)
-            Q(("wbt", e), 0, 2)
-            Q(("wbt", e), 2, 2)
-            first_product(e)
-            if e == 2:
-                round_behind(("wat", e), 1, (("wbt", e), 2))
-                make_factor(e)
-                make_factor(e + 1)
-                make_dh(e)
-                R(("wat", e), 0, 1, V)
-                quantise_dh(e)
-                R(("wat", e), 2, 1, V)
-                leave_psum(e - 1, 2, 2, S)
-                R(("wat", e), 3, 1, S)
-                scatter(e - 1, 2)
-                scatter(e - 1, 3)
-                Q(("wat", e), 0, 1)
-                Q(("wat", e), 1, 1)
-            else:
-                R(("wat", e), 0, 2, V)
-                make_dh(e)
-                R(("wat", e), 2, 1, V)
-                leave_psum(e - 1, 2, 2, S)
-                R(("wat", e), 3, 1, S)
-                scatter(e - 1, 2)
-                scatter(e - 1, 3)
-                quantise_dh(e)
-                Q(("wat", e), 0, 2)
-            second_product(e, 0, 2)
-            Q(("wat", e), 2, 1)
-            Q(("wat", e), 3, 1)
-            second_product(e, 2, 2)
+        send_back_singly(0, 0)
+        round_dealt(1, 0, V)
+        round_dealt(1, 2, V)
+        Q(("wbt", 1), 0, 2)
+        Q(("wbt", 1), 2, 2)
+        first_product(1)
+        R(("wat", 1), 0, 2, V)
+        leave_psum(0, 2, 2, S)
+        R(("wat", 1), 3, 1, S)
+        scatter(0, 2)
+        scatter(0, 3)
+        R(("wat", 1), 2, 1, V)
+        Q(("wat", 1), 0, 2)
+        make_dh(1)
+        Q(("wat", 1), 2, 1)
+        quantise_dh(1)
+        second_product(1, 0, 2)
+        send_back_singly(1, 0)
+        round_dealt(2, 0, V)
+        Q(("wat", 1), 3, 1)
+        second_product(1, 2, 2)
+        round_dealt(2, 2, V)
+        Q(("wbt", 2), 0, 2)
+        Q(("wbt", 2), 2, 2)
+        first_product(2)
+        make_factor(2)
+        make_factor(3)
+        make_dh(2)
+        R(("wat", 2), 0, 1, V)
+        quantise_dh(2)
+        R(("wat", 2), 1, 1, V)
+        leave_psum(1, 2, 2, S)
+        R(("wat", 2), 3, 1, S)
+        scatter(1, 2)
+        scatter(1, 3)
+        Q(("wat", 2), 0, 1)
+        R(("wat", 2), 2, 1, V)
+        Q(("wat", 2), 1, 1)
+        second_product(2, 0, 2)
+        Q(("wat", 2), 3, 1)
+        Q(("wat", 2), 2, 1)
+        second_product(2, 2, 2)
+        send_back_singly(2, 0)
+        round_dealt(3, 0, V)
+        round_dealt(3, 2, V)
+        Q(("wbt", 3), 0, 2)
+        Q(("wbt", 3), 2, 2)
+        first_product(3)
+        R(("wat", 3), 0, 2, V)
+        leave_psum(2, 2, 2, S)
+        R(("wat", 3), 3, 1, S)
+        scatter(2, 2)
+        scatter(2, 3)
+        R(("wat", 3), 2, 1, V)
+        Q(("wat", 3), 0, 2)
+        make_dh(3)
+        Q(("wat", 3), 2, 1)
+        quantise_dh(3)
+        second_product(3, 0, 2)
         send_back_singly(3, 0)
         round_dealt(4, 0, V)
+        Q(("wat", 3), 3, 1)
+        second_product(3, 2, 2)
         round_dealt(4, 2, V)
         Q(("wbt", 4), 0, 2)
         Q(("wbt", 4), 2, 2)
         first_product(4)
         round_behind(("wat", 4), 1, (("wbt", 4), 2))
         make_factor(4)
-        R(("wat", 4), 0, 1, S)
-        leave_psum(3, 2, 2, V)
+        make_factor(5)
+        leave_psum(3, 2, 1, S)
+        leave_psum(3, 3, 1, S)
         scatter(3, 2)
         scatter(3, 3)
         make_dh(4)
-        Q(("wat", 4), 1, 1)
+        R(("wat", 4), 0, 1, V)
         quantise_dh(4)
+        Q(("wat", 4), 1, 1)
         second_product(4, 1, 1)
         Q(("wat", 4), 0, 1)
         second_product(4, 0, 1)
@@ -390,54 +416,47 @@ def tile_moe_adb_relu_kernel(tc, dy_words, dy_scales, wt, wbt, wat, a, gate, off
         R(("wat", 4), 2, 1, V)
         Q(("wbt", 5), 2, 2)
         first_product(5)
-        Q(("wat", 4), 3, 1)
         Q(("wat", 4), 2, 1)
+        R(("wat", 5), 0, 1, V)
+        Q(("wat", 4), 3, 1)
         second_product(4, 2, 2)
-        make_factor(5)
-        R(W, 0, 1, V)
+        R(("wat", 5), 1, 1, V)
+        Q(("wat", 5), 0, 1)
         make_dh(5)
+        Q(("wat", 5), 1, 1)
+        quantise_dh(5)
+        second_product(5, 0, 2)
         leave_psum(4, 2, 1, S)
         leave_psum(4, 3, 1, S)
         scatter(4, 2)
         scatter(4, 3)
-        R(("wat", 5), 0, 1, V)
-        quantise_dh(5)
-        R(("wat", 5), 1, 1, V)
-        Q(("wat", 5), 0, 1)
-        second_product(5, 0, 1)
+        R(W, 0, 1, V)
+        R(("wat", 5), 2, 2, V)
         Q(W, 0, 1)
-        Q(("wat", 5), 1, 1)
-        second_product(5, 1, 1)
         frozen_long(0)
         R(W, 1, 1, V)
+        Q(("wat", 5), 2, 2)
+        second_product(5, 2, 2)
         leave_psum(5, 0, 1, S)
         leave_psum(5, 1, 1, S)
         scatter(5, 0)
         scatter(5, 1)
-        R(("wat", 5), 2, 1, V)
         Q(W, 1, 1)
         frozen_short(0)
-        R(("wat", 5), 3, 1, V)
-        Q(("wat", 5), 2, 1)
-        second_product(5, 2, 1)
-        R(W, 2, 1, V)
-        Q(("wat", 5), 3, 1)
-        second_product(5, 3, 1)
         frozen_long(1)
+        R(W, 2, 1, V)
+        R(W, 3, 1, V)
         Q(W, 2, 1)
         frozen_long(2)
-        round_behind(W, 3, (W, 2))
-        finish_piece(0, 0, BANK)
-        finish_piece(0, BANK, T - BANK)
-        frozen_short_alone(2)
-        leave_psum(5, 2, 1, S)
-        leave_psum(5, 3, 1, S)
+        leave_psum(5, 2, 2, V)
         scatter(5, 2)
         scatter(5, 3)
-        finish_whole(1)
         Q(W, 3, 1)
+        frozen_short(2)
         frozen_long(3)
-        frozen_short_alone(3)
+        finish_piece(0, 0, BANK)
+        finish_piece(0, BANK, T - BANK)
+        finish_whole(1)
         finish_whole(2)
         finish_piece(3, 0, BANK)
         finish_piece(3, BANK, T - BANK)

@@ -383,10 +383,10 @@ def tile_moe_adb_relu_kernel(tc, dy_words, dy_scales, wt, wbt, wat, a, gate, off
         Q(("wat", 3), 2, 1)
         quantise_dh(3)
         second_product(3, 0, 2)
-        send_back_singly(3, 0)
-        round_dealt(4, 0, V)
         Q(("wat", 3), 3, 1)
         second_product(3, 2, 2)
+        send_back_singly(3, 0)
+        round_dealt(4, 0, V)
         round_dealt(4, 2, V)
         Q(("wbt", 4), 0, 2)
         Q(("wbt", 4), 2, 2)
@@ -417,9 +417,10 @@ def tile_moe_adb_relu_kernel(tc, dy_words, dy_scales, wt, wbt, wat, a, gate, off
         Q(("wbt", 5), 2, 2)
         first_product(5)
         Q(("wat", 4), 2, 1)
+        second_product(4, 2, 1)
         R(("wat", 5), 0, 1, V)
         Q(("wat", 4), 3, 1)
-        second_product(4, 2, 2)
+        second_product(4, 3, 1)
         R(("wat", 5), 1, 1, V)
         Q(("wat", 5), 0, 1)
         make_dh(5)
@@ -431,29 +432,33 @@ def tile_moe_adb_relu_kernel(tc, dy_words, dy_scales, wt, wbt, wat, a, gate, off
         scatter(4, 2)
         scatter(4, 3)
         R(W, 0, 1, V)
-        R(("wat", 5), 2, 2, V)
+        R(W, 1, 1, V)
         Q(W, 0, 1)
         frozen_long(0)
-        R(W, 1, 1, V)
-        Q(("wat", 5), 2, 2)
-        second_product(5, 2, 2)
+        R(("wat", 5), 2, 1, V)
+        R(("wat", 5), 3, 1, V)
         leave_psum(5, 0, 1, S)
         leave_psum(5, 1, 1, S)
         scatter(5, 0)
         scatter(5, 1)
+        Q(("wat", 5), 2, 1)
+        second_product(5, 2, 1)
         Q(W, 1, 1)
+        Q(("wat", 5), 3, 1)
+        second_product(5, 3, 1)
         frozen_short(0)
         frozen_long(1)
         R(W, 2, 1, V)
         R(W, 3, 1, V)
         Q(W, 2, 1)
         frozen_long(2)
-        leave_psum(5, 2, 2, V)
-        scatter(5, 2)
-        scatter(5, 3)
         Q(W, 3, 1)
         frozen_short(2)
         frozen_long(3)
+        leave_psum(5, 2, 1, V)
+        scatter(5, 2)
+        leave_psum(5, 3, 1, V)
+        scatter(5, 3)
         finish_piece(0, 0, BANK)
         finish_piece(0, BANK, T - BANK)
         finish_whole(1)

@@ -418,20 +418,21 @@ def tile_moe_adb_relu_kernel(tc, dy_words, dy_scales, wt, wbt, wat, a, gate, off
         first_product(5)
         Q(("wat", 4), 2, 1)
         second_product(4, 2, 1)
-        R(("wat", 5), 0, 1, V)
         Q(("wat", 4), 3, 1)
         second_product(4, 3, 1)
+        R(("wat", 5), 0, 1, V)
         R(("wat", 5), 1, 1, V)
         Q(("wat", 5), 0, 1)
-        make_dh(5)
         Q(("wat", 5), 1, 1)
+        make_dh(5)
+        R(W, 0, 1, V)
         quantise_dh(5)
-        second_product(5, 0, 2)
+        second_product(5, 0, 1)
+        second_product(5, 1, 1)
         leave_psum(4, 2, 1, S)
         leave_psum(4, 3, 1, S)
         scatter(4, 2)
         scatter(4, 3)
-        R(W, 0, 1, V)
         R(W, 1, 1, V)
         Q(W, 0, 1)
         frozen_long(0)
@@ -452,11 +453,11 @@ def tile_moe_adb_relu_kernel(tc, dy_words, dy_scales, wt, wbt, wat, a, gate, off
         R(W, 3, 1, V)
         Q(W, 2, 1)
         frozen_long(2)
+        leave_psum(5, 2, 1, V)
+        scatter(5, 2)
         Q(W, 3, 1)
         frozen_short(2)
         frozen_long(3)
-        leave_psum(5, 2, 1, V)
-        scatter(5, 2)
         leave_psum(5, 3, 1, V)
         scatter(5, 3)
         finish_piece(0, 0, BANK)

from contextlib import ExitStack

import concourse.mybir as mybir
from concourse.masks import make_identity

K, T, E, C, H, N = 512, 768, 6, 128, 512, 512
FLOPS = 2 * T * (N * K + N * H + H * K)

F32 = mybir.dt.float32
BF16 = mybir.dt.bfloat16
I32 = mybir.dt.int32
U32 = mybir.dt.uint32
U16 = mybir.dt.uint16
U8 = mybir.dt.uint8
FP8X4 = mybir.dt.float8_e4m3fn_x4
ALU = mybir.AluOpType
COPY = mybir.ActivationFunctionType.Copy

P = 128
PACK = 4
TILES = 4
RUN = 2
AXI = 256
QUADRANT = 32
SCALE_ROWS = 4
PER_COLUMN = 16
BANK = 512
BANKS = 8
PAIR = 2
STAGED_BUFS = 28
PLANE_BUFS = 44
LAST = E - 1


def tile_moe_adb_relu_kernel(tc, dy_words, dy_scales, wt, wbt, wat, a, gate, offs, out):
    nc = tc.nc
    with ExitStack() as ctx:
        keep = ctx.enter_context(tc.tile_pool(name="keep", bufs=1))
        ring = ctx.enter_context(tc.tile_pool(name="ring", bufs=2))
        psum = ctx.enter_context(tc.psum_pool(name="psum", bufs=BANKS))

        offsets = keep.tile([P, T // PER_COLUMN], U16, name="offsets")
        words = keep.tile([P, T], I32, name="words", align_bytes=AXI)
        scales = keep.tile([P, T], U8, name="scales", align_bytes=AXI)
        gate_rows = keep.tile([P, C], F32, name="gate_rows")
        gate_cols = keep.tile([P, E], F32, name="gate_cols")
        identity = keep.tile([P, P], F32, name="identity")
        windows = [keep.tile([P, T], F32, name=f"window{kt}") for kt in range(TILES)]

        def staged(shape, dtype, name):
            return ring.tile(shape, dtype, name=name, tag="staged", bufs=STAGED_BUFS, align_bytes=AXI)

        def bank(shape, name):
            return psum.tile(shape, F32, name=name, tag="bank", bufs=BANKS - 2)

        raw = {}
        saved = {}

        def load_part(matrix, first, count):
            source = {"wbt": wbt[matrix[1]], "wat": wat[matrix[1]], "wt": wt}[matrix[0]]
            part = keep.tile([P, PACK, count * P], F32, name=f"{matrix[0]}{matrix[1]}_{first}", align_bytes=AXI)
            cols = slice(first * P, (first + count) * P)
            nc.sync.dma_start(part[:], source[:, cols].rearrange("(p r) c -> p r c", r=PACK))
            for place in range(count):
                raw[matrix, first + place] = part[:, :, place * P : count * P]

        def load_saved(first, count):
            part = keep.tile([P, PACK, count * C], F32, name=f"saved{first}", align_bytes=AXI)
            nc.sync.dma_start(part[:], a[:, first * C : (first + count) * C].rearrange("(p r) s -> p r s", r=PACK))
            for place in range(count):
                saved[first + place] = part[:, :, place * C : (place + 1) * C]

        nc.gpsimd.memset(scales[:].bitcast(I32), 0)
        nc.gpsimd.memset(gate_rows[:], 0.0)
        nc.sync.dma_start(words[:], dy_words[0].rearrange("p t r -> p (t r)").bitcast(I32))
        nc.sync.dma_start(offsets[:], offs)
        load_part(("wbt", 0), 0, TILES)
        for row in range(SCALE_ROWS):
            nc.sync.dma_start(scales[row:P:QUADRANT, :].bitcast(I32), dy_scales[0, row::SCALE_ROWS, :].bitcast(I32))
        nc.sync.dma_start(gate_rows[0:E, :], gate[0].rearrange("(e u) -> e u", u=C))
        load_saved(0, 2)
        load_part(("wat", 0), 0, 4)
        load_part(("wbt", 1), 0, 4)
        load_part(("wat", 1), 0, 4)
        load_part(("wbt", 2), 0, 4)
        load_saved(2, 2)
        load_part(("wat", 2), 0, 4)
        load_part(("wbt", 3), 0, 4)
        load_part(("wat", 3), 0, 4)
        load_part(("wbt", 4), 0, 4)
        load_saved(4, 2)
        load_part(("wat", 4), 0, 2)
        load_part(("wbt", 5), 0, 4)
        load_part(("wat", 4), 2, 2)
        load_part(("wat", 5), 0, 2)
        load_part(("wt", 0), 0, 2)
        load_part(("wat", 5), 2, 2)
        load_part(("wt", 0), 2, 2)

        on_vector = nc.vector.tensor_copy
        on_scalar = nc.scalar.copy
        gate_wide = {}

        def spread_gate():
            make_identity(nc, identity[:])
            turned = bank([P, P], "turned")
            nc.tensor.transpose(turned[:], gate_rows[:], identity[:])
            nc.scalar.copy(gate_cols[:], turned[:, 0:E])
            for first in range(0, E, BANK // C):
                wide = psum.tile([P, min(BANK // C, E - first), C], F32, name="wide", tag="wide", bufs=2)
                for e in range(first, min(first + BANK // C, E)):
                    gate_wide[e] = wide[:, e - first, :]
                    nc.tensor.transpose(gate_wide[e], gate_cols[:, e : e + 1].to_broadcast([P, P]), identity[:])

        slot_words = {}
        slot_scales = {}

        def entries(first, count):
            return offsets[:, first * C // PER_COLUMN : (first + count) * C // PER_COLUMN]

        def gather(table, dtype, gathered, first, count):
            part = staged([P, count * C], dtype, "gathered")
            nc.vector.tensor_copy(part[:], table.indirect(entries(first, count)))
            for place in range(count):
                gathered[first + place] = part[:, place * C : (place + 1) * C]

        def by_lines(written, read):
            return (
                written.rearrange("p (c i) r -> p c r i", i=RUN),
                read.rearrange("p r (c i) -> p c r i", i=RUN),
            )

        rounded = {}
        codes = {}
        planes = {}

        def on_gpsimd(written, read):
            nc.gpsimd.tensor_scalar(written, read, 1.0, 0.0, ALU.mult, ALU.add)

        def relay(shape, dtype):
            return ring.tile(shape, dtype, name="relay", tag="relay", bufs=1, align_bytes=AXI)

        def round_part(matrix, first, count, engine, relayed=False):
            shape = [P, count, P, PACK]
            rounded[matrix, first] = relay(shape, BF16) if relayed else staged(shape, BF16, "rounded")
            written = rounded[matrix, first][:].rearrange("p s m r -> p (s m) r")
            read = raw[matrix, first][:, :, 0 : count * P]
            if engine is on_gpsimd:
                engine(written, read.rearrange("p r c -> p c r"))
            else:
                engine(*by_lines(written, read))

        def round_behind(matrix, st, spent):
            rounded[matrix, st] = rounded[spent][:, 0:1]
            written = rounded[matrix, st].rearrange("p s m r -> p (s m) r")
            on_gpsimd(written, raw[matrix, st][:, :, 0:P].rearrange("p r c -> p c r"))

        def round_dealt(e, first, engine, relayed=False):
            shape = [P, 2, P, PACK]
            rounded[("wbt", e), first] = relay(shape, BF16) if relayed else staged(shape, BF16, "rounded")
            read = raw[("wbt", e), 0].rearrange("p r (m s) -> p m r s", s=TILES)[:, :, :, first : first + 2]
            engine(rounded[("wbt", e), first][:].rearrange("p s m r -> p m r s"), read)

        def quantise_part(matrix, first, count, relayed=False):
            packed = relay([P, count * P], U32) if relayed else staged([P, count * P], U32, "codes")
            plane = ring.tile([P, count * P], U8, name="plane", tag="plane", bufs=PLANE_BUFS, align_bytes=64)
            nc.vector.quantize_mx(
                out=packed[:].bitcast(FP8X4),
                scales=plane[:],
                in_=rounded[matrix, first][:].rearrange("p s m r -> p (s m r)"),
            )
            for place in range(count):
                codes[matrix, first + place] = packed[:, place * P : (place + 1) * P]
                planes[matrix, first + place] = plane[:, place * P : (place + 1) * P]

        def quantise_one(matrix, first, place):
            packed = staged([P, P], U32, "codes")
            plane = ring.tile([P, P], U8, name="plane", tag="plane", bufs=PLANE_BUFS, align_bytes=64)
            nc.vector.quantize_mx(
                out=packed[:].bitcast(FP8X4),
                scales=plane[:],
                in_=rounded[matrix, first][:, place].rearrange("p m r -> p (m r)"),
            )
            codes[matrix, first + place] = packed[:]
            planes[matrix, first + place] = plane[:]

        def multiply(sums, matrix, st, moving, moving_scales):
            nc.tensor.matmul_mx(
                out=sums,
                lhsT=codes[matrix, st].bitcast(FP8X4),
                lhsT_scale=planes[matrix, st],
                rhs=moving.bitcast(FP8X4),
                rhs_scale=moving_scales,
                start=True,
                stop=True,
            )

        sums = {}
        factor = {}
        dh = {}
        dh_codes = {}
        dh_planes = {}

        def first_product(e):
            sums[e] = bank([P, PACK, C], "sums")
            for r in range(PACK):
                multiply(sums[e][:, r, :], ("wbt", e), r, slot_words[e], slot_scales[e])

        def make_factor(e):
            factor[e] = staged([P, PACK, C], F32, "factor")
            spread = gate_wide[e].unsqueeze(1).to_broadcast([P, PACK, C])
            nc.vector.scalar_tensor_tensor(factor[e][:], saved[e], 0.0, spread, ALU.is_gt, ALU.mult)

        def make_dh(e):
            dh[e] = staged([P, C, PACK], BF16, "dh")
            written, read = by_lines(dh[e][:], sums[e][:])
            nc.vector.tensor_tensor(written, read, factor[e][:].rearrange("p r (c i) -> p c r i", i=RUN), ALU.mult)

        def quantise_dh(e):
            dh_codes[e] = staged([P, C], U32, "dh_codes")
            dh_planes[e] = ring.tile([P, C], U8, name="dh_planes", tag="dh_planes", bufs=E, align_bytes=64)
            nc.vector.quantize_mx(
                out=dh_codes[e][:].bitcast(FP8X4),
                scales=dh_planes[e][:],
                in_=dh[e][:].rearrange("p u r -> p (u r)"),
            )

        products = {}

        def second_product(e, first, count):
            product = bank([P, count, C], "product")
            for place in range(count):
                products[e, first + place] = (product, place)
                multiply(product[:, place, :], ("wat", e), first + place, dh_codes[e][:], dh_planes[e][:])

        dx = {}

        def leave_psum(e, first, count, engine):
            part = staged([P, count, C], F32, "dx")
            product, place = products[e, first]
            engine(part[:], product[:, place : place + count, :])
            for kt in range(first, first + count):
                dx[e, kt] = part[:, kt - first, :]

        def scatter(e, kt, by_vector=False):
            window = windows[kt][:].indirect(entries(e, 1))
            if by_vector:
                nc.vector.tensor_copy(window, dx[e, kt])
            else:
                nc.scalar.activation(window, dx[e, kt], COPY)

        def send_back(e, first, count):
            leave_psum(e, first, count, on_scalar)
            for kt in range(first, first + count):
                scatter(e, kt)

        def send_back_singly(e, first):
            leave_psum(e, first, 1, on_scalar)
            leave_psum(e, first + 1, 1, on_scalar)
            scatter(e, first)
            scatter(e, first + 1)

        tokens = (slice(0, BANK), slice(BANK, T))
        base = {}

        def frozen_long(kt):
            base[kt, 0] = bank([P, BANK], "long")[:]
            multiply(base[kt, 0], ("wt", 0), kt, words[:, tokens[0]], scales[:, tokens[0]])

        def frozen_short(first):
            both = bank([P, 2, T - BANK], "short")
            for place in range(2):
                base[first + place, 1] = both[:, place, :]
                multiply(both[:, place, :], ("wt", 0), first + place, words[:, tokens[1]], scales[:, tokens[1]])

        def frozen_short_alone(kt):
            base[kt, 1] = bank([P, T - BANK], "short")[:]
            multiply(base[kt, 1], ("wt", 0), kt, words[:, tokens[1]], scales[:, tokens[1]])

        def add(kt, result, first, count):
            n = first // BANK
            sums_of_piece = base[kt, n][:, first - n * BANK : first - n * BANK + count]
            nc.vector.tensor_tensor(result, sums_of_piece, windows[kt][:, first : first + count], ALU.add)

        def finish_whole(kt):
            result = staged([P, T], F32, "result")
            for cols in tokens:
                add(kt, result[:, cols], cols.start, cols.stop - cols.start)
            nc.sync.dma_start(out[kt * P : (kt + 1) * P, :], result[:])

        def finish_piece(kt, first, count):
            result = staged([P, count], F32, "result")
            add(kt, result[:], first, count)
            nc.sync.dma_start(out[kt * P : (kt + 1) * P, first : first + count], result[:])

        def prepare(matrix, first):
            round_part(matrix, first, 1, on_vector)
            round_part(matrix, first + 1, 1, on_vector)
            quantise_part(matrix, first, 1)
            quantise_part(matrix, first + 1, 1)

        V, S, G = on_vector, on_scalar, on_gpsimd
        R, Q = round_part, quantise_part
        W = ("wt", 0)
        gather(words[:].bitcast(U32), U32, slot_words, 0, PAIR)
        gather(words[:].bitcast(U32), U32, slot_words, PAIR, E - PAIR)
        round_dealt(0, 2, on_scalar)
        round_dealt(0, 0, on_vector)
        spread_gate()
        gather(scales[:], U8, slot_scales, 0, PAIR)
        quantise_part(("wbt", 0), 0, 2)
        quantise_part(("wbt", 0), 2, 2)
        first_product(0)
        gather(scales[:], U8, slot_scales, PAIR, E - PAIR)
        make_factor(0)
        make_factor(1)
        make_dh(0)
        round_part(("wat", 0), 2, 2, on_scalar)
        round_part(("wat", 0), 0, 1, on_vector)
        quantise_dh(0)
        round_part(("wat", 0), 1, 1, on_vector)
        quantise_part(("wat", 0), 0, 1)
        quantise_part(("wat", 0), 1, 1)
        second_product(0, 0, 2)
        quantise_part(("wat", 0), 2, 2)
        second_product(0, 2, 2)
        send_back_singly(0, 0)
        round_dealt(1, 0, V)
        round_dealt(1, 2, V)
        Q(("wbt", 1), 0, 2)
        Q(("wbt", 1), 2, 2)
        first_product(1)
        R(("wat", 1), 0, 2, V)
        leave_psum(0, 2, 2, S)
        R(("wat", 1), 3, 1, S)
        scatter(0, 2)
        scatter(0, 3)
        R(("wat", 1), 2, 1, V)
        Q(("wat", 1), 0, 2)
        make_dh(1)
        Q(("wat", 1), 2, 1)
        quantise_dh(1)
        second_product(1, 0, 2)
        send_back_singly(1, 0)
        round_dealt(2, 0, V)
        Q(("wat", 1), 3, 1)
        second_product(1, 2, 2)
        round_dealt(2, 2, V)
        Q(("wbt", 2), 0, 2)
        Q(("wbt", 2), 2, 2)
        first_product(2)
        make_factor(2)
        make_factor(3)
        make_dh(2)
        R(("wat", 2), 0, 1, V)
        quantise_dh(2)
        R(("wat", 2), 1, 1, V)
        leave_psum(1, 2, 2, S)
        R(("wat", 2), 3, 1, S)
        scatter(1, 2)
        scatter(1, 3)
        Q(("wat", 2), 0, 1)
        R(("wat", 2), 2, 1, V)
        Q(("wat", 2), 1, 1)
        second_product(2, 0, 2)
        Q(("wat", 2), 3, 1)
        Q(("wat", 2), 2, 1)
        second_product(2, 2, 2)
        send_back_singly(2, 0)
        round_dealt(3, 0, V)
        round_dealt(3, 2, V)
        Q(("wbt", 3), 0, 2)
        Q(("wbt", 3), 2, 2)
        first_product(3)
        R(("wat", 3), 0, 2, V)
        leave_psum(2, 2, 2, S)
        R(("wat", 3), 3, 1, S)
        scatter(2, 2)
        scatter(2, 3)
        R(("wat", 3), 2, 1, V)
        Q(("wat", 3), 0, 2)
        make_dh(3)
        Q(("wat", 3), 2, 1)
        quantise_dh(3)
        second_product(3, 0, 2)
        Q(("wat", 3), 3, 1)
        second_product(3, 2, 2)
        send_back_singly(3, 0)
        round_dealt(4, 0, V)
        round_dealt(4, 2, V)
        Q(("wbt", 4), 0, 2)
        Q(("wbt", 4), 2, 2)
        first_product(4)
        round_behind(("wat", 4), 1, (("wbt", 4), 2))
        make_factor(4)
        make_factor(5)
        leave_psum(3, 2, 1, S)
        leave_psum(3, 3, 1, S)
        scatter(3, 2)
        scatter(3, 3)
        make_dh(4)
        R(("wat", 4), 0, 1, V)
        quantise_dh(4)
        Q(("wat", 4), 1, 1)
        second_product(4, 1, 1)
        Q(("wat", 4), 0, 1)
        second_product(4, 0, 1)
        round_dealt(5, 0, V)
        round_dealt(5, 2, V)
        Q(("wbt", 5), 0, 2)
        leave_psum(4, 1, 1, S)
        leave_psum(4, 0, 1, S)
        R(("wat", 4), 3, 1, S)
        scatter(4, 1)
        scatter(4, 0)
        R(("wat", 4), 2, 1, V)
        Q(("wbt", 5), 2, 2)
        first_product(5)
        Q(("wat", 4), 2, 1)
        second_product(4, 2, 1)
        Q(("wat", 4), 3, 1)
        second_product(4, 3, 1)
        R(("wat", 5), 0, 1, V)
        R(("wat", 5), 1, 1, V)
        Q(("wat", 5), 0, 1)
        Q(("wat", 5), 1, 1)
        make_dh(5)
        R(W, 0, 1, V)
        quantise_dh(5)
        second_product(5, 0, 1)
        second_product(5, 1, 1)
        leave_psum(4, 2, 1, S)
        leave_psum(4, 3, 1, S)
        scatter(4, 2)
        scatter(4, 3)
        R(W, 1, 1, V)
        Q(W, 0, 1)
        frozen_long(0)
        R(("wat", 5), 2, 1, V)
        R(("wat", 5), 3, 1, V)
        leave_psum(5, 0, 1, S)
        leave_psum(5, 1, 1, S)
        scatter(5, 0)
        scatter(5, 1)
        Q(("wat", 5), 2, 1)
        second_product(5, 2, 1)
        Q(W, 1, 1)
        Q(("wat", 5), 3, 1)
        second_product(5, 3, 1)
        frozen_short(0)
        frozen_long(1)
        R(W, 2, 1, V)
        R(W, 3, 1, V)
        Q(W, 2, 1)
        frozen_long(2)
        leave_psum(5, 2, 1, V)
        scatter(5, 2)
        Q(W, 3, 1)
        frozen_short(2)
        frozen_long(3)
        leave_psum(5, 3, 1, V)
        scatter(5, 3)
        finish_piece(0, 0, BANK)
        finish_piece(0, BANK, T - BANK)
        finish_whole(1)
        finish_whole(2)
        finish_piece(3, 0, BANK)
        finish_piece(3, BANK, T - BANK)
